import numpy as np, ml_dtypes
CORES = [3,11,19,27,35,43,51,59]
N = 8
import mx_ref
BF = ml_dtypes.bfloat16
def cols(t, e):
    v = np.concatenate([t.reshape(128, -1, 4), np.zeros((128, 1, 4), BF)], axis=1)
    return np.ascontiguousarray(v[:, e]).reshape(128, -1)
def cut(t, i, w=512):
    return t[:, w * i:w * i + w]
def f(rng, *shape):
    return mx_ref.flush((rng.standard_normal(shape, dtype=np.float32) * np.exp2(rng.integers(-2, 3, shape[:-1] + (1,)))).astype(BF))
def wide(rng, *shape, cols=0):
    v = rng.standard_normal(shape, dtype=np.float32) * np.exp2(rng.integers(-12, 13, shape)).astype(np.float32)
    if cols: v *= np.repeat(np.exp2(rng.integers(-cols, cols + 1, shape[:-2] + (1, shape[-1] // 4))) * (rng.random(shape[:-2] + (1, shape[-1] // 4)) > 0.0625), 4, axis=-1).astype(np.float32)
    return mx_ref.flush(v.astype(BF))
WD, T, PL, CP, NC = 16, 256, 128, 16, 56
def scores(u, x):
    return np.stack([mx_ref.matmul(mx_ref.quantize(u[r]), mx_ref.quantize(x[r]))[0] for r in range(N)])
def fronts(P):
    a = np.zeros(P.shape, bool)
    v, h = P[1:] != P[:-1], P[:, 1:] != P[:, :-1]
    a[1:] |= v; a[:-1] |= v; a[:, 1:] |= h; a[:, :-1] |= h
    return a
def dealt(P):
    i, j = np.nonzero(fronts(P))
    g = np.full((16 * N + 2, WD + 2), -1)
    g[1:-1, 1:-1] = np.arange(N * T).reshape(16 * N, WD)
    n = np.arange(len(i)); D = np.full((N, PL, 5), -1)
    D[(n // 8) % N, 8 * (n // (8 * N)) + n % 8] = np.stack([g[i + 1, j + 1], g[i, j + 1], g[i + 2, j + 1], g[i + 1, j], g[i + 1, j + 2]], axis=1)
    return D
def needed(P):
    return np.stack([np.bincount(e[e >= 0] // T, minlength=N) for e in [np.unique(k) for k in dealt(P)]])
def broken(P):
    if np.sum(fronts(P)) > PL * N: return ["too many active cells"]
    b = []; D = dealt(P)
    for r in range(N):
        c, e = D[r, :, 0], np.unique(D[r])
        if np.bincount(c[c >= 0] // T, minlength=N).max() > CP: b.append("cells of one stripe dealt to one rank")
        if np.bincount(e[e >= 0] // T, minlength=N).max() > NC: b.append("columns of one stripe that one rank needs")
    return b
def smooth(rng, i):
    a, b = np.indices((16 * N, WD)); g = 0
    for _ in range(6):
        t, k, p = rng.uniform(-1, 1), 0.7 * 0.97 ** i * rng.uniform(0.7, 1.4), rng.uniform(0, 6.2832)
        g = g + np.cos(k * (np.cos(t) * a + np.sin(t) * b) + p)
    return g > 0
def straight(rng, i):
    a = np.indices((16 * N, WD))[0]
    return ((a + rng.integers(1, 4)) // 4) % 2 == 0
def islands(rng, i):
    at = [(0, 0), (15, WD // 2)]
    for c in rng.permutation(N * T):
        if len(at) >= int(N * T * 0.0625 * 0.98 ** i): break
        p, q = divmod(int(c), WD)
        if all(abs(p - a) + abs(q - b) >= 3 for a, b in at): at.append((p, q))
    P = np.zeros((16 * N, WD), bool)
    for p, q in at: P[p, q] = True
    return P
def few(rng, i):
    gone = [int(q) for q in 1 + rng.permutation(N - 1)[:rng.integers(1, 3)]]
    if len(gone) == 2 and abs(gone[0] - gone[1]) == 1: gone.pop()
    here = [q for q in range(N) if q not in gone]
    free = [q for q in here if q - 1 not in gone and q + 1 not in gone]
    P = np.zeros((16 * N, WD), bool)
    for q in here:
        if q - 1 in gone: P[16 * q + 1, rng.integers(0, WD)] = True
        if q + 1 in gone: P[16 * q + 14, rng.integers(0, WD)] = True
    for q in free + here[:rng.integers(0, 2)]: P[16 * q + rng.integers(1, 16 if q + 1 in here else 15), rng.integers(0, WD)] = True
    return P
def heavy(rng, i):
    a, b = np.indices((16 * N, WD)); n = np.zeros(a.shape, int); most = rng.integers(0, N)
    low = b % 2 == 1 if WD == 8 else ((b % 2 == 0) & (b > 0)) | (b == WD - 1)
    for r in range(N):
        if r == most:
            for k in (6, 10): n += a >= 16 * r + k + low
            n += a >= 16 * r + 14
            if WD == 8: n[16 * r + 2, 0] += 1
            else: n += a >= 16 * r + 2
        else:
            w = rng.integers(5, 12) + max(0, 3 - 0.1 * i) * np.sin(rng.uniform(0.2, 0.8) * np.arange(WD) + rng.uniform(0, 6.2832))
            n += a >= 16 * r + np.clip(np.rint(w), 2, 14)[None, :]
    return n % 2 == 0
def borders(rng, i):
    a, b = np.indices((16 * N, WD))
    return (a // 16 + (b < rng.integers(1, WD))) % 2 == 0
def drawn(rng, make, uneven=False, idle=False):
    for i in range(50):
        P = make(rng, i) ^ bool(rng.integers(0, 2))
        c = fronts(P).reshape(N, T).sum(axis=1)
        if c.sum() < (1 if idle else 8 * N) or broken(P): continue
        m = needed(P) * (1 - np.eye(N, dtype=int))
        if uneven and (c.max() < 3 * c.min() or m.max() != NC): continue
        if idle and not 1 <= (c == 0).sum() <= 2: continue
        if idle and (c.sum() > 8 * (N - 1) or (c.sum() - 1) % 8 < 3): continue
        if idle and not (m.sum(axis=0)[c == 0] > 0).all(): continue
        return P
    raise RuntimeError("no field in 50 tries")
def sized(t):
    v = t.astype(np.float32)
    return np.where(np.abs(v) < 2.0 ** -30, np.float32(0), v).astype(BF)
def plant(rng, P, spread=False):
    u = sized(f(rng, 128, 512)); qu = mx_ref.quantize(u)
    x = np.zeros((N, 128, T, 4), BF); want = P.reshape(N, T)
    for r in range(N):
        left = np.arange(T)
        for i in range(50):
            k = len(left); m = 8 * -(-k // 8)
            t = sized(wide(rng, 128, 4 * m, cols=2) if spread else f(rng, 128, 4 * m))
            s = mx_ref.matmul(qu, mx_ref.quantize(t))[0][:k]
            turn = np.where((s > 0) == want[r, left], 1, -1)
            t = (t.astype(np.float32).reshape(128, m, 4)[:, :k] * turn[None, :, None]).astype(BF)
            ok = np.abs(s) > 32
            x[r][:, left[ok]] = t[:, ok]
            left = left[~ok]
            if len(left) == 0: break
        else: raise RuntimeError("scores too small in 50 tries")
    return {"x": x.reshape(N, 128, 4 * T), "u": np.stack([u] * N), "w": sized(f(rng, N, 128, 5120))}
def setup_inputs(rng):
    return plant(rng, drawn(rng, smooth))
def setup_inputs_few(rng):
    return plant(rng, drawn(rng, few, idle=True))
def setup_inputs_near(rng):
    for i in range(50):
        d = plant(rng, drawn(rng, borders))
        s = scores(d["u"], d["x"])
        e = 1 + int(np.floor(np.log2(float(np.abs(s).min()))))
        d["u"] = sized((d["u"].astype(np.float32) * np.float32(2.0 ** -e)).astype(BF))
        t = scores(d["u"], d["x"])
        if 0.5 < np.abs(t).min() <= 1 and np.array_equal(t > 0, s > 0): return d
    raise RuntimeError("no scores near 0.5 in 50 tries")
def setup_inputs_spread(rng):
    return plant(rng, drawn(rng, islands), spread=True)
def setup_inputs_straight(rng):
    return plant(rng, drawn(rng, straight))
def setup_inputs_uneven(rng):
    return plant(rng, drawn(rng, heavy, uneven=True))
def check_inputs(d):
    b = []
    for k in ("x", "u", "w"):
        v = np.abs(d[k].astype(np.float32))
        if not ((v == 0) | ((v >= 2.0 ** -30) & (v <= 2.0 ** 30))).all(): b.append("sizes of " + k)
    if b: return b
    for r in range(N):
        if not np.array_equal(d["u"][r].astype(np.float32), d["u"][0].astype(np.float32)): b.append("u")
    s = scores(d["u"], d["x"])
    if not (np.abs(s) > 0.5).all(): b.append("score")
    return b + broken((s > 0).reshape(16 * N, WD))
def reference(x, u, w):
    P = (scores(u, x) > 0).reshape(16 * N, WD)
    D = dealt(P)
    m = max(8, 8 * -(-int(np.sum(fronts(P))) // (8 * N)))
    X = np.concatenate(list(x), axis=1)
    y = np.zeros((N, 128, 2 * PL), np.float32)
    for r in range(N):
        for k in range(5):
            q = mx_ref.quantize(cols(X, D[r, :m, k]))
            for o in range(2): y[r][:, PL * o:PL * o + m] += mx_ref.matmul(mx_ref.quantize(cut(w[r], 2 * k + o)), q)
    return {"y": y}

@@ -1,0 +1,373 @@
+from concourse.bass import DstId, RemoteDMATransfer
+from concourse.mybir import dt, AluOpType, ActivationFunctionType, AxisListType
+
+N = 8
+NS = 16
+NC = 5 * NS
+SL = NC + 16
+LW = SL * N + 16 + 128
+PW = 16 + 256 + 16 + 128
+MID = 144
+KW = (1, 3, 0, 4, 2)
+F8, U8, BF, F32 = "float8_e4m3fn_x4", "uint8", "bfloat16", "float32"
+SCRATCH = {"aF": ("sbuf", [128, 4096], F32), "aH": ("sbuf", [128, 6144], BF), "aI": ("sbuf", [128, 256], "int32"),
+           "aU": ("sbuf", [128, 512], "uint16"), "sg": ("sbuf", [128, 128], BF), "xt": ("sbuf", [128, 1088], BF),
+           "uc": ("sbuf", [128, 16], BF), "ut": ("sbuf", [128, 512], BF), "wt": ("sbuf", [128, 5120], BF), "zt": ("sbuf", [128, 640], BF),
+           "yo": ("sbuf", [128, 256], F32), "ps": ("psum", [128, 2048], F32)}
+for _n, _w in (("e", 128), ("u", 128), ("w", 1280), ("gr", PW), ("sl", NC * 7), ("la", LW), ("t", 640)):
+    SCRATCH[_n + "q"] = ("sbuf", [128, _w], F8)
+    SCRATCH[_n + "s"] = ("sbuf", [128, _w], U8)
+DMAS = ["de0", "de1", "dx0", "dx1", "du", "dw0", "dw1", "dw2", "dy0", "dy1"]
+SEMAPHORES = ["qv", "qs", "qt", "qg"] + DMAS + ["rsign", "lsign", "rhc", "rhs", "lhalo", "rlc", "rls", "lland"]
+A = AluOpType
+AF = ActivationFunctionType
+AX = AxisListType.X
+MUL, ADD, SUB, MAX, MIN = A.mult, A.add, A.subtract, A.max, A.min
+EQ, NE, LT, GE = A.is_equal, A.not_equal, A.is_lt, A.is_ge
+
+
+def rank_program(g, core, T, topo):
+    r = T.rank_of(core)
+    if r is None:
+        return
+    queues = {"v": g.vector, "s": g.scalar, "t": g.tensor, "g": g, "y": g.sync}
+    csem = {"v": "qv", "s": "qs", "t": "qt", "g": "qg"}
+    count = {}
+    known = {q: {} for q in queues}
+    hist = {}
+    used = {"aF": 0, "aH": 0, "aI": 0, "aU": 0}
+    unit = {"aF": 8, "aH": 16, "aI": 8, "aU": 16}
+
+    def V(name, a, b, step=1):
+        return (name, a, b, step)
+
+    def new(arena, n):
+        a = used[arena]
+        used[arena] = a + -(-n // unit[arena]) * unit[arena]
+        return V(arena, a, a + n)
+
+    def sub(v, a, b, step=1):
+        return V(v[0], v[1] + a, v[1] + b, step)
+
+    def ap(v):
+        return T[v[0]][:, v[1]:v[2]:v[3]] if v[3] != 1 else T[v[0]][:, v[1]:v[2]]
+
+    def note(v, write, q, sem, val, clock):
+        hist.setdefault(v[0], []).append((v, write, q, sem, val, clock))
+
+    def sync(q, outs, ins):
+        need = {}
+        for group, out in ((outs, True), (ins, False)):
+            for v in group:
+                for (o, write, oq, sem, val, clock) in hist.get(v[0], []):
+                    if not (write or out) or o[1] >= v[2] or v[1] >= o[2]:
+                        continue
+                    if not write and oq == q and sem == csem.get(q):
+                        continue
+                    if v[3] == o[3] and v[3] > 1 and (v[1] - o[1]) % v[3]:
+                        continue
+                    if val > need.get(sem, (0, None))[0]:
+                        need[sem] = (val, clock)
+        mine = csem.get(q)
+        for sem in sorted(need, key=lambda s: (s == mine, s in DMAS, s)):
+            val, clock = need[sem]
+            if known[q].get(sem, 0) >= val:
+                continue
+            queues[q].wait_ge(T.sem[sem], val)
+            for s2, v2 in list(clock.items()) + [(sem, val)]:
+                known[q][s2] = max(known[q].get(s2, 0), v2)
+
+    def run(q, outs, ins, call, sem=None, n=1):
+        sync(q, outs, ins)
+        sem = sem or csem[q]
+        count[sem] = count.get(sem, 0) + n
+        call(queues[q]).then_inc(T.sem[sem], n)
+        clock = dict(known[q])
+        for v in outs:
+            note(v, True, q, sem, count[sem], clock)
+        for v in ins:
+            note(v, False, q, sem, count[sem], clock)
+
+    def sc(s, ins):
+        if isinstance(s, tuple):
+            ins.append(s)
+            return ap(s)
+        return s
+
+    def ts(o, i, s1, op0, s2=None, op1=None):
+        ins = [i]
+        a, b = sc(s1, ins), sc(s2, ins)
+        if op1 is None:
+            run("v", [o], ins, lambda e: e.tensor_scalar(ap(o), ap(i), a, None, op0))
+        else:
+            run("v", [o], ins, lambda e: e.tensor_scalar(ap(o), ap(i), a, b, op0, op1))
+        return o
+
+    def tt(o, a, b, op):
+        run("v", [o], [a, b], lambda e: e.tensor_tensor(ap(o), ap(a), ap(b), op))
+        return o
+
+    def cp(o, i):
+        run("v", [o], [i], lambda e: e.tensor_copy(ap(o), ap(i)))
+        return o
+
+    def tr(o, i):
+        run("v", [o], [i], lambda e: e.transpose(ap(o), ap(i)))
+        return o
+
+    def scan(o, d0, d1, init=0.0):
+        ins = [d0, d1]
+        s = sc(init, ins)
+        run("v", [o], ins, lambda e: e.tensor_tensor_scan(ap(o), ap(d0), ap(d1), s, MUL, ADD))
+        return o
+
+    def fill(o, c):
+        run("v", [o], [], lambda e: e.memset(ap(o), c))
+        return o
+
+    def minus_total(o, i):
+        run("v", [o], [i], lambda e: e.tensor_reduce(ap(o), ap(i), AX, ADD, negate=True))
+        return o
+
+    def gather(o, win, off, q="v"):
+        if q == "v":
+            run("v", [o], [win, off], lambda e: e.tensor_copy(ap(o), ap(win).indirect(ap(off))))
+        else:
+            run("s", [o], [win, off], lambda e: e.activation(ap(o), ap(win).indirect(ap(off)), AF.Copy))
+        return o
+
+    def act(o, i, func, scale=1.0, bias=0.0):
+        ins = [i]
+        a, b = sc(scale, ins), sc(bias, ins)
+        run("s", [o], ins, lambda e: e.activation(ap(o), ap(i), func, bias=b, scale=a))
+        return o
+
+    def iota(o, pattern, base=0, lane=0):
+        run("g", [o], [], lambda e: e.iota(ap(o), pattern, base, lane, allow_small_or_imprecise_dtypes=o[0] != "aI"))
+        return o
+
+    def const(o, c):
+        return iota(o, [[0, o[2] - o[1]]], c)
+
+    def asel(o, i, pattern, op, c, base):
+        run("g", [o], [i], lambda e: e.affine_select(ap(o), ap(i), pattern, op, c, base, 0))
+        return o
+
+    def dma(q, o, i, sem):
+        run(q, [v for v in (o,) if isinstance(v, tuple)], [v for v in (i,) if isinstance(v, tuple)],
+            lambda e: e.dma_start(ap(o) if isinstance(o, tuple) else o, ap(i) if isinstance(i, tuple) else i), sem, 16)
+
+    def quant(n, a, b, t, c):
+        q, s, i = V(n + "q", a, b), V(n + "s", a, b), V(t, c, c + 4 * (b - a))
+        run("v", [q, s], [i], lambda e: e.quantize_mx(ap(q), ap(s), ap(i)))
+
+    def pickc(cq, wq, off):
+        run("v", [cq], [wq, off], lambda e: e.tensor_copy(ap(cq).bitcast(dt.uint32), ap(wq).bitcast(dt.uint32).indirect(ap(off))))
+
+    def mm(o, wq, ws, xq, xs, start, stop):
+        run("t", [o] if start else [], [wq, ws, xq, xs], lambda e: e.matmul_mx(ap(o), ap(wq), ap(ws), ap(xq), ap(xs), start, stop))
+        if not start:
+            note(o, True, "t", "qt", count["qt"], dict(known["t"]))
+
+    def send(pairs, width, bits, rsem, lsem, ins, arrive):
+        sync("g", [], ins)
+        xs = []
+        for k, (d, src, dst) in enumerate(pairs):
+            to = T.cores[d]
+            rid, pid, _ = topo.addr(to)
+            a, b = ap(src), ap(dst)
+            if bits:
+                a, b = a.bitcast(dt.uint8), b.bitcast(dt.uint8)
+            mask = sum(1 << e for e in topo.engines(core, to)[width * k:width * k + width])
+            xs.append(RemoteDMATransfer(dst_ids=[DstId(rid=rid, pnc=pid)], dma_engine_mask=mask,
+                                        remote_sem=T.sem[rsem], src=a, dst=b))
+        g.remote_dma_fused(xs, local_sem=T.sem[lsem])
+        count[lsem] = count.get(lsem, 0) + width * len(xs)
+        count[rsem] = count.get(rsem, 0) + arrive
+
+    F1 = lambda: new("aF", 1)
+    turn = 1 if r % 2 == 0 else -1
+    order = [d for b in range(0, N, 2) for d in ((r + b) % N, (r + b) % N + turn)]
+    others = order[1:]
+
+    dma("y", V("uc", 0, 8), T.u[:, 0:8], "du")
+    dma("s", V("zt", 64, 128), T.x[:, 960:1024], "de1")
+    dma("y", V("zt", 0, 64), T.x[:, 0:64], "de0")
+    dma("s", V("xt", 64, 576), T.x[:, 0:512], "dx0")
+    dma("y", V("xt", 576, 1088), T.x[:, 512:1024], "dx1")
+
+    lane = iota(new("aI", 1), [[0, 1]], 0, 1)
+    jj = iota(new("aH", 64), [[0, 4], [1, 16]])
+    ones = fill(new("aH", 128), 1.0)
+    bI = ts(new("aI", 1), lane, 31, A.bitwise_and)
+    bm = ts(F1(), bI, -15.5, ADD)
+    w = act(F1(), bm, AF.Abs)
+    half = act(new("aF", 16), sub(ones, 0, 16), AF.Copy, 1.0 / 36)
+    fill(V("zt", 128, 640), 0.0)
+    first = ts(F1(), w, 15.0, GE, -0.0625, MUL)
+    q0 = ts(F1(), w, 15.9375, MUL, 0.0625 - 15.9375 * 15.5, ADD)
+    cut = tt(F1(), first, q0, ADD)
+    ft = new("aH", 256)
+    f1 = ts(new("aH", 64), jj, 15.9375, MUL, cut, ADD)
+    ts(sub(ft, 0, 64), f1, 0.0, MAX, 16.0, MIN)
+    eq = scan(new("aF", 16), sub(ft, 0, 16), half)
+    nrm = F1()
+
+    halo = [(k, a, b) for k, a, b in ((r + 1, 16, 0), (r - 1, 0, 272)) if 0 <= k < N]
+    wide = lambda k: 8 // sum(0 <= j < N for j in (k - 1, k + 1))
+    quant("e", 0, 128, "zt", 0)
+    for n, bits, rsem in (("q", True, "rhc"), ("s", False, "rhs")):
+        at = lambda m, a: V(m + n, a, a + 16)
+        send([(k, at("e", a), at("gr", b)) for k, a, b in halo], wide(r), bits, rsem, "lhalo",
+             [at("e", a) for k, a, b in halo], sum(wide(k) for k, a, b in halo))
+        for k, a, b in halo:
+            note(at("gr", 0 if k < r else 272), True, None, rsem, count[rsem], {})
+    t_e = iota(new("aF", 2), [[2, 2]], 1)
+    t_y = const(new("aF", 2), 16 * r)
+    t_l = iota(new("aF", 3), [[16, 3]], -1)
+    t_d = new("aF", 8)
+    nb = (N - r + 1) // 2
+    iota(sub(t_d, 0, 2 * nb), [[-16, nb], [0, 2]], 383 - 8 * r)
+    if nb < 4:
+        iota(sub(t_d, 2 * nb, 8), [[-16, 4 - nb], [0, 2]], 383 - 8 * ((r + 2 * nb) % N))
+
+    for t in (1, 2, 3):
+        act(V("ut", t, 512, 4), ones, AF.Identity, 0.0, V("uc", t, t + 1))
+    ts(V("ut", 0, 512, 4), ones, V("uc", 0, 1), MUL)
+    for a in (64, 128, 192):
+        act(sub(ft, a, a + 64), sub(ft, 0, 64), AF.Copy)
+    if r == 0:
+        fill(V("xt", 0, 64), 0.0)
+    sgn, cells = new("aH", 256), new("aH", 256)
+    for h in (0, 1):
+        a = 0 if r == 0 and h == 0 else 16 + 128 * h
+        quant("gr", a, 144 + 128 * h, "xt", 4 * a)
+        if h == 0:
+            quant("u", 0, 128, "ut", 0)
+        a = 16 + 128 * h
+        mm(V("ps", 512 * h, 512 * h + 128), V("uq", 0, 128), V("us", 0, 128), V("grq", a, a + 128), V("grs", a, a + 128), True, True)
+    run("v", [nrm], [sub(eq, 15, 16)], lambda e: e.reciprocal(ap(nrm), ap(sub(eq, 15, 16))))
+    for h in (0, 1):
+        ts(sub(sgn, 128 * h, 128 * h + 128), V("ps", 512 * h, 512 * h + 128), 0.0, A.is_gt, -0.5, ADD)
+    scan(cells, ft, sgn)
+    own = V("sg", 16 * r, 16 * r + 16)
+    ts(own, sub(cells, 15, 256, 16), nrm, MUL)
+    send([(k, own, own) for k in others], 1, False, "rsign", "lsign", [own], N - 1)
+    for k in others:
+        note(V("sg", 16 * k, 16 * k + 16), True, None, "rsign", count["rsign"], {})
+    g.sync.wait_ge(T.sem["lsign"], count["lsign"])
+    known["y"]["lsign"] = count["lsign"]
+    for k, (a, b) in enumerate(((0, 2048), (2048, 4096), (4096, 5120))):
+        dma("y", V("wt", a, b), T.w[:, a:b], "dw%d" % k)
+
+    t_tr = iota(new("aF", 16), [[1, 16]], (1 << 20) - 256)
+    base = iota(new("aH", 256), [[-1, 16], [16, 16]], 31 - MID)
+    onef = const(new("aF", 32), 1)
+    rs = asel(new("aF", 32), asel(new("aF", 32), onef, [[1, 32]], NE, 0.0, 0), [[1, 32]], NE, -1.0, -16)
+    win = const(new("aH", 384), MID)
+    XS = const(new("aH", 32), 1000)
+    npt = new("aF", 256)
+    for a in range(8):
+        iota(sub(npt, 32 * a, 32 * a + 32), [[0, 2], [128, 2], [2, 8]], 256 * a + 16 * r + 3)
+    r32 = asel(new("aH", 256), const(new("aH", 256), 1), [[0, 8], [1, 32]], NE, 0.0, 0)
+
+    alpha = act(new("aH", 128), ones, AF.Copy, scale=1.0 / 32)
+    lo = ts(F1(), bm, 0.0, LT)
+    one0 = ts(F1(), bm, -15.5, EQ)
+    iF = ts(F1(), ts(new("aI", 1), lane, 15, A.bitwise_and), 0.0, ADD)
+    d0 = act(new("aH", 128), ones, AF.Copy, scale=lo)
+    hb = act(F1(), bm, AF.Identity, 0.5 * turn, 7.75 * turn)
+    s1 = act(F1(), iF, AF.Identity, 1.0 - 0.5 * turn, hb)
+    off_y = ts(new("aU", 2), t_y, iF, ADD)
+    high = ts(F1(), iF, 8.0, GE, 56.0, MUL)
+    la = ts(new("aF", 3), t_l, iF, ADD, 39.0, MIN)
+    lb = ts(new("aI", 3), la, 0.2, MUL, -0.4, ADD)
+    e13 = ts(new("aF", 2), t_e, iF, EQ)
+    n13 = ts(new("aF", 2), t_e, iF, NE)
+    lc = ts(new("aF", 3), lb, 11.0, MUL)
+    off_d = ts(new("aU", 8), t_d, s1, SUB, high, SUB)
+    ld = tt(new("aF", 3), lc, la, ADD)
+    off_l = ts(new("aU", 3), ld, 0.0, MAX)
+    quant("gr", 288 if r < N - 1 else 272, 416 if r < N - 1 else 400, "zt", 128)
+    quant("la", SL * N + 16, LW, "zt", 128)
+    i16 = act(F1(), iF, AF.Copy, scale=16.0)
+    trash = act(new("aF", 16), t_tr, AF.Identity, bias=i16)
+    sx = act(F1(), iF, AF.Identity, bias=-2.0)
+    sx2 = act(F1(), sx, AF.Square)
+    delta = act(F1(), act(F1(), sx2, AF.Identity, 7.0 / 3, -4.0 / 3), AF.Copy, scale=sx)
+    z1 = act(F1(), sub(e13, 0, 1), AF.Identity, float(MID + 1), delta)
+    z3 = act(F1(), sub(e13, 1, 2), AF.Identity, float(MID - 1), delta)
+    val = new("aH", 256)
+    act(sub(val, 16, 240), sub(base, 16, 240), AF.Identity, 1.0, delta)
+    act(sub(val, 0, 16), sub(base, 0, 16), AF.Identity, sub(n13, 1, 2), z3)
+    act(sub(val, 240, 256), sub(base, 240, 256), AF.Identity, sub(n13, 0, 1), z1)
+
+    SV, X = new("aH", 128), new("aH", 128)
+    sg = V("sg", 0, 128)
+    act(sub(SV, 0, 127), sub(sg, 1, 128), AF.Sign)
+    st = scan(new("aH", 128), alpha, sg, sub(sg, 0, 1))
+    ts(sub(SV, 127, 128), sub(sg, 127, 128), -1.0, MAX, 1.0, MIN)
+    pr = tt(new("aH", 128), st, SV, MUL)
+    av = ts(new("aH", 128), pr, 18.0, LT)
+    scan(X, d0, av, one0)
+
+    Y = gather(new("aH", 32), X, off_y)
+    act(sub(XS, 0, 8), sub(X, 15, 128, 16), AF.Copy)
+    lbk = [act(F1(), iF, AF.Identity, bias=16.0 + 16 * k + 16 * SL) for k in range(5)]
+    YT = tr(new("aH", 32), Y)
+    S6 = scan(new("aF", 32), rs, YT)
+    V6 = tt(new("aI", 16), sub(S6, 16, 32), sub(YT, 16, 32), MUL)
+    A6 = ts(new("aI", 16), V6, 127 | 1 << 20, A.bitwise_and)
+    o6 = tt(new("aF", 16), A6, trash, MAX)
+    off = ts(new("aU", 16), o6, float((1 << 20) - 256), SUB)
+    run("v", [win], [off, val], lambda e: e.tensor_copy(ap(win).indirect(ap(off)), ap(val)))
+    D = gather(new("aH", 128), win, off_d)
+    DT = tr(new("aH", 128), D)
+    lw = new("aU", 48)
+    run("v", [lw], [DT, off_l], lambda e: e.tensor_scalar(ap(lw), ap(DT).indirect(ap(off_l)), float(MID), None, ADD))
+
+    gq, gs = V("grq", 0, 304), V("grs", 0, 304)
+    home = lambda n, k: V(n, SL * k + 16, SL * k + SL)
+    slot = lambda n, i: V(n, NC * i, NC * i + NC)
+    for a, b in ((4, 7), (0, 4)):
+        pickc(V("slq", NC * a, NC * b), gq, sub(lw, 6 + 5 * a, 6 + 5 * b))
+        gather(V("sls", NC * a, NC * b), gs, sub(lw, 6 + 5 * a, 6 + 5 * b), "s")
+    for n, bits, m, a, b, width in (("q", True, "rlc", 4, 7, 2), ("q", True, "rlc", 0, 4, 2), ("s", False, "rls", 0, 7, 1)):
+        send([(others[i], slot("sl" + n, i), home("la" + n, r)) for i in range(a, b)], width, bits, m, "lland",
+             [slot("sl" + n, i) for i in range(a, b)], width * (N - 1) if a == 0 else 0)
+        if a == 0:
+            for k in others:
+                note(home("la" + n, k), True, None, m, count[m], {})
+
+    XT = tr(new("aH", 32), XS)
+    C = minus_total(F1(), sub(XT, 0, 16))
+    ind = act(new("aH", 256), npt, AF.Sign, 0.5, C)
+    pickc(V("laq", SL * r, SL * r + SL), gq, sub(lw, 0, 6))
+    gather(V("las", SL * r, SL * r + SL), gs, sub(lw, 0, 6), "s")
+    quant("w", 0, 512, "wt", 0)
+    it = tr(new("aH", 256), ind)
+    iq = scan(new("aH", 256), r32, it)
+    lf, lu = new("aF", 40), new("aU", 40)
+    for k in range(5):
+        act(sub(lf, 8 * k, 8 * k + 8), sub(iq, 31, 256, 32), AF.Identity, SL / 2.0, lbk[k])
+    for a, b in ((512, 1024), (1024, 1280)):
+        quant("w", a, b, "wt", 4 * a)
+    ts(lu, lf, 0.0, ADD)
+
+    tk = lambda n, k: V(n, 128 * k, 128 * k + 128)
+    lk = lambda k: sub(lu, 8 * k, 8 * k + 8)
+    for k in range(5):
+        pickc(tk("tq", k), V("laq", 0, LW), lk(k))
+    for k in range(5):
+        gather(tk("ts", k), V("las", 0, LW), lk(k), "ssvsv"[k])
+    for k in range(5):
+        for o in (0, 1):
+            a = 128 * (2 * KW[k] + o)
+            mm(V("ps", 1024 + 512 * o, 1152 + 512 * o), V("wq", a, a + 128), V("ws", a, a + 128), tk("tq", k), tk("ts", k), k == 0, k == 4)
+    cp(V("yo", 0, 128), V("ps", 1024, 1152))
+    act(V("yo", 128, 256), V("ps", 1536, 1664), AF.Copy)
+    dma("y", T.y[:, 0:128], V("yo", 0, 128), "dy0")
+    dma("s", T.y[:, 128:256], V("yo", 128, 256), "dy1")
+    for sem in SEMAPHORES:
+        if count.get(sem, 0) > known["g"].get(sem, 0):
+            g.wait_ge(T.sem[sem], count[sem])

@@ -6,12 +6,17 @@ NS = 16
 NC = 5 * NS
 SL = NC + 16
 LW = SL * N + 16 + 128
-PW = 16 + 256 + 16 + 128
-MID = 144
+ZERO, UP, DOWN, PW = 256, 272, 288, 304
+MID = 128
 KW = (1, 3, 0, 4, 2)
+NV = 17
+CARRY = 1.0 / 16
+LEVEL = 1.096
+ROUND = 1.5 * 2 ** 30
+EARLY = 1024
 F8, U8, BF, F32 = "float8_e4m3fn_x4", "uint8", "bfloat16", "float32"
 SCRATCH = {"aF": ("sbuf", [128, 4096], F32), "aH": ("sbuf", [128, 6144], BF), "aI": ("sbuf", [128, 256], "int32"),
-           "aU": ("sbuf", [128, 512], "uint16"), "sg": ("sbuf", [128, 128], BF), "xt": ("sbuf", [128, 1088], BF),
+           "aU": ("sbuf", [128, 512], "uint16"), "sg": ("sbuf", [128, 144], BF), "xt": ("sbuf", [128, 1088], BF),
            "uc": ("sbuf", [128, 16], BF), "ut": ("sbuf", [128, 512], BF), "wt": ("sbuf", [128, 5120], BF), "zt": ("sbuf", [128, 640], BF),
            "yo": ("sbuf", [128, 256], F32), "ps": ("psum", [128, 2048], F32)}
 for _n, _w in (("e", 128), ("u", 128), ("w", 1280), ("gr", PW), ("sl", NC * 7), ("la", LW), ("t", 640)):
@@ -23,7 +28,7 @@ A = AluOpType
 AF = ActivationFunctionType
 AX = AxisListType.X
 MUL, ADD, SUB, MAX, MIN = A.mult, A.add, A.subtract, A.max, A.min
-EQ, NE, LT, GE = A.is_equal, A.not_equal, A.is_lt, A.is_ge
+EQ, NE, LT, GE, GT = A.is_equal, A.not_equal, A.is_lt, A.is_ge, A.is_gt
 
 
 def rank_program(g, core, T, topo):
@@ -49,7 +54,12 @@ def rank_program(g, core, T, topo):
     def sub(v, a, b, step=1):
         return V(v[0], v[1] + a, v[1] + b, step)
 
+    def col(v, a):
+        return sub(v, a, a + 1)
+
     def ap(v):
+        if v[3] < 0:
+            return T[v[0]][:, v[2] - 1:v[1] - 1:v[3]]
         return T[v[0]][:, v[1]:v[2]:v[3]] if v[3] != 1 else T[v[0]][:, v[1]:v[2]]
 
     def note(v, write, q, sem, val, clock):
@@ -125,8 +135,8 @@ def rank_program(g, core, T, topo):
         run("v", [o], [], lambda e: e.memset(ap(o), c))
         return o
 
-    def minus_total(o, i):
-        run("v", [o], [i], lambda e: e.tensor_reduce(ap(o), ap(i), AX, ADD, negate=True))
+    def reduce(o, i, op):
+        run("v", [o], [i], lambda e: e.tensor_reduce(ap(o), ap(i), AX, op))
         return o
 
     def gather(o, win, off, q="v"):
@@ -136,18 +146,21 @@ def rank_program(g, core, T, topo):
             run("s", [o], [win, off], lambda e: e.activation(ap(o), ap(win).indirect(ap(off)), AF.Copy))
         return o
 
+    def scatter(win, off, val):
+        run("v", [win], [off, val], lambda e: e.tensor_copy(ap(win).indirect(ap(off)), ap(val)))
+
     def act(o, i, func, scale=1.0, bias=0.0):
         ins = [i]
         a, b = sc(scale, ins), sc(bias, ins)
         run("s", [o], ins, lambda e: e.activation(ap(o), ap(i), func, bias=b, scale=a))
         return o
 
+    def lin(o, i, scale=1.0, bias=0.0):
+        return act(o, i, AF.Identity, scale, bias)
+
     def iota(o, pattern, base=0, lane=0):
         run("g", [o], [], lambda e: e.iota(ap(o), pattern, base, lane, allow_small_or_imprecise_dtypes=o[0] != "aI"))
         return o
-
-    def const(o, c):
-        return iota(o, [[0, o[2] - o[1]]], c)
 
     def asel(o, i, pattern, op, c, base):
         run("g", [o], [i], lambda e: e.affine_select(ap(o), ap(i), pattern, op, c, base, 0))
@@ -185,7 +198,14 @@ def rank_program(g, core, T, topo):
         count[lsem] = count.get(lsem, 0) + width * len(xs)
         count[rsem] = count.get(rsem, 0) + arrive
 
+    spare = []
+
+    def gap(n=1):
+        for _ in range(min(n, len(spare))):
+            spare.pop(0)()
+
     F1 = lambda: new("aF", 1)
+    H, F, I1 = lambda n: new("aH", n), lambda n: new("aF", n), lambda: new("aI", 1)
     turn = 1 if r % 2 == 0 else -1
     order = [d for b in range(0, N, 2) for d in ((r + b) % N, (r + b) % N + turn)]
     others = order[1:]
@@ -193,140 +213,218 @@ def rank_program(g, core, T, topo):
     dma("y", V("uc", 0, 8), T.u[:, 0:8], "du")
     dma("s", V("zt", 64, 128), T.x[:, 960:1024], "de1")
     dma("y", V("zt", 0, 64), T.x[:, 0:64], "de0")
-    dma("s", V("xt", 64, 576), T.x[:, 0:512], "dx0")
-    dma("y", V("xt", 576, 1088), T.x[:, 512:1024], "dx1")
+    dma("s", V("xt", 0, 512), T.x[:, 0:512], "dx0")
+    dma("y", V("xt", 512, 1024), T.x[:, 512:1024], "dx1")
+    dma("y", V("wt", 0, EARLY), T.w[:, 0:EARLY], "dw0")
 
-    lane = iota(new("aI", 1), [[0, 1]], 0, 1)
-    jj = iota(new("aH", 64), [[0, 4], [1, 16]])
-    ones = fill(new("aH", 128), 1.0)
-    bI = ts(new("aI", 1), lane, 31, A.bitwise_and)
-    bm = ts(F1(), bI, -15.5, ADD)
-    w = act(F1(), bm, AF.Abs)
-    half = act(new("aF", 16), sub(ones, 0, 16), AF.Copy, 1.0 / 36)
-    fill(V("zt", 128, 640), 0.0)
-    first = ts(F1(), w, 15.0, GE, -0.0625, MUL)
-    q0 = ts(F1(), w, 15.9375, MUL, 0.0625 - 15.9375 * 15.5, ADD)
-    cut = tt(F1(), first, q0, ADD)
-    ft = new("aH", 256)
-    f1 = ts(new("aH", 64), jj, 15.9375, MUL, cut, ADD)
-    ts(sub(ft, 0, 64), f1, 0.0, MAX, 16.0, MIN)
-    eq = scan(new("aF", 16), sub(ft, 0, 16), half)
-    nrm = F1()
+    lane = iota(I1(), [[0, 1]], 0, 1)
+    jj = iota(H(64), [[0, 4], [1, 16]])
+    pos = iota(F(36), [[1, 36]], -2)
+    base = H(256)
+    iota(sub(base, 0, 64), [[1, 4], [16, 16]], -MID)
+    t_w = iota(F(16), [[1, 16]], 200)
+    t_l = iota(F(3), [[16, 3]], -1)
 
-    halo = [(k, a, b) for k, a, b in ((r + 1, 16, 0), (r - 1, 0, 272)) if 0 <= k < N]
+    ones = fill(H(160), 1.0)
+
+    def put(o, c):
+        return act(o, sub(ones, 0, len(range(o[1], o[2], o[3]))), AF.Copy, scale=c)
+
+    win, cells, Z, XB, fd, rs, d96, PT, ra = H(592), H(272), H(80), H(176), H(136), H(64), H(96), H(48), H(NV)
+    jI = ts(I1(), lane, 31, A.bitwise_and, 1, A.logical_shift_right)
+    oI = ts(I1(), lane, 1, A.bitwise_and)
+    iI = ts(I1(), lane, 15, A.bitwise_and)
+    cut = ts(F1(), jI, -15.9375, MUL, 0.0625, ADD)
+    bI = ts(I1(), lane, 31, A.bitwise_and)
+    iF = ts(F1(), iI, 0.0, ADD)
+    f1 = ts(H(64), jj, 15.9375, MUL, cut, ADD)
+    sig = ts(F1(), oI, -2.0, MUL, 1.0, ADD)
+    ft = H(256)
+    ts(sub(ft, 0, 64), f1, 0.0625, MAX, 16.0, MIN)
+    bF = ts(F1(), bI, -16.0, MUL)
+    for a in range(128, 640, 128):
+        put(V("zt", a, a + 128), 0.0)
+    put(V("xt", 1024, 1088), 0.0)
+    z = reduce(F1(), sub(ft, 0, 16), MUL)
+    eq = scan(F(16), sub(ft, 0, 16), sub(ones, 0, 16))
+    rz = F1()
+    run("v", [rz], [z], lambda e: e.reciprocal(ap(rz), ap(z)))
+    for a in (64, 128, 192):
+        act(sub(ft, a, a + 64), sub(ft, 0, 64), AF.Copy)
+    fill(ra, CARRY)
+    la = ts(F(3), t_l, iF, ADD, 39.0, MIN)
+    fill(col(cells, 271), 0.0)
+    lb = ts(new("aI", 3), la, 0.2, MUL, -0.4, ADD)
+    thr = ts(F1(), col(eq, 15), LEVEL, MUL)
+    lc = ts(F(3), lb, 11.0, MUL)
+    fill(col(ra, 1), 1.0 if r == N - 1 else 0.0)
+    ld = tt(F(3), lc, la, ADD)
+    ts(sub(ft, 0, 256, 16), sub(ones, 0, 16), rz, MUL, CARRY / 16, MUL)
+
+    halo = [(k, a, b) for k, a, b in ((r + 1, 16, UP), (r - 1, 0, DOWN)) if 0 <= k < N]
     wide = lambda k: 8 // sum(0 <= j < N for j in (k - 1, k + 1))
-    quant("e", 0, 128, "zt", 0)
-    for n, bits, rsem in (("q", True, "rhc"), ("s", False, "rhs")):
+
+    def send_halo(n, bits, rsem):
         at = lambda m, a: V(m + n, a, a + 16)
         send([(k, at("e", a), at("gr", b)) for k, a, b in halo], wide(r), bits, rsem, "lhalo",
              [at("e", a) for k, a, b in halo], sum(wide(k) for k, a, b in halo))
         for k, a, b in halo:
-            note(at("gr", 0 if k < r else 272), True, None, rsem, count[rsem], {})
-    t_e = iota(new("aF", 2), [[2, 2]], 1)
-    t_y = const(new("aF", 2), 16 * r)
-    t_l = iota(new("aF", 3), [[16, 3]], -1)
-    t_d = new("aF", 8)
-    nb = (N - r + 1) // 2
-    iota(sub(t_d, 0, 2 * nb), [[-16, nb], [0, 2]], 383 - 8 * r)
-    if nb < 4:
-        iota(sub(t_d, 2 * nb, 8), [[-16, 4 - nb], [0, 2]], 383 - 8 * ((r + 2 * nb) % N))
+            note(at("gr", UP if k < r else DOWN), True, None, rsem, count[rsem], {})
+
+    quant("e", 0, 128, "zt", 0)
+    send_halo("q", True, "rhc")
 
     for t in (1, 2, 3):
-        act(V("ut", t, 512, 4), ones, AF.Identity, 0.0, V("uc", t, t + 1))
-    ts(V("ut", 0, 512, 4), ones, V("uc", 0, 1), MUL)
-    for a in (64, 128, 192):
-        act(sub(ft, a, a + 64), sub(ft, 0, 64), AF.Copy)
-    if r == 0:
-        fill(V("xt", 0, 64), 0.0)
-    sgn, cells = new("aH", 256), new("aH", 256)
+        lin(V("ut", t, 512, 4), sub(ones, 0, 128), 0.0, V("uc", t, t + 1))
+    ts(V("ut", 0, 512, 4), sub(ones, 0, 128), V("uc", 0, 1), MUL)
+    sgn = H(256)
     for h in (0, 1):
-        a = 0 if r == 0 and h == 0 else 16 + 128 * h
-        quant("gr", a, 144 + 128 * h, "xt", 4 * a)
+        a = 128 * h
+        quant("gr", a, a + 128 + 16 * h, "xt", 4 * a)
         if h == 0:
             quant("u", 0, 128, "ut", 0)
-        a = 16 + 128 * h
         mm(V("ps", 512 * h, 512 * h + 128), V("uq", 0, 128), V("us", 0, 128), V("grq", a, a + 128), V("grs", a, a + 128), True, True)
-    run("v", [nrm], [sub(eq, 15, 16)], lambda e: e.reciprocal(ap(nrm), ap(sub(eq, 15, 16))))
+    spare += [lambda: fill(sub(Z, 15, 80), 0.0), lambda: fill(sub(win, 0, 128), float(ZERO - MID))]
     for h in (0, 1):
-        ts(sub(sgn, 128 * h, 128 * h + 128), V("ps", 512 * h, 512 * h + 128), 0.0, A.is_gt, -0.5, ADD)
-    scan(cells, ft, sgn)
-    own = V("sg", 16 * r, 16 * r + 16)
-    ts(own, sub(cells, 15, 256, 16), nrm, MUL)
-    send([(k, own, own) for k in others], 1, False, "rsign", "lsign", [own], N - 1)
+        ts(sub(sgn, 128 * h, 128 * h + 128), V("ps", 512 * h, 512 * h + 128), sig, MUL, 0.0, GT)
+    gap()
+    scan(sub(cells, 0, 256), ft, sgn, col(eq, 15) if r == 0 else 0.0)
+    gap()
+    own = scan(H(NV), ra, sub(cells, 15, 272, -16), col(cells, 255))
+    seen = lambda k: V("sg", NV * (N - 1 - k), NV * (N - k))
+    send([(k, own, seen(r)) for k in others], 1, False, "rsign", "lsign", [own], N - 1)
     for k in others:
-        note(V("sg", 16 * k, 16 * k + 16), True, None, "rsign", count["rsign"], {})
+        note(seen(k), True, None, "rsign", count["rsign"], {})
+    send_halo("s", False, "rhs")
     g.sync.wait_ge(T.sem["lsign"], count["lsign"])
     known["y"]["lsign"] = count["lsign"]
-    for k, (a, b) in enumerate(((0, 2048), (2048, 4096), (4096, 5120))):
+    for k, (a, b) in ((1, (EARLY, 3072)), (2, (3072, 5120))):
         dma("y", V("wt", a, b), T.w[:, a:b], "dw%d" % k)
+    t_d = F(8)
+    nb = (N - r + 1) // 2
+    iota(sub(t_d, 0, 2 * nb), [[16, nb], [0, 2]], 8 * r)
+    if nb < 4:
+        iota(sub(t_d, 2 * nb, 8), [[16, 4 - nb], [0, 2]], 8 * ((r + 2 * nb) % N))
+    npt = F(256)
+    iota(sub(npt, 0, 32), [[0, 2], [128, 2], [2, 8]], 16 * r + 1)
+    XS = iota(H(32), [[0, 32]], 1000)
+    r32 = asel(H(256), iota(H(256), [[0, 256]], 1), [[0, 8], [1, 32]], NE, 0.0, 0)
 
-    t_tr = iota(new("aF", 16), [[1, 16]], (1 << 20) - 256)
-    base = iota(new("aH", 256), [[-1, 16], [16, 16]], 31 - MID)
-    onef = const(new("aF", 32), 1)
-    rs = asel(new("aF", 32), asel(new("aF", 32), onef, [[1, 32]], NE, 0.0, 0), [[1, 32]], NE, -1.0, -16)
-    win = const(new("aH", 384), MID)
-    XS = const(new("aH", 32), 1000)
-    npt = new("aF", 256)
-    for a in range(8):
-        iota(sub(npt, 32 * a, 32 * a + 32), [[0, 2], [128, 2], [2, 8]], 256 * a + 16 * r + 3)
-    r32 = asel(new("aH", 256), const(new("aH", 256), 1), [[0, 8], [1, 32]], NE, 0.0, 0)
-
-    alpha = act(new("aH", 128), ones, AF.Copy, scale=1.0 / 32)
-    lo = ts(F1(), bm, 0.0, LT)
-    one0 = ts(F1(), bm, -15.5, EQ)
-    iF = ts(F1(), ts(new("aI", 1), lane, 15, A.bitwise_and), 0.0, ADD)
-    d0 = act(new("aH", 128), ones, AF.Copy, scale=lo)
-    hb = act(F1(), bm, AF.Identity, 0.5 * turn, 7.75 * turn)
-    s1 = act(F1(), iF, AF.Identity, 1.0 - 0.5 * turn, hb)
-    off_y = ts(new("aU", 2), t_y, iF, ADD)
-    high = ts(F1(), iF, 8.0, GE, 56.0, MUL)
-    la = ts(new("aF", 3), t_l, iF, ADD, 39.0, MIN)
-    lb = ts(new("aI", 3), la, 0.2, MUL, -0.4, ADD)
-    e13 = ts(new("aF", 2), t_e, iF, EQ)
-    n13 = ts(new("aF", 2), t_e, iF, NE)
-    lc = ts(new("aF", 3), lb, 11.0, MUL)
-    off_d = ts(new("aU", 8), t_d, s1, SUB, high, SUB)
-    ld = tt(new("aF", 3), lc, la, ADD)
-    off_l = ts(new("aU", 3), ld, 0.0, MAX)
-    quant("gr", 288 if r < N - 1 else 272, 416 if r < N - 1 else 400, "zt", 128)
-    quant("la", SL * N + 16, LW, "zt", 128)
-    i16 = act(F1(), iF, AF.Copy, scale=16.0)
-    trash = act(new("aF", 16), t_tr, AF.Identity, bias=i16)
-    sx = act(F1(), iF, AF.Identity, bias=-2.0)
+    sx = lin(F1(), iF, 1.0, -2.0)
+    hs = lin(F1(), sig, 0.5)
     sx2 = act(F1(), sx, AF.Square)
-    delta = act(F1(), act(F1(), sx2, AF.Identity, 7.0 / 3, -4.0 / 3), AF.Copy, scale=sx)
-    z1 = act(F1(), sub(e13, 0, 1), AF.Identity, float(MID + 1), delta)
-    z3 = act(F1(), sub(e13, 1, 2), AF.Identity, float(MID - 1), delta)
-    val = new("aH", 256)
-    act(sub(val, 16, 240), sub(base, 16, 240), AF.Identity, 1.0, delta)
-    act(sub(val, 0, 16), sub(base, 0, 16), AF.Identity, sub(n13, 1, 2), z3)
-    act(sub(val, 240, 256), sub(base, 240, 256), AF.Identity, sub(n13, 0, 1), z1)
+    d5 = act(F(8), sub(pos, 0, 8), AF.Abs, -1.0, sx)
+    put(rs, 1.0)
+    sx3 = lin(F1(), sx2, 7.0 / 3, -4.0 / 3)
+    put(d96, 1.0)
+    no5 = act(F(8), d5, AF.Sign)
+    is5 = act(F(8), d5, AF.Relu, -1.0, 1.0)
+    delta = act(F1(), sx3, AF.Copy, scale=sx)
+    put(col(rs, 16), 0.0)
+    i16 = lin(F1(), iF, 16.0)
+    for a in (64, 128, 192):
+        lin(sub(base, a, a + 64), sub(base, 0, 64), 1.0, a / 16.0)
+    z1 = lin(F1(), col(is5, 1), float(ZERO - MID + 1), delta)
+    z3 = lin(F1(), col(is5, 3), float(ZERO - MID - 1), delta)
+    put(col(d96, 32), 4096.0)
+    put(col(d96, 64), 1.0 / 4096)
+    w2 = lin(F(16), t_w, 1.0, i16)
+    i2 = lin(F1(), iF, 2.0)
+    val, vb = H(256), H(32)
+    lin(sub(val, 16, 240), sub(base, 16, 240), 1.0, delta)
+    for a in (16, 32):
+        act(sub(Z, a, a + 16, 15), sub(ones, 0, 2), AF.Copy, scale=hs)
+    lin(sub(val, 0, 16), sub(base, 0, 16), col(no5, 1), z1)
+    lin(sub(val, 240, 256), sub(base, 240, 256), col(no5, 3), z3)
+    d0 = act(F(36), pos, AF.Abs, -1.0, i2)
+    up = lin(F1(), col(is5, 0), float((UP if r > 0 else ZERO) + 16))
+    down = lin(F1(), col(is5, 4), float((DOWN if r < N - 1 else ZERO) - 256))
+    e0 = act(F(36), d0, AF.Relu, -1.0, 1.0)
+    s8 = act(F1(), iF, AF.Sign, 1.0, -7.5)
+    s16 = act(F1(), bF, AF.Sign, -1.0, -248.0)
+    wa = lin(F1(), iF, -1.0, 15.0)
+    wb = lin(F1(), iF, 1.0 / (256 * 271), -1.0 - 1.0 / 256)
+    lin(sub(vb, 0, 16), sub(val, 0, 256, 16), 1.0, up)
+    lin(sub(vb, 16, 32), sub(val, 15, 256, 16), 1.0, down)
+    GT_, dg, dA, dB = F(72), F(72), F(72), F(72)
+    lin(sub(dA, 0, 32), sub(e0, 0, 32), wa, 1.0)
+    lin(sub(dA, 32, 65), sub(e0, 0, 33), float(2 ** 20 - 1), 1.0)
+    lin(sub(dB, 0, 32), sub(e0, 2, 34), -1.0)
+    lin(sub(dB, 32, 65), sub(e0, 2, 35), wb)
+    c0 = lin(F1(), iF, -1.0, 143.0)
+    wlast = lin(F1(), iF, 2.0 ** -20, 256 * 2.0 ** -20)
+    padc = lin(F1(), iF, 4.0, 226.0)
+    i4 = lin(F1(), iF, -1.0, 63.5 - 28 - 16 * max(r - 1, 0))
+    hb = lin(F1(), s16, 4.0 * turn, 63.5 + 4 * turn)
+    put(col(PT, 32), ROUND)
+    put(col(PT, 33), -ROUND)
+    i5 = lin(F1(), s8, -28.0, i4)
 
-    SV, X = new("aH", 128), new("aH", 128)
-    sg = V("sg", 0, 128)
-    act(sub(SV, 0, 127), sub(sg, 1, 128), AF.Sign)
-    st = scan(new("aH", 128), alpha, sg, sub(sg, 0, 1))
-    ts(sub(SV, 127, 128), sub(sg, 127, 128), -1.0, MAX, 1.0, MIN)
-    pr = tt(new("aH", 128), st, SV, MUL)
-    av = ts(new("aH", 128), pr, 18.0, LT)
-    scan(X, d0, av, one0)
+    for a in (17, 33):
+        ts(sub(Z, a, a + 14), sub(own, 2, 16, -1), thr, LT, -0.5, ADD)
+    PI = H(96)
+    th0, th15 = F1(), F1()
+    spare += [lambda: fill(fd, 0.0), lambda: ts(th0, col(own, 16), thr, SUB), lambda: fill(sub(fd, 0, 136, NV), 1.0),
+              lambda: ts(th15, col(own, 1), thr, SUB, 1.0 / CARRY, MUL), lambda: fill(sub(fd, 1, 136, NV), CARRY),
+              lambda: fill(sub(XB, 144, 176), 0.0)]
+    off_l = ts(new("aU", 3), ld, 0.0, MAX)
+    gap()
+    AC = scan(H(64), rs, sub(Z, 15, 79))
+    tr(sub(PI, 64, 96), sub(Z, 16, 48))
+    gap()
+    tr(sub(PI, 0, 64), AC)
+    idle = tt(F(16), sub(PI, 64, 96, 2), sub(PI, 65, 96, 2), NE)
+    gap()
+    num = scan(F(96), d96, PI)
+    away = tt(F(16), idle, w2, MUL)
+    ci = reduce(F1(), sub(PI, 32, 64), ADD)
+    o6 = tt(F(16), sub(num, 65, 96, 2), away, ADD)
+    gap(2)
+    off = ts(new("aU", 16), o6, -1.0, ADD)
+    gap()
+    tt(sub(dg, 0, 65), sub(dA, 0, 65), sub(dB, 0, 65), ADD)
+    scatter(win, off, val)
+    lin(col(GT_, 64), ci, 2.0, padc)
+    put(col(dg, 32), 0.0)
+    act(col(dg, 64), col(dg, 64), AF.Copy, scale=wlast)
+    tabd = lin(F(8), t_d, 1.0, hb)
 
-    Y = gather(new("aH", 32), X, off_y)
-    act(sub(XS, 0, 8), sub(X, 15, 128, 16), AF.Copy)
-    lbk = [act(F1(), iF, AF.Identity, bias=16.0 + 16 * k + 16 * SL) for k in range(5)]
-    YT = tr(new("aH", 32), Y)
-    S6 = scan(new("aF", 32), rs, YT)
-    V6 = tt(new("aI", 16), sub(S6, 16, 32), sub(YT, 16, 32), MUL)
-    A6 = ts(new("aI", 16), V6, 127 | 1 << 20, A.bitwise_and)
-    o6 = tt(new("aF", 16), A6, trash, MAX)
-    off = ts(new("aU", 16), o6, float((1 << 20) - 256), SUB)
-    run("v", [win], [off, val], lambda e: e.tensor_copy(ap(win).indirect(ap(off)), ap(val)))
-    D = gather(new("aH", 128), win, off_d)
-    DT = tr(new("aH", 128), D)
+    G = F(64)
+    act(sub(G, 0, 32), sub(ones, 0, 32), AF.Sign, th0, col(seen(r - 1), 0) if r > 0 else 0.0)
+    act(sub(G, 32, 64), sub(ones, 0, 32), AF.Sign, th15, col(seen(r + 1), 16) if r < N - 1 else 0.0)
+    fx, sb = H(144), H(176)
+    n = NV * r
+    if r > 0:
+        scan(sub(fx, 144 - n, 144), sub(fd, 0, n), V("sg", 136 - n, 136), col(own, 16))
+        ts(sub(XB, 144 - n, 144), sub(fx, 144 - n, 144), thr, LT, -0.5, ADD)
+    else:
+        n = 1
+        ts(col(XB, 143), col(own, 16), thr, LT, -0.5, ADD)
+    tr(sub(GT_, 0, 64), G)
+    scan(sub(sb, 144 - n, 176), sub(ones, 0, n + 32), sub(XB, 144 - n, 176))
+    FB = scan(F(65), sub(dg, 0, 65), sub(GT_, 0, 65))
+    tr(sub(PT, 0, 32), sub(sb, 144, 176))
+    offb = ts(new("aU", 2), sub(FB, 31, 65, 33), 0.5, MUL, c0, ADD)
+    w5 = scan(F(34), sub(ones, 0, 34), sub(PT, 0, 34), i5)
+    scatter(win, offb, vb)
+    off_d = ts(new("aU", 8), tabd, col(w5, 31), SUB, col(w5, 33), ADD)
+    cp(sub(win, 128, 192), sub(win, 0, 64))
+    m = NV * (N - 1 - r)
+    if m:
+        scan(sub(fx, 8, 8 + m), sub(fd, 0, m), V("sg", 0, m))
+    D = gather(H(128), sub(win, 0, 192), off_d)
+    scan(sub(fx, 8 + m, 8 + m + NV), sub(fd, 0, NV), own, V("sg", m - 1, m) if m else 0.0)
+    DT = tr(H(128), D)
+    m = min(m + NV, 136 - n)
+    ts(sub(XB, 8, 8 + m), sub(fx, 8, 8 + m), thr, LT, -0.5, ADD)
     lw = new("aU", 48)
     run("v", [lw], [DT, off_l], lambda e: e.tensor_scalar(ap(lw), ap(DT).indirect(ap(off_l)), float(MID), None, ADD))
+    X = scan(H(136), sub(ones, 0, 136), sub(XB, 8, 144, -1))
+    for a in range(1, 8):
+        lin(sub(npt, 32 * a, 32 * a + 32), sub(npt, 0, 32), 1.0, 256.0 * a)
+    lbk = [lin(F1(), iF, 1.0, 16.0 + 16 * k + 16 * SL) for k in range(5)]
 
-    gq, gs = V("grq", 0, 304), V("grs", 0, 304)
+    gq, gs = V("grq", 0, PW), V("grs", 0, PW)
     home = lambda n, k: V(n, SL * k + 16, SL * k + SL)
     slot = lambda n, i: V(n, NC * i, NC * i + NC)
     for a, b in ((4, 7), (0, 4)):
@@ -339,19 +437,21 @@ def rank_program(g, core, T, topo):
             for k in others:
                 note(home("la" + n, k), True, None, m, count[m], {})
 
-    XT = tr(new("aH", 32), XS)
-    C = minus_total(F1(), sub(XT, 0, 16))
-    ind = act(new("aH", 256), npt, AF.Sign, 0.5, C)
+    cp(sub(XS, 0, 8), sub(X, 15, 136, NV))
     pickc(V("laq", SL * r, SL * r + SL), gq, sub(lw, 0, 6))
+    XT = tr(H(32), XS)
+    quant("la", SL * N + 16, LW, "zt", 128)
+    C = scan(F(32), sub(ones, 0, 32), XT, bF)
+    quant("w", 0, 256, "wt", 0)
+    ind = act(H(256), npt, AF.Sign, -0.5, col(C, 31))
     gather(V("las", SL * r, SL * r + SL), gs, sub(lw, 0, 6), "s")
-    quant("w", 0, 512, "wt", 0)
-    it = tr(new("aH", 256), ind)
-    iq = scan(new("aH", 256), r32, it)
-    lf, lu = new("aF", 40), new("aU", 40)
+    it = tr(H(256), ind)
+    quant("w", 256, 768, "wt", 1024)
+    iq = scan(H(256), r32, it)
+    lf, lu = F(40), new("aU", 40)
     for k in range(5):
-        act(sub(lf, 8 * k, 8 * k + 8), sub(iq, 31, 256, 32), AF.Identity, SL / 2.0, lbk[k])
-    for a, b in ((512, 1024), (1024, 1280)):
-        quant("w", a, b, "wt", 4 * a)
+        lin(sub(lf, 8 * k, 8 * k + 8), sub(iq, 31, 256, 32), -SL / 2.0, lbk[k])
+    quant("w", 768, 1280, "wt", 3072)
     ts(lu, lf, 0.0, ADD)
 
     tk = lambda n, k: V(n, 128 * k, 128 * k + 128)

@@ -13,17 +13,20 @@ NV = 17
 CARRY = 1.0 / 16
 LEVEL = 1.096
 ROUND = 1.5 * 2 ** 30
-EARLY = 1024
+EARLY = 3072
 F8, U8, BF, F32 = "float8_e4m3fn_x4", "uint8", "bfloat16", "float32"
-SCRATCH = {"aF": ("sbuf", [128, 4096], F32), "aH": ("sbuf", [128, 6144], BF), "aI": ("sbuf", [128, 256], "int32"),
+SCRATCH = {"aF": ("sbuf", [128, 4096], F32), "aH": ("sbuf", [128, 8192], BF), "aI": ("sbuf", [128, 256], "int32"),
            "aU": ("sbuf", [128, 512], "uint16"), "sg": ("sbuf", [128, 144], BF), "xt": ("sbuf", [128, 1088], BF),
            "uc": ("sbuf", [128, 16], BF), "ut": ("sbuf", [128, 512], BF), "wt": ("sbuf", [128, 5120], BF), "zt": ("sbuf", [128, 640], BF),
            "yo": ("sbuf", [128, 256], F32), "ps": ("psum", [128, 2048], F32)}
 for _n, _w in (("e", 128), ("u", 128), ("w", 1280), ("gr", PW), ("sl", NC * 7), ("la", LW), ("t", 640)):
     SCRATCH[_n + "q"] = ("sbuf", [128, _w], F8)
     SCRATCH[_n + "s"] = ("sbuf", [128, _w], U8)
+SCRATCH.update({"hes": ("sbuf", [128, 64], U8), "hdq": ("sbuf", [128, NC], F8), "hds": ("sbuf", [128, 4 * NC], U8)})
+RELAYED = (4, 6)
+PLANES = ((0, 0), (3, 4))
 DMAS = ["de0", "de1", "dx0", "dx1", "du", "dw0", "dw1", "dw2", "dy0", "dy1"]
-SEMAPHORES = ["qv", "qs", "qt", "qg"] + DMAS + ["rsign", "lsign", "rhc", "rhs", "lhalo", "rlc", "rls", "lland"]
+SEMAPHORES = ["qv", "qs", "qt", "qg"] + DMAS + ["rsign", "lsign", "rhc", "rhs", "lhalo", "rlc", "rls", "lland", "h0", "h1", "h2"]
 A = AluOpType
 AF = ActivationFunctionType
 AX = AxisListType.X
@@ -31,10 +34,66 @@ MUL, ADD, SUB, MAX, MIN = A.mult, A.add, A.subtract, A.max, A.min
 EQ, NE, LT, GE, GT = A.is_equal, A.not_equal, A.is_lt, A.is_ge, A.is_gt
 
 
+def fused(g, T, topo, writes, lsem):
+    xs = []
+    for to, src, dst, engines, rsem in writes:
+        rid, pid, _ = topo.addr(to)
+        a, b = T[src[0]][:, src[1]:src[2]], T[dst[0]][:, dst[1]:dst[2]]
+        if SCRATCH[src[0]][2] == F8:
+            a, b = a.bitcast(dt.uint8), b.bitcast(dt.uint8)
+        xs.append(RemoteDMATransfer(dst_ids=[DstId(rid=rid, pnc=pid)], dma_engine_mask=sum(1 << e for e in engines),
+                                    remote_sem=T.sem[rsem], src=a, dst=b))
+    g.remote_dma_fused(xs, local_sem=T.sem[lsem])
+    return sum(len(w[3]) for w in writes)
+
+
+def ranks_after(r):
+    turn = 1 if r % 2 == 0 else -1
+    return [d for b in range(0, N, 2) for d in ((r + b) % N, (r + b) % N + turn)]
+
+
+def helpers(core, T, topo):
+    return [c for c in topo.cores_of(core) if topo.die(c) != topo.die(core) and all(topo.may_write(c, d) for d in T.cores)]
+
+
+def share(engines, k, n):
+    w = len(engines) // n
+    return engines[w * k:w * k + w]
+
+
+def neighbours(r):
+    return [(k, a, b) for k, a, b in ((r + 1, 16, UP), (r - 1, 0, DOWN)) if 0 <= k < N]
+
+
+def home(n, k):
+    return (n, SL * k + 16, SL * k + SL, 1)
+
+
+def hand_on(g, core, T, topo):
+    mine = [c for c in topo.cores_of(core) if T.rank_of(c) is not None]
+    if not mine or core not in helpers(mine[0], T, topo):
+        return
+    r, h = T.rank_of(mine[0]), helpers(mine[0], T, topo).index(core)
+    others = ranks_after(r)[1:]
+    out = topo.engines(core, T.cores[others[0]])
+    near = neighbours(r)
+    a, b = PLANES[h]
+    n = 0
+    for sem, writes in (
+            ("h0", [(T.cores[k], ("hes", c + 8 * h, c + 8 * h + 8), ("grs", d + 8 * h, d + 8 * h + 8), share(out, i, len(near)), "rhs")
+                    for i, (k, c, d) in enumerate(near)]),
+            ("h1", [(T.cores[others[i]], ("hds", NC * (i - a), NC * (i - a + 1)), home("las", r), share(out, i - a, 4), "rls")
+                    for i in range(b, a + 4)]),
+            ("h2", [(T.cores[others[RELAYED[h]]], ("hdq", 0, NC), home("laq", r), out, "rlc")])):
+        g.wait_ge(T.sem[sem], 4)
+        n += fused(g, T, topo, writes, "lland")
+    g.wait_ge(T.sem["lland"], n)
+
+
 def rank_program(g, core, T, topo):
     r = T.rank_of(core)
     if r is None:
-        return
+        return hand_on(g, core, T, topo)
     queues = {"v": g.vector, "s": g.scalar, "t": g.tensor, "g": g, "y": g.sync}
     csem = {"v": "qv", "s": "qs", "t": "qt", "g": "qg"}
     count = {}
@@ -182,21 +241,14 @@ def rank_program(g, core, T, topo):
         if not start:
             note(o, True, "t", "qt", count["qt"], dict(known["t"]))
 
-    def send(pairs, width, bits, rsem, lsem, ins, arrive):
-        sync("g", [], ins)
-        xs = []
-        for k, (d, src, dst) in enumerate(pairs):
-            to = T.cores[d]
-            rid, pid, _ = topo.addr(to)
-            a, b = ap(src), ap(dst)
-            if bits:
-                a, b = a.bitcast(dt.uint8), b.bitcast(dt.uint8)
-            mask = sum(1 << e for e in topo.engines(core, to)[width * k:width * k + width])
-            xs.append(RemoteDMATransfer(dst_ids=[DstId(rid=rid, pnc=pid)], dma_engine_mask=mask,
-                                        remote_sem=T.sem[rsem], src=a, dst=b))
-        g.remote_dma_fused(xs, local_sem=T.sem[lsem])
-        count[lsem] = count.get(lsem, 0) + width * len(xs)
-        count[rsem] = count.get(rsem, 0) + arrive
+    def send(writes, lsem):
+        sync("g", [], [w[1] for w in writes])
+        count[lsem] = count.get(lsem, 0) + fused(g, T, topo, writes, lsem)
+
+    def lands(views, rsem, n):
+        count[rsem] = count.get(rsem, 0) + n
+        for v in views:
+            note(v, True, None, rsem, count[rsem], {})
 
     spare = []
 
@@ -206,9 +258,11 @@ def rank_program(g, core, T, topo):
 
     F1 = lambda: new("aF", 1)
     H, F, I1 = lambda n: new("aH", n), lambda n: new("aF", n), lambda: new("aI", 1)
-    turn = 1 if r % 2 == 0 else -1
-    order = [d for b in range(0, N, 2) for d in ((r + b) % N, (r + b) % N + turn)]
-    others = order[1:]
+    others = ranks_after(r)[1:]
+    turn = others[0] - r
+    aides = helpers(core, T, topo)
+    out = topo.engines(core, T.cores[others[0]])
+    inner = [e for e in topo.engines(core, aides[0]) if e not in out]
 
     dma("y", V("uc", 0, 8), T.u[:, 0:8], "du")
     dma("s", V("zt", 64, 128), T.x[:, 960:1024], "de1")
@@ -222,7 +276,7 @@ def rank_program(g, core, T, topo):
     pos = iota(F(36), [[1, 36]], -2)
     base = H(256)
     iota(sub(base, 0, 64), [[1, 4], [16, 16]], -MID)
-    t_w = iota(F(16), [[1, 16]], 200)
+    w2 = iota(F(16), [[1, 16]], 200, 16)
     t_l = iota(F(3), [[16, 3]], -1)
 
     ones = fill(H(160), 1.0)
@@ -230,7 +284,7 @@ def rank_program(g, core, T, topo):
     def put(o, c):
         return act(o, sub(ones, 0, len(range(o[1], o[2], o[3]))), AF.Copy, scale=c)
 
-    win, cells, Z, XB, fd, rs, d96, PT, ra = H(592), H(272), H(80), H(176), H(136), H(64), H(96), H(48), H(NV)
+    win, cells, Z, XB, fd, rs, d96, PT, ra = H(2400), H(272), H(80), H(176), H(136), H(64), H(96), H(48), H(NV)
     jI = ts(I1(), lane, 31, A.bitwise_and, 1, A.logical_shift_right)
     oI = ts(I1(), lane, 1, A.bitwise_and)
     iI = ts(I1(), lane, 15, A.bitwise_and)
@@ -249,57 +303,58 @@ def rank_program(g, core, T, topo):
     eq = scan(F(16), sub(ft, 0, 16), sub(ones, 0, 16))
     rz = F1()
     run("v", [rz], [z], lambda e: e.reciprocal(ap(rz), ap(z)))
-    for a in (64, 128, 192):
-        act(sub(ft, a, a + 64), sub(ft, 0, 64), AF.Copy)
-    fill(ra, CARRY)
-    la = ts(F(3), t_l, iF, ADD, 39.0, MIN)
-    fill(col(cells, 271), 0.0)
-    lb = ts(new("aI", 3), la, 0.2, MUL, -0.4, ADD)
-    thr = ts(F1(), col(eq, 15), LEVEL, MUL)
-    lc = ts(F(3), lb, 11.0, MUL)
-    fill(col(ra, 1), 1.0 if r == N - 1 else 0.0)
-    ld = tt(F(3), lc, la, ADD)
-    ts(sub(ft, 0, 256, 16), sub(ones, 0, 16), rz, MUL, CARRY / 16, MUL)
+    quant("la", SL * N + 16, LW, "zt", 128)
+    GT_, dg, dA, dB = F(72), F(72), F(72), F(72)
+    d0 = act(F(36), pos, AF.Abs, -0.5, iF)
+    wa = lin(F1(), iF, -1.0, 15.0)
+    e0 = act(F(36), d0, AF.Relu, -2.0, 1.0)
+    wb = lin(F1(), iF, 1.0 / (256 * 271), -1.0 - 1.0 / 256)
+    act(sub(ft, 64, 128), sub(ft, 0, 64), AF.Copy)
+    for t in (0, 1):
+        lin(V("ut", t + 2, 512, 4), sub(ones, 0, 128), 0.0, V("uc", t + 2, t + 3))
+        ts(V("ut", t, 512, 4), sub(ones, 0, 128), V("uc", t, t + 1), MUL)
+    lin(sub(dA, 32, 65), sub(e0, 0, 33), float(2 ** 20 - 1), 1.0)
+    lin(sub(dB, 0, 32), sub(e0, 2, 34), -1.0)
+    lin(sub(dA, 0, 32), sub(e0, 0, 32), wa, 1.0)
+    lin(sub(dB, 32, 65), sub(e0, 2, 35), wb)
+    put(ra, CARRY)
+    put(col(cells, 271), 0.0)
+    thr = lin(F1(), col(eq, 15), LEVEL)
+    put(col(ra, 1), 1.0 if r == N - 1 else 0.0)
 
-    halo = [(k, a, b) for k, a, b in ((r + 1, 16, UP), (r - 1, 0, DOWN)) if 0 <= k < N]
-    wide = lambda k: 8 // sum(0 <= j < N for j in (k - 1, k + 1))
-
-    def send_halo(n, bits, rsem):
-        at = lambda m, a: V(m + n, a, a + 16)
-        send([(k, at("e", a), at("gr", b)) for k, a, b in halo], wide(r), bits, rsem, "lhalo",
-             [at("e", a) for k, a, b in halo], sum(wide(k) for k, a, b in halo))
-        for k, a, b in halo:
-            note(at("gr", UP if k < r else DOWN), True, None, rsem, count[rsem], {})
-
+    near = neighbours(r)
     quant("e", 0, 128, "zt", 0)
-    send_halo("q", True, "rhc")
+    send([(T.cores[k], V("eq", a, a + 16), V("grq", b, b + 16), share(out, i, len(near)), "rhc") for i, (k, a, b) in enumerate(near)]
+         + [(c, V("es", 0, 64), V("hes", 0, 64), share(inner, h, 2), "h0") for h, c in enumerate(aides)], "lhalo")
+    wide = sum(len(out) // len(neighbours(k)) for k, a, b in near)
+    for n, rsem, m in (("grq", "rhc", 1), ("grs", "rhs", 2)):
+        lands([V(n, UP if k < r else DOWN, 16 + (UP if k < r else DOWN)) for k, a, b in near], rsem, m * wide)
 
-    for t in (1, 2, 3):
-        lin(V("ut", t, 512, 4), sub(ones, 0, 128), 0.0, V("uc", t, t + 1))
-    ts(V("ut", 0, 512, 4), sub(ones, 0, 128), V("uc", 0, 1), MUL)
     sgn = H(256)
+    quant("u", 0, 128, "ut", 0)
     for h in (0, 1):
         a = 128 * h
         quant("gr", a, a + 128 + 16 * h, "xt", 4 * a)
-        if h == 0:
-            quant("u", 0, 128, "ut", 0)
         mm(V("ps", 512 * h, 512 * h + 128), V("uq", 0, 128), V("us", 0, 128), V("grq", a, a + 128), V("grs", a, a + 128), True, True)
-    spare += [lambda: fill(sub(Z, 15, 80), 0.0), lambda: fill(sub(win, 0, 128), float(ZERO - MID))]
+    ts(sub(ft, 0, 128, 16), sub(ones, 0, 8), rz, MUL, CARRY / 16, MUL)
     for h in (0, 1):
         ts(sub(sgn, 128 * h, 128 * h + 128), V("ps", 512 * h, 512 * h + 128), sig, MUL, 0.0, GT)
-    gap()
-    scan(sub(cells, 0, 256), ft, sgn, col(eq, 15) if r == 0 else 0.0)
-    gap()
+    for h in (0, 1):
+        scan(sub(cells, 128 * h, 128 * h + 128), sub(ft, 0, 128), sub(sgn, 128 * h, 128 * h + 128),
+             col(cells, 127) if h else col(eq, 15) if r == 0 else 0.0)
+        if h == 0:
+            la = ts(F(3), t_l, iF, ADD, 39.0, MIN)
+    ts(sub(Z, 15, 80), sub(ones, 0, 65), sig, MUL, 0.5, MUL)
     own = scan(H(NV), ra, sub(cells, 15, 272, -16), col(cells, 255))
     seen = lambda k: V("sg", NV * (N - 1 - k), NV * (N - k))
-    send([(k, own, seen(r)) for k in others], 1, False, "rsign", "lsign", [own], N - 1)
-    for k in others:
-        note(seen(k), True, None, "rsign", count["rsign"], {})
-    send_halo("s", False, "rhs")
+    send([(T.cores[k], own, seen(r), share(out, i, 8), "rsign") for i, k in enumerate(others)], "lsign")
+    lands([seen(k) for k in others], "rsign", N - 1)
     g.sync.wait_ge(T.sem["lsign"], count["lsign"])
     known["y"]["lsign"] = count["lsign"]
-    for k, (a, b) in ((1, (EARLY, 3072)), (2, (3072, 5120))):
+    for k, (a, b) in ((1, (EARLY, 4096)), (2, (4096, 5120))):
         dma("y", V("wt", a, b), T.w[:, a:b], "dw%d" % k)
+    t_f = iota(H(136), [[0, 8], [-15, NV]], 16)
+    iota(sub(XB, 144, 176), [[0, 32]], 0)
     t_d = F(8)
     nb = (N - r + 1) // 2
     iota(sub(t_d, 0, 2 * nb), [[16, nb], [0, 2]], 8 * r)
@@ -311,82 +366,67 @@ def rank_program(g, core, T, topo):
     r32 = asel(H(256), iota(H(256), [[0, 256]], 1), [[0, 8], [1, 32]], NE, 0.0, 0)
 
     sx = lin(F1(), iF, 1.0, -2.0)
-    hs = lin(F1(), sig, 0.5)
+    put(rs, 1.0)
     sx2 = act(F1(), sx, AF.Square)
     d5 = act(F(8), sub(pos, 0, 8), AF.Abs, -1.0, sx)
-    put(rs, 1.0)
+    put(col(rs, 16), 0.0)
     sx3 = lin(F1(), sx2, 7.0 / 3, -4.0 / 3)
     put(d96, 1.0)
     no5 = act(F(8), d5, AF.Sign)
     is5 = act(F(8), d5, AF.Relu, -1.0, 1.0)
     delta = act(F1(), sx3, AF.Copy, scale=sx)
-    put(col(rs, 16), 0.0)
-    i16 = lin(F1(), iF, 16.0)
+    put(col(d96, 32), 4096.0)
+    put(col(d96, 64), 1.0 / 4096)
     for a in (64, 128, 192):
         lin(sub(base, a, a + 64), sub(base, 0, 64), 1.0, a / 16.0)
     z1 = lin(F1(), col(is5, 1), float(ZERO - MID + 1), delta)
     z3 = lin(F1(), col(is5, 3), float(ZERO - MID - 1), delta)
-    put(col(d96, 32), 4096.0)
-    put(col(d96, 64), 1.0 / 4096)
-    w2 = lin(F(16), t_w, 1.0, i16)
-    i2 = lin(F1(), iF, 2.0)
     val, vb = H(256), H(32)
     lin(sub(val, 16, 240), sub(base, 16, 240), 1.0, delta)
-    for a in (16, 32):
-        act(sub(Z, a, a + 16, 15), sub(ones, 0, 2), AF.Copy, scale=hs)
     lin(sub(val, 0, 16), sub(base, 0, 16), col(no5, 1), z1)
     lin(sub(val, 240, 256), sub(base, 240, 256), col(no5, 3), z3)
-    d0 = act(F(36), pos, AF.Abs, -1.0, i2)
-    up = lin(F1(), col(is5, 0), float((UP if r > 0 else ZERO) + 16))
-    down = lin(F1(), col(is5, 4), float((DOWN if r < N - 1 else ZERO) - 256))
-    e0 = act(F(36), d0, AF.Relu, -1.0, 1.0)
+    put(sub(win, 0, 128), float(ZERO - MID))
+    below = [lin(F1(), col(eq, 15), -LEVEL * c) for c in (1.0, 1.0 / CARRY)]
     s8 = act(F1(), iF, AF.Sign, 1.0, -7.5)
     s16 = act(F1(), bF, AF.Sign, -1.0, -248.0)
-    wa = lin(F1(), iF, -1.0, 15.0)
-    wb = lin(F1(), iF, 1.0 / (256 * 271), -1.0 - 1.0 / 256)
-    lin(sub(vb, 0, 16), sub(val, 0, 256, 16), 1.0, up)
-    lin(sub(vb, 16, 32), sub(val, 15, 256, 16), 1.0, down)
-    GT_, dg, dA, dB = F(72), F(72), F(72), F(72)
-    lin(sub(dA, 0, 32), sub(e0, 0, 32), wa, 1.0)
-    lin(sub(dA, 32, 65), sub(e0, 0, 33), float(2 ** 20 - 1), 1.0)
-    lin(sub(dB, 0, 32), sub(e0, 2, 34), -1.0)
-    lin(sub(dB, 32, 65), sub(e0, 2, 35), wb)
-    c0 = lin(F1(), iF, -1.0, 143.0)
-    wlast = lin(F1(), iF, 2.0 ** -20, 256 * 2.0 ** -20)
-    padc = lin(F1(), iF, 4.0, 226.0)
+    th0 = lin(F1(), col(own, 16), 1.0, below[0])
+    th15 = lin(F1(), col(own, 1), 1.0 / CARRY, below[1])
     i4 = lin(F1(), iF, -1.0, 63.5 - 28 - 16 * max(r - 1, 0))
     hb = lin(F1(), s16, 4.0 * turn, 63.5 + 4 * turn)
+    up = lin(F1(), col(is5, 0), float((UP if r > 0 else ZERO) + 16))
+    down = lin(F1(), col(is5, 4), float((DOWN if r < N - 1 else ZERO) - 256))
+    wlast = lin(F1(), iF, 2.0 ** -20, 256 * 2.0 ** -20)
+    padc = lin(F1(), iF, 4.0, 226.0)
+    lin(sub(vb, 0, 16), sub(val, 0, 256, 16), 1.0, up)
+    lin(sub(vb, 16, 32), sub(val, 15, 256, 16), 1.0, down)
+    c0 = lin(F1(), iF, -1.0, 143.0)
     put(col(PT, 32), ROUND)
     put(col(PT, 33), -ROUND)
     i5 = lin(F1(), s8, -28.0, i4)
 
+    tt(sub(dg, 0, 65), sub(dA, 0, 65), sub(dB, 0, 65), ADD)
     for a in (17, 33):
         ts(sub(Z, a, a + 14), sub(own, 2, 16, -1), thr, LT, -0.5, ADD)
     PI = H(96)
-    th0, th15 = F1(), F1()
-    spare += [lambda: fill(fd, 0.0), lambda: ts(th0, col(own, 16), thr, SUB), lambda: fill(sub(fd, 0, 136, NV), 1.0),
-              lambda: ts(th15, col(own, 1), thr, SUB, 1.0 / CARRY, MUL), lambda: fill(sub(fd, 1, 136, NV), CARRY),
-              lambda: fill(sub(XB, 144, 176), 0.0)]
-    off_l = ts(new("aU", 3), ld, 0.0, MAX)
-    gap()
+    lb = ts(new("aI", 3), la, 0.2, MUL, -0.4, ADD)
     AC = scan(H(64), rs, sub(Z, 15, 79))
     tr(sub(PI, 64, 96), sub(Z, 16, 48))
-    gap()
     tr(sub(PI, 0, 64), AC)
     idle = tt(F(16), sub(PI, 64, 96, 2), sub(PI, 65, 96, 2), NE)
-    gap()
     num = scan(F(96), d96, PI)
     away = tt(F(16), idle, w2, MUL)
-    ci = reduce(F1(), sub(PI, 32, 64), ADD)
+    lc = ts(F(3), lb, 11.0, MUL)
     o6 = tt(F(16), sub(num, 65, 96, 2), away, ADD)
-    gap(2)
+    ld = tt(F(3), lc, la, ADD)
     off = ts(new("aU", 16), o6, -1.0, ADD)
-    gap()
-    tt(sub(dg, 0, 65), sub(dA, 0, 65), sub(dB, 0, 65), ADD)
+    off_l = ts(new("aU", 3), ld, 0.0, MAX)
     scatter(win, off, val)
-    lin(col(GT_, 64), ci, 2.0, padc)
+    ci, c32 = F1(), F(32)
+    run("s", [ci, c32], [sub(PI, 32, 64)], lambda e: e.activation(ap(c32), ap(sub(PI, 32, 64)), AF.Copy, accum_out=ap(ci)))
     put(col(dg, 32), 0.0)
     act(col(dg, 64), col(dg, 64), AF.Copy, scale=wlast)
+    lin(col(GT_, 64), ci, 2.0, padc)
+    act(fd, t_f, AF.Relu, CARRY)
     tabd = lin(F(8), t_d, 1.0, hb)
 
     G = F(64)
@@ -422,25 +462,25 @@ def rank_program(g, core, T, topo):
     X = scan(H(136), sub(ones, 0, 136), sub(XB, 8, 144, -1))
     for a in range(1, 8):
         lin(sub(npt, 32 * a, 32 * a + 32), sub(npt, 0, 32), 1.0, 256.0 * a)
-    lbk = [lin(F1(), iF, 1.0, 16.0 + 16 * k + 16 * SL) for k in range(5)]
+    lbk = [lin(F1(), iF, 1.0, 16.0 + 16 * k + 16 * SL) for k in range(2)]
 
     gq, gs = V("grq", 0, PW), V("grs", 0, PW)
-    home = lambda n, k: V(n, SL * k + 16, SL * k + SL)
     slot = lambda n, i: V(n, NC * i, NC * i + NC)
+    for a, b, q in ((4, 7, "v"), (0, 4, "s")):
+        gather(V("sls", NC * a, NC * b), gs, sub(lw, 6 + 5 * a, 6 + 5 * b), q)
     for a, b in ((4, 7), (0, 4)):
         pickc(V("slq", NC * a, NC * b), gq, sub(lw, 6 + 5 * a, 6 + 5 * b))
-        gather(V("sls", NC * a, NC * b), gs, sub(lw, 6 + 5 * a, 6 + 5 * b), "s")
-    for n, bits, m, a, b, width in (("q", True, "rlc", 4, 7, 2), ("q", True, "rlc", 0, 4, 2), ("s", False, "rls", 0, 7, 1)):
-        send([(others[i], slot("sl" + n, i), home("la" + n, r)) for i in range(a, b)], width, bits, m, "lland",
-             [slot("sl" + n, i) for i in range(a, b)], width * (N - 1) if a == 0 else 0)
-        if a == 0:
-            for k in others:
-                note(home("la" + n, k), True, None, m, count[m], {})
+    direct = lambda part: [(T.cores[others[i]], slot("slq", i), home("laq", r), share(out, j, len(part)), "rlc") for j, i in enumerate(part)]
+    send([(c, V("sls", NC * PLANES[h][0], NC * (PLANES[h][0] + 4)), V("hds", 0, 4 * NC), share(inner, h, 2), "h1")
+          for h, c in enumerate(aides)], "lland")
+    send([(c, slot("slq", RELAYED[h]), V("hdq", 0, NC), share(inner, h, 2), "h2") for h, c in enumerate(aides)] + direct([5]), "lland")
+    send(direct([0, 1, 2, 3]), "lland")
+    lands([home("laq", k) for k in others], "rlc", 4 * len(out))
+    lands([home("las", k) for k in others], "rls", 2 * (N - 1))
 
-    cp(sub(XS, 0, 8), sub(X, 15, 136, NV))
-    pickc(V("laq", SL * r, SL * r + SL), gq, sub(lw, 0, 6))
+    act(sub(XS, 0, 8), sub(X, 15, 136, NV), AF.Copy)
     XT = tr(H(32), XS)
-    quant("la", SL * N + 16, LW, "zt", 128)
+    pickc(V("laq", SL * r, SL * r + SL), gq, sub(lw, 0, 6))
     C = scan(F(32), sub(ones, 0, 32), XT, bF)
     quant("w", 0, 256, "wt", 0)
     ind = act(H(256), npt, AF.Sign, -0.5, col(C, 31))
@@ -448,18 +488,15 @@ def rank_program(g, core, T, topo):
     it = tr(H(256), ind)
     quant("w", 256, 768, "wt", 1024)
     iq = scan(H(256), r32, it)
-    lf, lu = F(40), new("aU", 40)
-    for k in range(5):
-        lin(sub(lf, 8 * k, 8 * k + 8), sub(iq, 31, 256, 32), -SL / 2.0, lbk[k])
-    quant("w", 768, 1280, "wt", 3072)
-    ts(lu, lf, 0.0, ADD)
+    quant("w", 768, 1024, "wt", 3072)
+    lu = [ts(new("aU", 8), sub(iq, 31, 256, 32), -SL / 2.0, MUL, lbk[k], ADD) for k in range(2)]
+    quant("w", 1024, 1280, "wt", 4096)
 
     tk = lambda n, k: V(n, 128 * k, 128 * k + 128)
-    lk = lambda k: sub(lu, 8 * k, 8 * k + 8)
     for k in range(5):
-        pickc(tk("tq", k), V("laq", 0, LW), lk(k))
+        pickc(tk("tq", k), V("laq", 32 * (k // 2), LW), lu[k % 2])
     for k in range(5):
-        gather(tk("ts", k), V("las", 0, LW), lk(k), "ssvsv"[k])
+        gather(tk("ts", k), V("las", 32 * (k // 2), LW), lu[k % 2], "s")
     for k in range(5):
         for o in (0, 1):
             a = 128 * (2 * KW[k] + o)

@@ -13,7 +13,7 @@ NV = 17
 CARRY = 1.0 / 16
 LEVEL = 1.096
 ROUND = 1.5 * 2 ** 30
-EARLY = 3072
+EARLY = 2560
 F8, U8, BF, F32 = "float8_e4m3fn_x4", "uint8", "bfloat16", "float32"
 SCRATCH = {"aF": ("sbuf", [128, 4096], F32), "aH": ("sbuf", [128, 8192], BF), "aI": ("sbuf", [128, 256], "int32"),
            "aU": ("sbuf", [128, 512], "uint16"), "sg": ("sbuf", [128, 144], BF), "xt": ("sbuf", [128, 1088], BF),
@@ -25,6 +25,10 @@ for _n, _w in (("e", 128), ("u", 128), ("w", 1280), ("gr", PW), ("sl", NC * 7), 
 SCRATCH.update({"hes": ("sbuf", [128, 64], U8), "hdq": ("sbuf", [128, NC], F8), "hds": ("sbuf", [128, 4 * NC], U8)})
 RELAYED = (4, 6)
 PLANES = ((0, 0), (3, 4))
+PICKS = (("s", 4, 7, "v"), ("s", 0, 4, "s"), ("q", 4, 7, "v"), ("q", 0, 4, "v"))
+CALLS = ((("S", "i"),), (("R", "i"), ("D", (5,))), (("D", (0, 1, 2, 3)),))
+HORDER = (0, 1, 2)
+TAIL = "sssss"
 DMAS = ["de0", "de1", "dx0", "dx1", "du", "dw0", "dw1", "dw2", "dy0", "dy1"]
 SEMAPHORES = ["qv", "qs", "qt", "qg"] + DMAS + ["rsign", "lsign", "rhc", "rhs", "lhalo", "rlc", "rls", "lland", "h0", "h1", "h2"]
 A = AluOpType
@@ -37,12 +41,12 @@ EQ, NE, LT, GE, GT = A.is_equal, A.not_equal, A.is_lt, A.is_ge, A.is_gt
 def fused(g, T, topo, writes, lsem):
     xs = []
     for to, src, dst, engines, rsem in writes:
-        rid, pid, _ = topo.addr(to)
+        to = to if isinstance(to, list) else [to]
         a, b = T[src[0]][:, src[1]:src[2]], T[dst[0]][:, dst[1]:dst[2]]
         if SCRATCH[src[0]][2] == F8:
             a, b = a.bitcast(dt.uint8), b.bitcast(dt.uint8)
-        xs.append(RemoteDMATransfer(dst_ids=[DstId(rid=rid, pnc=pid)], dma_engine_mask=sum(1 << e for e in engines),
-                                    remote_sem=T.sem[rsem], src=a, dst=b))
+        xs.append(RemoteDMATransfer(dst_ids=[DstId(rid=topo.addr(c)[0], pnc=topo.addr(c)[1]) for c in to],
+                                    dma_engine_mask=sum(1 << e for e in engines), remote_sem=T.sem[rsem], srcs=[a], dsts=[b] * len(to)))
     g.remote_dma_fused(xs, local_sem=T.sem[lsem])
     return sum(len(w[3]) for w in writes)
 
@@ -79,13 +83,14 @@ def hand_on(g, core, T, topo):
     near = neighbours(r)
     a, b = PLANES[h]
     n = 0
-    for sem, writes in (
+    steps = (
             ("h0", [(T.cores[k], ("hes", c + 8 * h, c + 8 * h + 8), ("grs", d + 8 * h, d + 8 * h + 8), share(out, i, len(near)), "rhs")
                     for i, (k, c, d) in enumerate(near)]),
             ("h1", [(T.cores[others[i]], ("hds", NC * (i - a), NC * (i - a + 1)), home("las", r), share(out, i - a, 4), "rls")
                     for i in range(b, a + 4)]),
-            ("h2", [(T.cores[others[RELAYED[h]]], ("hdq", 0, NC), home("laq", r), out, "rlc")])):
-        g.wait_ge(T.sem[sem], 4)
+            ("h2", [(T.cores[others[RELAYED[h]]], ("hdq", 0, NC), home("laq", r), out, "rlc")]))
+    for sem, writes in [steps[k] for k in HORDER]:
+        g.wait_ge(T.sem[sem], 8 if sem == "h0" else 4)
         n += fused(g, T, topo, writes, "lland")
     g.wait_ge(T.sem["lland"], n)
 
@@ -264,9 +269,11 @@ def rank_program(g, core, T, topo):
     out = topo.engines(core, T.cores[others[0]])
     inner = [e for e in topo.engines(core, aides[0]) if e not in out]
 
-    dma("y", V("uc", 0, 8), T.u[:, 0:8], "du")
     dma("s", V("zt", 64, 128), T.x[:, 960:1024], "de1")
-    dma("y", V("zt", 0, 64), T.x[:, 0:64], "de0")
+    dma("y", V("uc", 0, 8), T.u[:, 0:8], "du")
+    dma("s", V("zt", 0, 64), T.x[:, 0:64], "de0")
+    ones = fill(H(160), 1.0)
+    sync("y", [], [ones])
     dma("s", V("xt", 0, 512), T.x[:, 0:512], "dx0")
     dma("y", V("xt", 512, 1024), T.x[:, 512:1024], "dx1")
     dma("y", V("wt", 0, EARLY), T.w[:, 0:EARLY], "dw0")
@@ -279,64 +286,50 @@ def rank_program(g, core, T, topo):
     w2 = iota(F(16), [[1, 16]], 200, 16)
     t_l = iota(F(3), [[16, 3]], -1)
 
-    ones = fill(H(160), 1.0)
-
     def put(o, c):
         return act(o, sub(ones, 0, len(range(o[1], o[2], o[3]))), AF.Copy, scale=c)
 
     win, cells, Z, XB, fd, rs, d96, PT, ra = H(2400), H(272), H(80), H(176), H(136), H(64), H(96), H(48), H(NV)
     jI = ts(I1(), lane, 31, A.bitwise_and, 1, A.logical_shift_right)
     oI = ts(I1(), lane, 1, A.bitwise_and)
+    cut = ts(F1(), jI, -1.0, MUL, -0.5, ADD)
     iI = ts(I1(), lane, 15, A.bitwise_and)
-    cut = ts(F1(), jI, -15.9375, MUL, 0.0625, ADD)
-    bI = ts(I1(), lane, 31, A.bitwise_and)
-    iF = ts(F1(), iI, 0.0, ADD)
-    f1 = ts(H(64), jj, 15.9375, MUL, cut, ADD)
     sig = ts(F1(), oI, -2.0, MUL, 1.0, ADD)
-    ft = H(256)
-    ts(sub(ft, 0, 64), f1, 0.0625, MAX, 16.0, MIN)
-    bF = ts(F1(), bI, -16.0, MUL)
-    for a in range(128, 640, 128):
+    iF = ts(F1(), iI, 0.0, ADD)
+    ft = H(128)
+    for a in range(128, 512, 128):
         put(V("zt", a, a + 128), 0.0)
-    put(V("xt", 1024, 1088), 0.0)
-    z = reduce(F1(), sub(ft, 0, 16), MUL)
-    eq = scan(F(16), sub(ft, 0, 16), sub(ones, 0, 16))
-    rz = F1()
-    run("v", [rz], [z], lambda e: e.reciprocal(ap(rz), ap(z)))
-    quant("la", SL * N + 16, LW, "zt", 128)
-    GT_, dg, dA, dB = F(72), F(72), F(72), F(72)
-    d0 = act(F(36), pos, AF.Abs, -0.5, iF)
-    wa = lin(F1(), iF, -1.0, 15.0)
-    e0 = act(F(36), d0, AF.Relu, -2.0, 1.0)
-    wb = lin(F1(), iF, 1.0 / (256 * 271), -1.0 - 1.0 / 256)
-    act(sub(ft, 64, 128), sub(ft, 0, 64), AF.Copy)
+    side = act(H(64), jj, AF.Sign, 1.0, cut)
+    back = lin(H(16), sub(side, 0, 16), -7.96875, 8.03125)
     for t in (0, 1):
         lin(V("ut", t + 2, 512, 4), sub(ones, 0, 128), 0.0, V("uc", t + 2, t + 3))
         ts(V("ut", t, 512, 4), sub(ones, 0, 128), V("uc", t, t + 1), MUL)
-    lin(sub(dA, 32, 65), sub(e0, 0, 33), float(2 ** 20 - 1), 1.0)
-    lin(sub(dB, 0, 32), sub(e0, 2, 34), -1.0)
-    lin(sub(dA, 0, 32), sub(e0, 0, 32), wa, 1.0)
-    lin(sub(dB, 32, 65), sub(e0, 2, 35), wb)
+    put(V("xt", 1024, 1088), 0.0)
+    forth = lin(H(16), sub(side, 0, 16), 7.96875, 8.03125)
+    for a in (0, 64):
+        lin(sub(ft, a, a + 64), side, 7.96875, 8.03125)
     put(ra, CARRY)
     put(col(cells, 271), 0.0)
-    thr = lin(F1(), col(eq, 15), LEVEL)
     put(col(ra, 1), 1.0 if r == N - 1 else 0.0)
 
     near = neighbours(r)
     quant("e", 0, 128, "zt", 0)
-    send([(T.cores[k], V("eq", a, a + 16), V("grq", b, b + 16), share(out, i, len(near)), "rhc") for i, (k, a, b) in enumerate(near)]
-         + [(c, V("es", 0, 64), V("hes", 0, 64), share(inner, h, 2), "h0") for h, c in enumerate(aides)], "lhalo")
+    send([(T.cores[k], V("eq", a, a + 16), V("grq", b, b + 16), share(out, i, len(near)), "rhc") for i, (k, a, b) in enumerate(near)], "lhalo")
+    send([(aides, V("es", 0, 32), V("hes", 0, 32), inner, "h0")], "lhalo")
     wide = sum(len(out) // len(neighbours(k)) for k, a, b in near)
     for n, rsem, m in (("grq", "rhc", 1), ("grs", "rhs", 2)):
         lands([V(n, UP if k < r else DOWN, 16 + (UP if k < r else DOWN)) for k, a, b in near], rsem, m * wide)
 
     sgn = H(256)
-    quant("u", 0, 128, "ut", 0)
+    rz = reduce(F1(), back, MUL)
     for h in (0, 1):
         a = 128 * h
         quant("gr", a, a + 128 + 16 * h, "xt", 4 * a)
+        if h == 0:
+            quant("u", 0, 128, "ut", 0)
         mm(V("ps", 512 * h, 512 * h + 128), V("uq", 0, 128), V("us", 0, 128), V("grq", a, a + 128), V("grs", a, a + 128), True, True)
     ts(sub(ft, 0, 128, 16), sub(ones, 0, 8), rz, MUL, CARRY / 16, MUL)
+    eq = scan(F(16), forth, sub(ones, 0, 16))
     for h in (0, 1):
         ts(sub(sgn, 128 * h, 128 * h + 128), V("ps", 512 * h, 512 * h + 128), sig, MUL, 0.0, GT)
     for h in (0, 1):
@@ -346,9 +339,10 @@ def rank_program(g, core, T, topo):
             la = ts(F(3), t_l, iF, ADD, 39.0, MIN)
     ts(sub(Z, 15, 80), sub(ones, 0, 65), sig, MUL, 0.5, MUL)
     own = scan(H(NV), ra, sub(cells, 15, 272, -16), col(cells, 255))
+    bI = ts(I1(), lane, 31, A.bitwise_and)
     seen = lambda k: V("sg", NV * (N - 1 - k), NV * (N - k))
-    send([(T.cores[k], own, seen(r), share(out, i, 8), "rsign") for i, k in enumerate(others)], "lsign")
-    lands([seen(k) for k in others], "rsign", N - 1)
+    send([([T.cores[k] for k in others], own, seen(r), out, "rsign")], "lsign")
+    lands([seen(k) for k in others], "rsign", (N - 1) * len(out))
     g.sync.wait_ge(T.sem["lsign"], count["lsign"])
     known["y"]["lsign"] = count["lsign"]
     for k, (a, b) in ((1, (EARLY, 4096)), (2, (4096, 5120))):
@@ -375,6 +369,7 @@ def rank_program(g, core, T, topo):
     no5 = act(F(8), d5, AF.Sign)
     is5 = act(F(8), d5, AF.Relu, -1.0, 1.0)
     delta = act(F1(), sx3, AF.Copy, scale=sx)
+    thr = lin(F1(), col(eq, 15), LEVEL)
     put(col(d96, 32), 4096.0)
     put(col(d96, 64), 1.0 / 4096)
     for a in (64, 128, 192):
@@ -386,25 +381,25 @@ def rank_program(g, core, T, topo):
     lin(sub(val, 0, 16), sub(base, 0, 16), col(no5, 1), z1)
     lin(sub(val, 240, 256), sub(base, 240, 256), col(no5, 3), z3)
     put(sub(win, 0, 128), float(ZERO - MID))
+    GT_, dg, dAB = F(72), F(72), F(144)
+    dA, dB = sub(dAB, 0, 72), sub(dAB, 72, 144)
+    d0 = act(F(36), pos, AF.Abs, -0.5, iF)
+    wa = lin(F1(), iF, -1.0, 15.0)
+    e0 = act(F(36), d0, AF.Relu, -2.0, 1.0)
+    wb = lin(F1(), iF, 1.0 / (256 * 271), -1.0 - 1.0 / 256)
+    wlast = lin(F1(), iF, 2.0 ** -20, 256 * 2.0 ** -20)
+    put(sub(dAB, 32, 105, 72), 0.0)
+    lin(sub(dA, 33, 65), sub(e0, 1, 33), float(2 ** 20 - 1), 1.0)
+    lin(sub(dB, 0, 32), sub(e0, 2, 34), -1.0)
+    lin(sub(dA, 0, 32), sub(e0, 0, 32), wa, 1.0)
+    lin(sub(dB, 33, 65), sub(e0, 3, 35), wb)
+    act(col(dA, 64), col(dA, 64), AF.Copy, scale=wlast)
     below = [lin(F1(), col(eq, 15), -LEVEL * c) for c in (1.0, 1.0 / CARRY)]
-    s8 = act(F1(), iF, AF.Sign, 1.0, -7.5)
-    s16 = act(F1(), bF, AF.Sign, -1.0, -248.0)
+    padc = lin(F1(), iF, 4.0, 226.0)
     th0 = lin(F1(), col(own, 16), 1.0, below[0])
     th15 = lin(F1(), col(own, 1), 1.0 / CARRY, below[1])
-    i4 = lin(F1(), iF, -1.0, 63.5 - 28 - 16 * max(r - 1, 0))
-    hb = lin(F1(), s16, 4.0 * turn, 63.5 + 4 * turn)
-    up = lin(F1(), col(is5, 0), float((UP if r > 0 else ZERO) + 16))
-    down = lin(F1(), col(is5, 4), float((DOWN if r < N - 1 else ZERO) - 256))
-    wlast = lin(F1(), iF, 2.0 ** -20, 256 * 2.0 ** -20)
-    padc = lin(F1(), iF, 4.0, 226.0)
-    lin(sub(vb, 0, 16), sub(val, 0, 256, 16), 1.0, up)
-    lin(sub(vb, 16, 32), sub(val, 15, 256, 16), 1.0, down)
-    c0 = lin(F1(), iF, -1.0, 143.0)
-    put(col(PT, 32), ROUND)
-    put(col(PT, 33), -ROUND)
-    i5 = lin(F1(), s8, -28.0, i4)
+    act(fd, t_f, AF.Relu, CARRY)
 
-    tt(sub(dg, 0, 65), sub(dA, 0, 65), sub(dB, 0, 65), ADD)
     for a in (17, 33):
         ts(sub(Z, a, a + 14), sub(own, 2, 16, -1), thr, LT, -0.5, ADD)
     PI = H(96)
@@ -419,23 +414,33 @@ def rank_program(g, core, T, topo):
     o6 = tt(F(16), sub(num, 65, 96, 2), away, ADD)
     ld = tt(F(3), lc, la, ADD)
     off = ts(new("aU", 16), o6, -1.0, ADD)
-    off_l = ts(new("aU", 3), ld, 0.0, MAX)
+    bF = ts(F1(), bI, -16.0, MUL)
     scatter(win, off, val)
     ci, c32 = F1(), F(32)
     run("s", [ci, c32], [sub(PI, 32, 64)], lambda e: e.activation(ap(c32), ap(sub(PI, 32, 64)), AF.Copy, accum_out=ap(ci)))
-    put(col(dg, 32), 0.0)
-    act(col(dg, 64), col(dg, 64), AF.Copy, scale=wlast)
     lin(col(GT_, 64), ci, 2.0, padc)
-    act(fd, t_f, AF.Relu, CARRY)
-    tabd = lin(F(8), t_d, 1.0, hb)
+    c0 = lin(F1(), iF, -1.0, 143.0)
+    s8 = act(F1(), iF, AF.Sign, 1.0, -7.5)
+    i4 = lin(F1(), iF, -1.0, 63.5 - 28 - 16 * max(r - 1, 0))
+    put(col(PT, 32), ROUND)
+    put(col(PT, 33), -ROUND)
+    i5 = lin(F1(), s8, -28.0, i4)
 
     G = F(64)
     act(sub(G, 0, 32), sub(ones, 0, 32), AF.Sign, th0, col(seen(r - 1), 0) if r > 0 else 0.0)
     act(sub(G, 32, 64), sub(ones, 0, 32), AF.Sign, th15, col(seen(r + 1), 16) if r < N - 1 else 0.0)
+    up = lin(F1(), col(is5, 0), float((UP if r > 0 else ZERO) + 16))
+    down = lin(F1(), col(is5, 4), float((DOWN if r < N - 1 else ZERO) - 256))
+    s16 = act(F1(), bF, AF.Sign, -1.0, -248.0)
+    lin(sub(vb, 0, 16), sub(val, 0, 256, 16), 1.0, up)
+    lin(sub(vb, 16, 32), sub(val, 15, 256, 16), 1.0, down)
+    tabd = lin(F(8), t_d, 1.0, lin(F1(), s16, 4.0 * turn, 63.5 + 4 * turn))
     fx, sb = H(144), H(176)
     n = NV * r
     if r > 0:
         scan(sub(fx, 144 - n, 144), sub(fd, 0, n), V("sg", 136 - n, 136), col(own, 16))
+    tt(sub(dg, 0, 65), sub(dA, 0, 65), sub(dB, 0, 65), ADD)
+    if r > 0:
         ts(sub(XB, 144 - n, 144), sub(fx, 144 - n, 144), thr, LT, -0.5, ADD)
     else:
         n = 1
@@ -453,34 +458,45 @@ def rank_program(g, core, T, topo):
     if m:
         scan(sub(fx, 8, 8 + m), sub(fd, 0, m), V("sg", 0, m))
     D = gather(H(128), sub(win, 0, 192), off_d)
-    scan(sub(fx, 8 + m, 8 + m + NV), sub(fd, 0, NV), own, V("sg", m - 1, m) if m else 0.0)
+    off_l = ts(new("aU", 3), ld, 0.0, MAX)
     DT = tr(H(128), D)
-    m = min(m + NV, 136 - n)
-    ts(sub(XB, 8, 8 + m), sub(fx, 8, 8 + m), thr, LT, -0.5, ADD)
+    scan(sub(fx, 8 + m, 8 + m + NV), sub(fd, 0, NV), own, V("sg", m - 1, m) if m else 0.0)
     lw = new("aU", 48)
     run("v", [lw], [DT, off_l], lambda e: e.tensor_scalar(ap(lw), ap(DT).indirect(ap(off_l)), float(MID), None, ADD))
-    X = scan(H(136), sub(ones, 0, 136), sub(XB, 8, 144, -1))
+    m = min(m + NV, 136 - n)
+    ts(sub(XB, 8, 8 + m), sub(fx, 8, 8 + m), thr, LT, -0.5, ADD)
     for a in range(1, 8):
         lin(sub(npt, 32 * a, 32 * a + 32), sub(npt, 0, 32), 1.0, 256.0 * a)
+    put(V("zt", 512, 640), 0.0)
     lbk = [lin(F1(), iF, 1.0, 16.0 + 16 * k + 16 * SL) for k in range(2)]
 
     gq, gs = V("grq", 0, PW), V("grs", 0, PW)
     slot = lambda n, i: V(n, NC * i, NC * i + NC)
-    for a, b, q in ((4, 7, "v"), (0, 4, "s")):
-        gather(V("sls", NC * a, NC * b), gs, sub(lw, 6 + 5 * a, 6 + 5 * b), q)
-    for a, b in ((4, 7), (0, 4)):
-        pickc(V("slq", NC * a, NC * b), gq, sub(lw, 6 + 5 * a, 6 + 5 * b))
-    direct = lambda part: [(T.cores[others[i]], slot("slq", i), home("laq", r), share(out, j, len(part)), "rlc") for j, i in enumerate(part)]
-    send([(c, V("sls", NC * PLANES[h][0], NC * (PLANES[h][0] + 4)), V("hds", 0, 4 * NC), share(inner, h, 2), "h1")
-          for h, c in enumerate(aides)], "lland")
-    send([(c, slot("slq", RELAYED[h]), V("hdq", 0, NC), share(inner, h, 2), "h2") for h, c in enumerate(aides)] + direct([5]), "lland")
-    send(direct([0, 1, 2, 3]), "lland")
+    for n, a, b, q in PICKS:
+        if n == "s":
+            gather(V("sls", NC * a, NC * b), gs, sub(lw, 6 + 5 * a, 6 + 5 * b), q)
+        else:
+            pickc(V("slq", NC * a, NC * b), gq, sub(lw, 6 + 5 * a, 6 + 5 * b))
+    eng = {"i": inner, "o": out}
+    for call in CALLS:
+        writes = []
+        for kind, e in call:
+            if kind == "S":
+                writes += [(c, V("sls", NC * PLANES[h][0], NC * (PLANES[h][0] + 4)), V("hds", 0, 4 * NC), share(eng[e], h, 2), "h1")
+                           for h, c in enumerate(aides)]
+            elif kind == "R":
+                writes += [(c, slot("slq", RELAYED[h]), V("hdq", 0, NC), share(eng[e], h, 2), "h2") for h, c in enumerate(aides)]
+            else:
+                writes += [(T.cores[others[i]], slot("slq", i), home("laq", r), share(out, j, len(e)), "rlc") for j, i in enumerate(e)]
+        send(writes, "lland")
     lands([home("laq", k) for k in others], "rlc", 4 * len(out))
     lands([home("las", k) for k in others], "rls", 2 * (N - 1))
 
-    act(sub(XS, 0, 8), sub(X, 15, 136, NV), AF.Copy)
-    XT = tr(H(32), XS)
+    X = scan(H(136), sub(ones, 0, 136), sub(XB, 8, 144, -1))
     pickc(V("laq", SL * r, SL * r + SL), gq, sub(lw, 0, 6))
+    act(sub(XS, 0, 8), sub(X, 15, 136, NV), AF.Copy)
+    quant("la", SL * N + 16, LW, "zt", 128)
+    XT = tr(H(32), XS)
     C = scan(F(32), sub(ones, 0, 32), XT, bF)
     quant("w", 0, 256, "wt", 0)
     ind = act(H(256), npt, AF.Sign, -0.5, col(C, 31))
@@ -496,7 +512,7 @@ def rank_program(g, core, T, topo):
     for k in range(5):
         pickc(tk("tq", k), V("laq", 32 * (k // 2), LW), lu[k % 2])
     for k in range(5):
-        gather(tk("ts", k), V("las", 32 * (k // 2), LW), lu[k % 2], "s")
+        gather(tk("ts", k), V("las", 32 * (k // 2), LW), lu[k % 2], TAIL[k])
     for k in range(5):
         for o in (0, 1):
             a = 128 * (2 * KW[k] + o)
@@ -505,6 +521,6 @@ def rank_program(g, core, T, topo):
     act(V("yo", 128, 256), V("ps", 1536, 1664), AF.Copy)
     dma("y", T.y[:, 0:128], V("yo", 0, 128), "dy0")
     dma("s", T.y[:, 128:256], V("yo", 128, 256), "dy1")
-    for sem in SEMAPHORES:
-        if count.get(sem, 0) > known["g"].get(sem, 0):
+    for sem in sorted(SEMAPHORES, key=lambda s: (s in ("dy0", "dy1"), s in csem.values())):
+        if count.get(sem, 0) > max(known[q].get(sem, 0) for q in queues):
             g.wait_ge(T.sem[sem], count[sem])

@@ -6,31 +6,32 @@ NS = 16
 NC = 5 * NS
 SL = NC + 16
 LW = SL * N + 16 + 128
-ZERO, UP, DOWN, PW = 256, 272, 288, 304
-MID = 128
+G0, ZERO, UP, DOWN, PW = 16, 256, 272, 288, 320
 KW = (1, 3, 0, 4, 2)
 NV = 17
 CARRY = 1.0 / 16
 LEVEL = 1.096
 ROUND = 1.5 * 2 ** 30
+RING = 96
+BIG = 193
 EARLY = 2560
 F8, U8, BF, F32 = "float8_e4m3fn_x4", "uint8", "bfloat16", "float32"
 SCRATCH = {"aF": ("sbuf", [128, 4096], F32), "aH": ("sbuf", [128, 8192], BF), "aI": ("sbuf", [128, 256], "int32"),
-           "aU": ("sbuf", [128, 512], "uint16"), "sg": ("sbuf", [128, 144], BF), "xt": ("sbuf", [128, 1088], BF),
-           "uc": ("sbuf", [128, 16], BF), "ut": ("sbuf", [128, 512], BF), "wt": ("sbuf", [128, 5120], BF), "zt": ("sbuf", [128, 640], BF),
+           "aU": ("sbuf", [128, 512], "uint16"), "sg": ("sbuf", [128, 144], BF), "xt": ("sbuf", [128, 1600], BF),
+           "uc": ("sbuf", [128, 16], BF), "ut": ("sbuf", [128, 512], BF), "wt": ("sbuf", [128, 5120], BF),
            "yo": ("sbuf", [128, 256], F32), "ps": ("psum", [128, 2048], F32)}
-for _n, _w in (("e", 128), ("u", 128), ("w", 1280), ("gr", PW), ("sl", NC * 7), ("la", LW), ("t", 640)):
+for _n, _w in (("u", 128), ("w", 1280), ("gr", PW), ("sl", NC * 7), ("la", LW), ("t", 640)):
     SCRATCH[_n + "q"] = ("sbuf", [128, _w], F8)
     SCRATCH[_n + "s"] = ("sbuf", [128, _w], U8)
 SCRATCH.update({"hes": ("sbuf", [128, 64], U8), "hdq": ("sbuf", [128, NC], F8), "hds": ("sbuf", [128, 4 * NC], U8)})
-RELAYED = (4, 6)
+RELAYED = (0, 1)
 PLANES = ((0, 0), (3, 4))
-PICKS = (("s", 4, 7, "v"), ("s", 0, 4, "s"), ("q", 4, 7, "v"), ("q", 0, 4, "v"))
-CALLS = ((("S", "i"),), (("R", "i"), ("D", (5,))), (("D", (0, 1, 2, 3)),))
-HORDER = (0, 1, 2)
-TAIL = "sssss"
-DMAS = ["de0", "de1", "dx0", "dx1", "du", "dw0", "dw1", "dw2", "dy0", "dy1"]
-SEMAPHORES = ["qv", "qs", "qt", "qg"] + DMAS + ["rsign", "lsign", "rhc", "rhs", "lhalo", "rlc", "rls", "lland", "h0", "h1", "h2"]
+PICKS = (("q", 0, 2, "v"), ("s", 0, 2, "s"), ("q", 2, 4, "v"), ("s", 2, 4, "s"), ("s", 4, 7, "s"), ("q", 4, 7, "v"))
+CALLS = ((("R", 0, "a", 0, 8), ("R", 1, "a", 8, 8)),
+         (("S", 0, "i", 0, 8), ("D", 2, "o", 0, 4), ("D", 3, "o", 4, 4)),
+         (("S", 1, "i", 0, 8), ("D", 4, "o", 0, 4), ("D", 5, "o", 4, 2), ("D", 6, "o", 6, 2)))
+DMAS = ["de", "dx0", "dx1", "du", "dw0", "dw1", "dw2", "dy0", "dy1"]
+SEMAPHORES = ["qv", "qs", "qt", "qg"] + DMAS + ["rsign", "lsign", "rhc", "rhs", "lhalo", "rlc", "rls", "lland", "h0", "hS", "hR"]
 A = AluOpType
 AF = ActivationFunctionType
 AX = AxisListType.X
@@ -51,9 +52,10 @@ def fused(g, T, topo, writes, lsem):
     return sum(len(w[3]) for w in writes)
 
 
-def ranks_after(r):
-    turn = 1 if r % 2 == 0 else -1
-    return [d for b in range(0, N, 2) for d in ((r + b) % N, (r + b) % N + turn)]
+def order(r, T, topo):
+    chip = [topo.chip(c) for c in T.cores]
+    plane = [d % N for d in range(r + 1, r + N + 1) if d % N == r or topo.same_plane(chip[r], chip[d % N])]
+    return [k for d in plane for k in ([m for m in range(N) if topo.mates(chip[m], chip[d])][0], d)]
 
 
 def helpers(core, T, topo):
@@ -66,11 +68,15 @@ def share(engines, k, n):
 
 
 def neighbours(r):
-    return [(k, a, b) for k, a, b in ((r + 1, 16, UP), (r - 1, 0, DOWN)) if 0 <= k < N]
+    return [(k, a, G0 + b) for k, a, b in ((r + 1, 0, UP), (r - 1, 16, DOWN)) if 0 <= k < N]
 
 
 def home(n, k):
     return (n, SL * k + 16, SL * k + SL, 1)
+
+
+def engines_of(kind, who):
+    return [w[4] for call in CALLS for w in call if w[:2] == (kind, who)][0]
 
 
 def hand_on(g, core, T, topo):
@@ -78,19 +84,19 @@ def hand_on(g, core, T, topo):
     if not mine or core not in helpers(mine[0], T, topo):
         return
     r, h = T.rank_of(mine[0]), helpers(mine[0], T, topo).index(core)
-    others = ranks_after(r)[1:]
+    others = order(r, T, topo)[:-1]
     out = topo.engines(core, T.cores[others[0]])
     near = neighbours(r)
     a, b = PLANES[h]
     n = 0
     steps = (
-            ("h0", [(T.cores[k], ("hes", c + 8 * h, c + 8 * h + 8), ("grs", d + 8 * h, d + 8 * h + 8), share(out, i, len(near)), "rhs")
-                    for i, (k, c, d) in enumerate(near)]),
-            ("h1", [(T.cores[others[i]], ("hds", NC * (i - a), NC * (i - a + 1)), home("las", r), share(out, i - a, 4), "rls")
-                    for i in range(b, a + 4)]),
-            ("h2", [(T.cores[others[RELAYED[h]]], ("hdq", 0, NC), home("laq", r), out, "rlc")]))
-    for sem, writes in [steps[k] for k in HORDER]:
-        g.wait_ge(T.sem[sem], 8 if sem == "h0" else 4)
+            ("h0", 8, [(T.cores[k], ("hes", c + 8 * h, c + 8 * h + 8), ("grs", d + 8 * h, d + 8 * h + 8), share(out, i, len(near)), "rhs")
+                       for i, (k, c, d) in enumerate(near)]),
+            ("hR", engines_of("R", h), [(T.cores[others[RELAYED[h]]], ("hdq", 0, NC), home("laq", r), out, "rlc")]),
+            ("hS", engines_of("S", h), [(T.cores[others[i]], ("hds", NC * (i - a), NC * (i - a + 1)), home("las", r), share(out, i - a, 4), "rls")
+                                        for i in range(b, a + 4)]))
+    for sem, k, writes in steps:
+        g.wait_ge(T.sem[sem], k)
         n += fused(g, T, topo, writes, "lland")
     g.wait_ge(T.sem["lland"], n)
 
@@ -104,7 +110,7 @@ def rank_program(g, core, T, topo):
     count = {}
     known = {q: {} for q in queues}
     hist = {}
-    used = {"aF": 0, "aH": 0, "aI": 0, "aU": 0}
+    used = {"aF": 8, "aH": 16, "aI": 0, "aU": 0}
     unit = {"aF": 8, "aH": 16, "aI": 8, "aU": 16}
 
     def V(name, a, b, step=1):
@@ -135,8 +141,6 @@ def rank_program(g, core, T, topo):
             for v in group:
                 for (o, write, oq, sem, val, clock) in hist.get(v[0], []):
                     if not (write or out) or o[1] >= v[2] or v[1] >= o[2]:
-                        continue
-                    if not write and oq == q and sem == csem.get(q):
                         continue
                     if v[3] == o[3] and v[3] > 1 and (v[1] - o[1]) % v[3]:
                         continue
@@ -219,15 +223,17 @@ def rank_program(g, core, T, topo):
         run("s", [o], ins, lambda e: e.activation(ap(o), ap(i), func, bias=b, scale=a))
         return o
 
+    def total(o, junk, i, func, bias=0.0):
+        ins = [i]
+        b = sc(bias, ins)
+        run("s", [o, junk], ins, lambda e: e.activation(ap(junk), ap(i), func, bias=b, accum_out=ap(o)))
+        return o
+
     def lin(o, i, scale=1.0, bias=0.0):
         return act(o, i, AF.Identity, scale, bias)
 
     def iota(o, pattern, base=0, lane=0):
         run("g", [o], [], lambda e: e.iota(ap(o), pattern, base, lane, allow_small_or_imprecise_dtypes=o[0] != "aI"))
-        return o
-
-    def asel(o, i, pattern, op, c, base):
-        run("g", [o], [i], lambda e: e.affine_select(ap(o), ap(i), pattern, op, c, base, 0))
         return o
 
     def dma(q, o, i, sem):
@@ -255,91 +261,92 @@ def rank_program(g, core, T, topo):
         for v in views:
             note(v, True, None, rsem, count[rsem], {})
 
-    spare = []
-
-    def gap(n=1):
-        for _ in range(min(n, len(spare))):
-            spare.pop(0)()
-
     F1 = lambda: new("aF", 1)
     H, F, I1 = lambda n: new("aH", n), lambda n: new("aF", n), lambda: new("aI", 1)
-    others = ranks_after(r)[1:]
-    turn = others[0] - r
+    ranks = order(r, T, topo)
+    others = ranks[:-1]
+    turn = ranks[-2] - r
     aides = helpers(core, T, topo)
     out = topo.engines(core, T.cores[others[0]])
     inner = [e for e in topo.engines(core, aides[0]) if e not in out]
+    above, below = (UP if r > 0 else ZERO) + 16, (DOWN if r < N - 1 else ZERO) - 256
+    MID = ZERO - (above + below) // 2
 
-    dma("s", V("zt", 64, 128), T.x[:, 960:1024], "de1")
     dma("y", V("uc", 0, 8), T.u[:, 0:8], "du")
-    dma("s", V("zt", 0, 64), T.x[:, 0:64], "de0")
-    ones = fill(H(160), 1.0)
+    dma("s", V("xt", 0, 64), T.x[:, 960:1024], "de")
+    rs = fill(H(192), 1.0)
+    ones = sub(rs, 32, 192)
+    dma("s", V("xt", 64, 576), T.x[:, 0:512], "dx0")
     sync("y", [], [ones])
-    dma("s", V("xt", 0, 512), T.x[:, 0:512], "dx0")
-    dma("y", V("xt", 512, 1024), T.x[:, 512:1024], "dx1")
+    dma("y", V("xt", 576, 1088), T.x[:, 512:1024], "dx1")
     dma("y", V("wt", 0, EARLY), T.w[:, 0:EARLY], "dw0")
+    fill(V("xt", 1088, 1600), 0.0)
 
     lane = iota(I1(), [[0, 1]], 0, 1)
     jj = iota(H(64), [[0, 4], [1, 16]])
-    pos = iota(F(36), [[1, 36]], -2)
-    base = H(256)
-    iota(sub(base, 0, 64), [[1, 4], [16, 16]], -MID)
+    base = iota(H(64), [[1, 4], [16, 16]], -MID)
+    gap = above - (ZERO - MID)
+    where = iota(F(4), [[10240 + gap, 2], [3072 + gap, 2]])
+    pos = iota(F(35), [[1, 35]], -2)
     w2 = iota(F(16), [[1, 16]], 200, 16)
-    t_l = iota(F(3), [[16, 3]], -1)
+    GT_, e0 = F(68), F(37)
+    t_l = iota(F(3), [[16, 3]], 0)
+    iota(sub(e0, 35, 37), [[-2, 2]], 2)
 
     def put(o, c):
         return act(o, sub(ones, 0, len(range(o[1], o[2], o[3]))), AF.Copy, scale=c)
 
-    win, cells, Z, XB, fd, rs, d96, PT, ra = H(2400), H(272), H(80), H(176), H(136), H(64), H(96), H(48), H(NV)
+    win, cells, Z, XB, fd, PT, ra = H(2500), H(272), H(80), H(176), H(136), H(48), H(NV)
     jI = ts(I1(), lane, 31, A.bitwise_and, 1, A.logical_shift_right)
     oI = ts(I1(), lane, 1, A.bitwise_and)
-    cut = ts(F1(), jI, -1.0, MUL, -0.5, ADD)
+    cut = ts(F1(), jI, -15.5, ADD)
     iI = ts(I1(), lane, 15, A.bitwise_and)
     sig = ts(F1(), oI, -2.0, MUL, 1.0, ADD)
     iF = ts(F1(), iI, 0.0, ADD)
+    quant("la", SL * N + 16, LW, "xt", 1088)
+    h8 = ts(I1(), lane, 8, A.bitwise_and)
+    g16 = ts(I1(), lane, 16, A.bitwise_and)
     ft = H(128)
-    for a in range(128, 512, 128):
-        put(V("zt", a, a + 128), 0.0)
+    put(ra, CARRY)
+    put(col(cells, 271), 0.0)
+    put(col(rs, 16), 0.0)
+    put(sub(win, RING, RING + 128), 0.0)
+    put(col(ra, 1), 1.0 if r == N - 1 else 0.0)
     side = act(H(64), jj, AF.Sign, 1.0, cut)
-    back = lin(H(16), sub(side, 0, 16), -7.96875, 8.03125)
     for t in (0, 1):
         lin(V("ut", t + 2, 512, 4), sub(ones, 0, 128), 0.0, V("uc", t + 2, t + 3))
         ts(V("ut", t, 512, 4), sub(ones, 0, 128), V("uc", t, t + 1), MUL)
-    put(V("xt", 1024, 1088), 0.0)
+    back = lin(H(16), sub(side, 0, 16), -7.96875, 8.03125)
     forth = lin(H(16), sub(side, 0, 16), 7.96875, 8.03125)
     for a in (0, 64):
         lin(sub(ft, a, a + 64), side, 7.96875, 8.03125)
-    put(ra, CARRY)
-    put(col(cells, 271), 0.0)
-    put(col(ra, 1), 1.0 if r == N - 1 else 0.0)
 
     near = neighbours(r)
-    quant("e", 0, 128, "zt", 0)
-    send([(T.cores[k], V("eq", a, a + 16), V("grq", b, b + 16), share(out, i, len(near)), "rhc") for i, (k, a, b) in enumerate(near)], "lhalo")
-    send([(aides, V("es", 0, 32), V("hes", 0, 32), inner, "h0")], "lhalo")
-    wide = sum(len(out) // len(neighbours(k)) for k, a, b in near)
-    for n, rsem, m in (("grq", "rhc", 1), ("grs", "rhs", 2)):
-        lands([V(n, UP if k < r else DOWN, 16 + (UP if k < r else DOWN)) for k, a, b in near], rsem, m * wide)
-
     sgn = H(256)
-    rz = reduce(F1(), back, MUL)
     for h in (0, 1):
-        a = 128 * h
-        quant("gr", a, a + 128 + 16 * h, "xt", 4 * a)
+        a = G0 + 128 * h
+        quant("gr", 144 * h, 144 * h + 144, "xt", 576 * h)
         if h == 0:
             quant("u", 0, 128, "ut", 0)
+            rz = reduce(F1(), back, MUL)
         mm(V("ps", 512 * h, 512 * h + 128), V("uq", 0, 128), V("us", 0, 128), V("grq", a, a + 128), V("grs", a, a + 128), True, True)
-    ts(sub(ft, 0, 128, 16), sub(ones, 0, 8), rz, MUL, CARRY / 16, MUL)
-    eq = scan(F(16), forth, sub(ones, 0, 16))
-    for h in (0, 1):
-        ts(sub(sgn, 128 * h, 128 * h + 128), V("ps", 512 * h, 512 * h + 128), sig, MUL, 0.0, GT)
-    for h in (0, 1):
-        scan(sub(cells, 128 * h, 128 * h + 128), sub(ft, 0, 128), sub(sgn, 128 * h, 128 * h + 128),
-             col(cells, 127) if h else col(eq, 15) if r == 0 else 0.0)
         if h == 0:
-            la = ts(F(3), t_l, iF, ADD, 39.0, MIN)
-    ts(sub(Z, 15, 80), sub(ones, 0, 65), sig, MUL, 0.5, MUL)
+            send([(T.cores[k], V("grq", a, a + 16), V("grq", b, b + 16), share(out, i, len(near)), "rhc") for i, (k, a, b) in enumerate(near)], "lhalo")
+            send([(aides, V("grs", 0, 32), V("hes", 0, 32), inner, "h0")], "lhalo")
+            t_f = iota(H(136), [[0, 8], [-15, NV]], 16)
+    wide = sum(len(out) // len(neighbours(k)) for k, a, b in near)
+    for n, rsem, m in (("grq", "rhc", 1), ("grs", "rhs", 2)):
+        lands([V(n, G0 + (UP if k < r else DOWN), G0 + 16 + (UP if k < r else DOWN)) for k, a, b in near], rsem, m * wide)
+    ts(sub(ft, 0, 128, 16), sub(ones, 0, 8), rz, MUL, CARRY / 16, MUL)
+    ts(sub(sgn, 0, 128), V("ps", 0, 128), sig, MUL, 0.0, GT)
+    eq = scan(F(16), forth, sub(ones, 0, 16))
+    ts(sub(sgn, 128, 256), V("ps", 512, 640), sig, MUL, 0.0, GT)
+    scan(sub(cells, 0, 128), ft, sub(sgn, 0, 128), col(eq, 15) if r == 0 else 0.0)
+    tl = ts(F1(), g16, -turn / 2.0, MUL, 63.5 + 8 * turn, ADD)
+    scan(sub(cells, 128, 256), ft, sub(sgn, 128, 256), col(cells, 127))
+    i4 = ts(F1(), h8, -7.0, MUL, 63.5 - 16 * max(r - 1, 0), ADD)
     own = scan(H(NV), ra, sub(cells, 15, 272, -16), col(cells, 255))
-    bI = ts(I1(), lane, 31, A.bitwise_and)
+    ts(sub(Z, 15, 80), sub(ones, 0, 65), sig, MUL, 0.5, MUL)
     seen = lambda k: V("sg", NV * (N - 1 - k), NV * (N - k))
     send([([T.cores[k] for k in others], own, seen(r), out, "rsign")], "lsign")
     lands([seen(k) for k in others], "rsign", (N - 1) * len(out))
@@ -347,172 +354,145 @@ def rank_program(g, core, T, topo):
     known["y"]["lsign"] = count["lsign"]
     for k, (a, b) in ((1, (EARLY, 4096)), (2, (4096, 5120))):
         dma("y", V("wt", a, b), T.w[:, a:b], "dw%d" % k)
-    t_f = iota(H(136), [[0, 8], [-15, NV]], 16)
     iota(sub(XB, 144, 176), [[0, 32]], 0)
-    t_d = F(8)
-    nb = (N - r + 1) // 2
-    iota(sub(t_d, 0, 2 * nb), [[16, nb], [0, 2]], 8 * r)
-    if nb < 4:
-        iota(sub(t_d, 2 * nb, 8), [[16, 4 - nb], [0, 2]], 8 * ((r + 2 * nb) % N))
-    npt = F(256)
-    iota(sub(npt, 0, 32), [[0, 2], [128, 2], [2, 8]], 16 * r + 1)
-    XS = iota(H(32), [[0, 32]], 1000)
-    r32 = asel(H(256), iota(H(256), [[0, 256]], 1), [[0, 8], [1, 32]], NE, 0.0, 0)
+    iota(col(GT_, 67), [[0, 1]], 256)
+    t_d, firsts = F(8), [8 * d for d in ranks[1::2]]
+    nb = [i for i in range(1, 5) if i == 4 or firsts[i] < firsts[i - 1]][0]
+    for a, b in ((0, nb), (nb, 4)):
+        if a < b:
+            iota(sub(t_d, 2 * a, 2 * b), [[firsts[min(a + 1, b - 1)] - firsts[a], b - a], [0, 2]], firsts[a])
+    t_n = iota(F(8), [[-128, 8]], -64 + 16 * max(r - 1, 0) - 8 * r)
 
-    sx = lin(F1(), iF, 1.0, -2.0)
-    put(rs, 1.0)
-    sx2 = act(F1(), sx, AF.Square)
-    d5 = act(F(8), sub(pos, 0, 8), AF.Abs, -1.0, sx)
-    put(col(rs, 16), 0.0)
-    sx3 = lin(F1(), sx2, 7.0 / 3, -4.0 / 3)
-    put(d96, 1.0)
-    no5 = act(F(8), d5, AF.Sign)
-    is5 = act(F(8), d5, AF.Relu, -1.0, 1.0)
-    delta = act(F1(), sx3, AF.Copy, scale=sx)
+    ahead = act(F1(), iF, AF.Relu, 5.0, -49.0)
+    d5 = act(F(4), where, AF.Abs, -1.0 / 1024, iF)
+    behind = act(F1(), iF, AF.Relu, -5.0, 16.0)
     thr = lin(F1(), col(eq, 15), LEVEL)
-    put(col(d96, 32), 4096.0)
-    put(col(d96, 64), 1.0 / 4096)
-    for a in (64, 128, 192):
-        lin(sub(base, a, a + 64), sub(base, 0, 64), 1.0, a / 16.0)
-    z1 = lin(F1(), col(is5, 1), float(ZERO - MID + 1), delta)
-    z3 = lin(F1(), col(is5, 3), float(ZERO - MID - 1), delta)
-    val, vb = H(256), H(32)
-    lin(sub(val, 16, 240), sub(base, 16, 240), 1.0, delta)
-    lin(sub(val, 0, 16), sub(base, 0, 16), col(no5, 1), z1)
-    lin(sub(val, 240, 256), sub(base, 240, 256), col(no5, 3), z3)
-    put(sub(win, 0, 128), float(ZERO - MID))
-    GT_, dg, dAB = F(72), F(72), F(144)
-    dA, dB = sub(dAB, 0, 72), sub(dAB, 72, 144)
-    d0 = act(F(36), pos, AF.Abs, -0.5, iF)
-    wa = lin(F1(), iF, -1.0, 15.0)
-    e0 = act(F(36), d0, AF.Relu, -2.0, 1.0)
-    wb = lin(F1(), iF, 1.0 / (256 * 271), -1.0 - 1.0 / 256)
-    wlast = lin(F1(), iF, 2.0 ** -20, 256 * 2.0 ** -20)
-    put(sub(dAB, 32, 105, 72), 0.0)
-    lin(sub(dA, 33, 65), sub(e0, 1, 33), float(2 ** 20 - 1), 1.0)
-    lin(sub(dB, 0, 32), sub(e0, 2, 34), -1.0)
-    lin(sub(dA, 0, 32), sub(e0, 0, 32), wa, 1.0)
-    lin(sub(dB, 33, 65), sub(e0, 3, 35), wb)
-    act(col(dA, 64), col(dA, 64), AF.Copy, scale=wlast)
-    below = [lin(F1(), col(eq, 15), -LEVEL * c) for c in (1.0, 1.0 / CARRY)]
-    padc = lin(F1(), iF, 4.0, 226.0)
-    th0 = lin(F1(), col(own, 16), 1.0, below[0])
-    th15 = lin(F1(), col(own, 1), 1.0 / CARRY, below[1])
+    delta = lin(F1(), behind, -1.0, ahead)
+    edge = act(F(4), d5, AF.Relu, -1024.0, float(above))
+    val, vb = H(256), H(48)
+    lin(sub(val, 0, 64), base, 1.0, delta)
+    keep = act(F(2), sub(d5, 1, 3), AF.Sign, 1.0, -gap / 1024.0)
+    lin(sub(val, 64, 128), sub(val, 0, 64), 1.0, 4.0)
+    d0 = act(F(35), pos, AF.Abs, -0.5, iF)
+    lin(sub(val, 128, 256), sub(val, 0, 128), 1.0, 8.0)
+    wa = lin(col(GT_, 65), iF, -1.0, -1.0 - BIG)
+    lin(sub(val, 0, 16), sub(val, 0, 16), col(keep, 0), col(edge, 1))
+    lin(sub(val, 240, 256), sub(val, 240, 256), col(keep, 1), col(edge, 2))
+    act(sub(e0, 0, 35), d0, AF.Relu, -2.0, 1.0)
+    th0 = lin(F1(), thr, -1.0, col(own, 16))
+    dA = lin(F(35), sub(e0, 0, 35), wa, 1.0)
+    t15 = lin(F1(), thr, -1.0, col(own, 1))
+    lin(col(GT_, 0), iF, -2.0, 2.0 * (127 - (BIG - 1) // 2 - BIG))
+    th15 = lin(F1(), t15, 1.0 / CARRY)
     act(fd, t_f, AF.Relu, CARRY)
+    lin(sub(PT, 32, 34), sub(pos, 2, 4), -2 * ROUND, ROUND)
+    for a in (0, 16):
+        lin(sub(vb, a, a + 16), sub(val, 15, 256, -16), 1.0, col(edge, 3))
+    lin(sub(vb, 32, 48), sub(val, 0, 256, 16), 1.0, col(edge, 0))
 
     for a in (17, 33):
         ts(sub(Z, a, a + 14), sub(own, 2, 16, -1), thr, LT, -0.5, ADD)
     PI = H(96)
-    lb = ts(new("aI", 3), la, 0.2, MUL, -0.4, ADD)
-    AC = scan(H(64), rs, sub(Z, 15, 79))
-    tr(sub(PI, 64, 96), sub(Z, 16, 48))
-    tr(sub(PI, 0, 64), AC)
-    idle = tt(F(16), sub(PI, 64, 96, 2), sub(PI, 65, 96, 2), NE)
-    num = scan(F(96), d96, PI)
+    i5 = ts(F1(), i4, iF, SUB)
+    AC = scan(H(64), sub(rs, 0, 64), sub(Z, 15, 79))
+    tr(sub(PI, 0, 32), sub(Z, 16, 48))
+    tr(sub(PI, 32, 96), AC)
+    idle = tt(F(16), sub(PI, 1, 32, -2), sub(PI, 0, 31, -2), NE)
+    num = scan(F(64), sub(ones, 0, 64), sub(PI, 0, 64, -1))
     away = tt(F(16), idle, w2, MUL)
-    lc = ts(F(3), lb, 11.0, MUL)
-    o6 = tt(F(16), sub(num, 65, 96, 2), away, ADD)
-    ld = tt(F(3), lc, la, ADD)
-    off = ts(new("aU", 16), o6, -1.0, ADD)
-    bF = ts(F1(), bI, -16.0, MUL)
+    ci = total(F1(), F(32), sub(PI, 64, 96), AF.Identity)
+    lin(col(GT_, 66), ci, 2.0, iF)
+    tabd = lin(F(8), t_d, 1.0, tl)
+    dg = tt(F(35), dA, sub(e0, 2, 37), SUB)
+    o6 = tt(F(16), sub(num, 33, 64, 2), away, ADD)
+    off_l = ts(new("aU", 3), t_l, iF, ADD, 3.2, MUL)
+    off = ts(new("aU", 16), o6, RING - 1.0, ADD)
+    bF = ts(F1(), iF, -16.0, MUL)
     scatter(win, off, val)
-    ci, c32 = F1(), F(32)
-    run("s", [ci, c32], [sub(PI, 32, 64)], lambda e: e.activation(ap(c32), ap(sub(PI, 32, 64)), AF.Copy, accum_out=ap(ci)))
-    lin(col(GT_, 64), ci, 2.0, padc)
-    c0 = lin(F1(), iF, -1.0, 143.0)
-    s8 = act(F1(), iF, AF.Sign, 1.0, -7.5)
-    i4 = lin(F1(), iF, -1.0, 63.5 - 28 - 16 * max(r - 1, 0))
-    put(col(PT, 32), ROUND)
-    put(col(PT, 33), -ROUND)
-    i5 = lin(F1(), s8, -28.0, i4)
+    DT = H(160)
+    put(sub(DT, 128, 160), 0.0)
+    nb = lin(F(8), t_n, 1.0, i5)
+    lbk = lin(F1(), iF, 1.0, 16.0 + 4 * SL)
 
     G = F(64)
     act(sub(G, 0, 32), sub(ones, 0, 32), AF.Sign, th0, col(seen(r - 1), 0) if r > 0 else 0.0)
     act(sub(G, 32, 64), sub(ones, 0, 32), AF.Sign, th15, col(seen(r + 1), 16) if r < N - 1 else 0.0)
-    up = lin(F1(), col(is5, 0), float((UP if r > 0 else ZERO) + 16))
-    down = lin(F1(), col(is5, 4), float((DOWN if r < N - 1 else ZERO) - 256))
-    s16 = act(F1(), bF, AF.Sign, -1.0, -248.0)
-    lin(sub(vb, 0, 16), sub(val, 0, 256, 16), 1.0, up)
-    lin(sub(vb, 16, 32), sub(val, 15, 256, 16), 1.0, down)
-    tabd = lin(F(8), t_d, 1.0, lin(F1(), s16, 4.0 * turn, 63.5 + 4 * turn))
-    fx, sb = H(144), H(176)
+    act(sub(win, RING + 128, RING + 192), sub(win, RING, RING + 64), AF.Copy)
+    fx, sb, FB = H(144), H(176), F(68)
     n = NV * r
     if r > 0:
         scan(sub(fx, 144 - n, 144), sub(fd, 0, n), V("sg", 136 - n, 136), col(own, 16))
-    tt(sub(dg, 0, 65), sub(dA, 0, 65), sub(dB, 0, 65), ADD)
+    m = NV * (N - 1 - r)
+    if m:
+        scan(sub(fx, 8, 8 + m), sub(fd, 0, m), V("sg", 0, m))
     if r > 0:
         ts(sub(XB, 144 - n, 144), sub(fx, 144 - n, 144), thr, LT, -0.5, ADD)
     else:
         n = 1
         ts(col(XB, 143), col(own, 16), thr, LT, -0.5, ADD)
-    tr(sub(GT_, 0, 64), G)
+    tr(sub(GT_, 1, 65), G)
     scan(sub(sb, 144 - n, 176), sub(ones, 0, n + 32), sub(XB, 144 - n, 176))
-    FB = scan(F(65), sub(dg, 0, 65), sub(GT_, 0, 65))
+    scan(sub(FB, 0, 35), dg, sub(GT_, 33, 68))
+    scan(sub(FB, 35, 68, -1), sub(dg, 0, 33), sub(GT_, 0, 33, -1))
     tr(sub(PT, 0, 32), sub(sb, 144, 176))
-    offb = ts(new("aU", 2), sub(FB, 31, 65, 33), 0.5, MUL, c0, ADD)
+    offb = ts(new("aU", 3), sub(FB, 33, 36), 0.5, MUL, RING + (BIG - 1) / 2, ADD)
     w5 = scan(F(34), sub(ones, 0, 34), sub(PT, 0, 34), i5)
     scatter(win, offb, vb)
     off_d = ts(new("aU", 8), tabd, col(w5, 31), SUB, col(w5, 33), ADD)
-    cp(sub(win, 128, 192), sub(win, 0, 64))
-    m = NV * (N - 1 - r)
-    if m:
-        scan(sub(fx, 8, 8 + m), sub(fd, 0, m), V("sg", 0, m))
-    D = gather(H(128), sub(win, 0, 192), off_d)
-    off_l = ts(new("aU", 3), ld, 0.0, MAX)
-    DT = tr(H(128), D)
     scan(sub(fx, 8 + m, 8 + m + NV), sub(fd, 0, NV), own, V("sg", m - 1, m) if m else 0.0)
-    lw = new("aU", 48)
-    run("v", [lw], [DT, off_l], lambda e: e.tensor_scalar(ap(lw), ap(DT).indirect(ap(off_l)), float(MID), None, ADD))
+    D = gather(H(128), sub(win, RING, RING + 192), off_d)
     m = min(m + NV, 136 - n)
     ts(sub(XB, 8, 8 + m), sub(fx, 8, 8 + m), thr, LT, -0.5, ADD)
-    for a in range(1, 8):
-        lin(sub(npt, 32 * a, 32 * a + 32), sub(npt, 0, 32), 1.0, 256.0 * a)
-    put(V("zt", 512, 640), 0.0)
-    lbk = [lin(F1(), iF, 1.0, 16.0 + 16 * k + 16 * SL) for k in range(2)]
+    tr(sub(DT, 0, 128), D)
+    X = scan(H(136), sub(ones, 0, 136), sub(XB, 8, 144, -1))
+    lw = new("aU", 48)
+    run("v", [lw], [DT, off_l], lambda e: e.tensor_scalar(ap(lw), ap(DT).indirect(ap(off_l)), float(MID + G0), None, ADD))
 
     gq, gs = V("grq", 0, PW), V("grs", 0, PW)
     slot = lambda n, i: V(n, NC * i, NC * i + NC)
     for n, a, b, q in PICKS:
         if n == "s":
-            gather(V("sls", NC * a, NC * b), gs, sub(lw, 6 + 5 * a, 6 + 5 * b), q)
+            gather(V("sls", NC * a, NC * b), gs, sub(lw, 5 * a, 5 * b), q)
         else:
-            pickc(V("slq", NC * a, NC * b), gq, sub(lw, 6 + 5 * a, 6 + 5 * b))
-    eng = {"i": inner, "o": out}
+            pickc(V("slq", NC * a, NC * b), gq, sub(lw, 5 * a, 5 * b))
+    eng = {"i": inner, "o": out, "a": out + inner}
     for call in CALLS:
         writes = []
-        for kind, e in call:
+        for kind, i, e, a, k in call:
+            e = eng[e][a:a + k]
             if kind == "S":
-                writes += [(c, V("sls", NC * PLANES[h][0], NC * (PLANES[h][0] + 4)), V("hds", 0, 4 * NC), share(eng[e], h, 2), "h1")
-                           for h, c in enumerate(aides)]
+                writes.append((aides[i], V("sls", NC * PLANES[i][0], NC * (PLANES[i][0] + 4)), V("hds", 0, 4 * NC), e, "hS"))
             elif kind == "R":
-                writes += [(c, slot("slq", RELAYED[h]), V("hdq", 0, NC), share(eng[e], h, 2), "h2") for h, c in enumerate(aides)]
+                writes.append((aides[i], slot("slq", RELAYED[i]), V("hdq", 0, NC), e, "hR"))
             else:
-                writes += [(T.cores[others[i]], slot("slq", i), home("laq", r), share(out, j, len(e)), "rlc") for j, i in enumerate(e)]
+                writes.append((T.cores[others[i]], slot("slq", i), home("laq", r), e, "rlc"))
         send(writes, "lland")
-    lands([home("laq", k) for k in others], "rlc", 4 * len(out))
+    lands([home("laq", k) for k in others], "rlc",
+          sum(len(out) if i in RELAYED else engines_of("D", i) for i in [order(k, T, topo).index(r) for k in others]))
     lands([home("las", k) for k in others], "rls", 2 * (N - 1))
 
-    X = scan(H(136), sub(ones, 0, 136), sub(XB, 8, 144, -1))
-    pickc(V("laq", SL * r, SL * r + SL), gq, sub(lw, 0, 6))
+    XS = sub(side, 0, 32)
     act(sub(XS, 0, 8), sub(X, 15, 136, NV), AF.Copy)
-    quant("la", SL * N + 16, LW, "zt", 128)
-    XT = tr(H(32), XS)
-    C = scan(F(32), sub(ones, 0, 32), XT, bF)
+    pickc(V("laq", SL * r, SL * r + SL), gq, sub(lw, 34, 40))
+    XT = tr(sub(XB, 112, 144), XS)
+    C = scan(F(64), sub(ones, 0, 64), sub(XB, 112, 176), bF)
     quant("w", 0, 256, "wt", 0)
-    ind = act(H(256), npt, AF.Sign, -0.5, col(C, 31))
-    gather(V("las", SL * r, SL * r + SL), gs, sub(lw, 0, 6), "s")
-    it = tr(H(256), ind)
+    CT = tr(F(32), sub(C, 32, 64))
     quant("w", 256, 768, "wt", 1024)
-    iq = scan(H(256), r32, it)
+    cnt, junk = F(16), F(64)
+    for c in range(8):
+        total(col(cnt, c), sub(junk, 8 * c, 8 * c + 8), sub(CT, 0, 8), AF.Sign, col(nb, c))
+    lin(sub(cnt, 8, 16), sub(cnt, 0, 8), 1.0, -32.0 / SL)
+    gather(V("las", SL * r, SL * r + SL), gs, sub(lw, 34, 40), "s")
     quant("w", 768, 1024, "wt", 3072)
-    lu = [ts(new("aU", 8), sub(iq, 31, 256, 32), -SL / 2.0, MUL, lbk[k], ADD) for k in range(2)]
+    lu = ts(new("aU", 16), cnt, -SL / 2.0, MUL, lbk, ADD)
     quant("w", 1024, 1280, "wt", 4096)
 
-    tk = lambda n, k: V(n, 128 * k, 128 * k + 128)
-    for k in range(5):
-        pickc(tk("tq", k), V("laq", 32 * (k // 2), LW), lu[k % 2])
-    for k in range(5):
-        gather(tk("ts", k), V("las", 32 * (k // 2), LW), lu[k % 2], TAIL[k])
+    tk = lambda n, k, w=1: V(n, 128 * k, 128 * (k + w))
+    for k in (0, 2, 4):
+        w = min(2, 5 - k)
+        pickc(tk("tq", k, w), V("laq", 16 * k, LW), sub(lu, 0, 8 * w))
+        gather(tk("ts", k, w), V("las", 16 * k, LW), sub(lu, 0, 8 * w), "s")
     for k in range(5):
         for o in (0, 1):
             a = 128 * (2 * KW[k] + o)

@@ -6,32 +6,34 @@ NS = 16
 NC = 5 * NS
 SL = NC + 16
 LW = SL * N + 16 + 128
-G0, ZERO, UP, DOWN, PW = 16, 256, 272, 288, 320
+G0, ZERO, UP, DOWN, PW = 0, 256, 272, 288, 304
 KW = (1, 3, 0, 4, 2)
 NV = 17
+PAD = 7
 CARRY = 1.0 / 16
 LEVEL = 1.096
 ROUND = 1.5 * 2 ** 30
 RING = 96
 BIG = 193
-EARLY = 2560
+EARLY = 2048
 F8, U8, BF, F32 = "float8_e4m3fn_x4", "uint8", "bfloat16", "float32"
 SCRATCH = {"aF": ("sbuf", [128, 4096], F32), "aH": ("sbuf", [128, 8192], BF), "aI": ("sbuf", [128, 256], "int32"),
-           "aU": ("sbuf", [128, 512], "uint16"), "sg": ("sbuf", [128, 144], BF), "xt": ("sbuf", [128, 1600], BF),
+           "aU": ("sbuf", [128, 512], "uint16"), "sg": ("sbuf", [128, 160], BF), "xt": ("sbuf", [128, 1600], BF),
            "uc": ("sbuf", [128, 16], BF), "ut": ("sbuf", [128, 512], BF), "wt": ("sbuf", [128, 5120], BF),
            "yo": ("sbuf", [128, 256], F32), "ps": ("psum", [128, 2048], F32)}
 for _n, _w in (("u", 128), ("w", 1280), ("gr", PW), ("sl", NC * 7), ("la", LW), ("t", 640)):
     SCRATCH[_n + "q"] = ("sbuf", [128, _w], F8)
     SCRATCH[_n + "s"] = ("sbuf", [128, _w], U8)
-SCRATCH.update({"hes": ("sbuf", [128, 64], U8), "hdq": ("sbuf", [128, NC], F8), "hds": ("sbuf", [128, 4 * NC], U8)})
-RELAYED = (0, 1)
-PLANES = ((0, 0), (3, 4))
-PICKS = (("q", 0, 2, "v"), ("s", 0, 2, "s"), ("q", 2, 4, "v"), ("s", 2, 4, "s"), ("s", 4, 7, "s"), ("q", 4, 7, "v"))
-CALLS = ((("R", 0, "a", 0, 8), ("R", 1, "a", 8, 8)),
-         (("S", 0, "i", 0, 8), ("D", 2, "o", 0, 4), ("D", 3, "o", 4, 4)),
-         (("S", 1, "i", 0, 8), ("D", 4, "o", 0, 4), ("D", 5, "o", 4, 2), ("D", 6, "o", 6, 2)))
-DMAS = ["de", "dx0", "dx1", "du", "dw0", "dw1", "dw2", "dy0", "dy1"]
-SEMAPHORES = ["qv", "qs", "qt", "qg"] + DMAS + ["rsign", "lsign", "rhc", "rhs", "lhalo", "rlc", "rls", "lland", "h0", "hS", "hR"]
+SCRATCH.update({"hes": ("sbuf", [128, 128], U8), "heq": ("sbuf", [128, 32], F8), "hdq": ("sbuf", [128, 7 * NC], F8), "hds": ("sbuf", [128, 7 * NC], U8)})
+PICKS = [(x, a, min(a + 2, 7), q) for a in (0, 2, 4, 6) for x, q in ("qv", "ss")]
+CALLS = ((("q", 0, 1, 0, 0, 8), ("q", 1, 2, 1, 8, 8)),
+         (("s", 0, 2, 0, 8, 4), ("s", 2, 4, 1, 12, 4)), (("q", 2, 3, None, 0, 4), ("q", 3, 4, None, 4, 4)),
+         (("s", 4, 6, 2, 8, 8),), (("q", 4, 5, None, 0, 4), ("q", 5, 6, None, 4, 4), ("q", 6, 7, 2, 8, 8)),
+         (("s", 6, 7, None, 0, 8),))
+HANDS = (((("q", 0, 0, 8),), (("s", 0, 0, 4), ("s", 1, 4, 4))), ((("q", 1, 0, 8),), (("s", 2, 0, 4), ("s", 3, 4, 4))),
+         ((("s", 4, 0, 4), ("s", 5, 4, 4)), (("q", 6, 0, 8),)))
+DMAS = ["dx0", "dx1", "du", "dw0", "dw1", "dw2", "dy0", "dy1"]
+SEMAPHORES = ["qv", "qs", "qt", "qg"] + DMAS + ["rsign", "lsign", "rhq", "rhs", "lhalo", "rlq", "rls", "lland", "h0"] + ["c%d" % _k for _k in range(len(CALLS))]
 A = AluOpType
 AF = ActivationFunctionType
 AX = AxisListType.X
@@ -43,11 +45,11 @@ def fused(g, T, topo, writes, lsem):
     xs = []
     for to, src, dst, engines, rsem in writes:
         to = to if isinstance(to, list) else [to]
-        a, b = T[src[0]][:, src[1]:src[2]], T[dst[0]][:, dst[1]:dst[2]]
+        sides = [T[v[0]][:, v[1]:v[2]] for v in [src] + (dst if isinstance(dst, list) else [dst] * len(to))]
         if SCRATCH[src[0]][2] == F8:
-            a, b = a.bitcast(dt.uint8), b.bitcast(dt.uint8)
+            sides = [v.bitcast(dt.uint8) for v in sides]
         xs.append(RemoteDMATransfer(dst_ids=[DstId(rid=topo.addr(c)[0], pnc=topo.addr(c)[1]) for c in to],
-                                    dma_engine_mask=sum(1 << e for e in engines), remote_sem=T.sem[rsem], srcs=[a], dsts=[b] * len(to)))
+                                    dma_engine_mask=sum(1 << e for e in engines), remote_sem=T.sem[rsem], srcs=sides[:1], dsts=sides[1:]))
     g.remote_dma_fused(xs, local_sem=T.sem[lsem])
     return sum(len(w[3]) for w in writes)
 
@@ -59,7 +61,8 @@ def order(r, T, topo):
 
 
 def helpers(core, T, topo):
-    return [c for c in topo.cores_of(core) if topo.die(c) != topo.die(core) and all(topo.may_write(c, d) for d in T.cores)]
+    free = [c for c in topo.cores_of(core) if c != core and all(topo.may_write(c, d) for d in T.cores)]
+    return sorted(free, key=lambda c: topo.die(c) == topo.die(core))
 
 
 def share(engines, k, n):
@@ -75,8 +78,14 @@ def home(n, k):
     return (n, SL * k + 16, SL * k + SL, 1)
 
 
-def engines_of(kind, who):
-    return [w[4] for call in CALLS for w in call if w[:2] == (kind, who)][0]
+def seen(k, r):
+    a = -(-NV * (N - 1 - r) // 8) * 8 + NV * (r - k) + (PAD if k < r else 0)
+    return ("sg", a, a + NV, 1)
+
+
+def last_engines(n, i):
+    return sum([w[5] for call in CALLS for w in call if w[:2] == (n, i) and w[3] is None] +
+               [w[3] for hand in HANDS for call in hand for w in call if w[:2] == (n, i)])
 
 
 def hand_on(g, core, T, topo):
@@ -87,17 +96,16 @@ def hand_on(g, core, T, topo):
     others = order(r, T, topo)[:-1]
     out = topo.engines(core, T.cores[others[0]])
     near = neighbours(r)
-    a, b = PLANES[h]
-    n = 0
-    steps = (
-            ("h0", 8, [(T.cores[k], ("hes", c + 8 * h, c + 8 * h + 8), ("grs", d + 8 * h, d + 8 * h + 8), share(out, i, len(near)), "rhs")
-                       for i, (k, c, d) in enumerate(near)]),
-            ("hR", engines_of("R", h), [(T.cores[others[RELAYED[h]]], ("hdq", 0, NC), home("laq", r), out, "rlc")]),
-            ("hS", engines_of("S", h), [(T.cores[others[i]], ("hds", NC * (i - a), NC * (i - a + 1)), home("las", r), share(out, i - a, 4), "rls")
-                                        for i in range(b, a + 4)]))
-    for sem, k, writes in steps:
-        g.wait_ge(T.sem[sem], k)
-        n += fused(g, T, topo, writes, "lland")
+    g.wait_ge(T.sem["h0"], 8)
+    x, a, w = ("s", 8 * h, 8) if h < 2 else ("q", 0, 16)
+    n = fused(g, T, topo, [(T.cores[k], ("he" + x, c + a, c + a + w), ("gr" + x, d + a, d + a + w), share(out, i, len(near)), "rh" + x)
+                           for i, (k, c, d) in enumerate(near)], "lland")
+    for hand in HANDS[h]:
+        for k, call in enumerate(CALLS):
+            if any(w[3] == h and w[0] == x[0] and w[1] <= x[1] < w[2] for w in call for x in hand):
+                g.wait_ge(T.sem["c%d" % k], sum(w[5] for w in call if w[3] == h))
+        n += fused(g, T, topo, [(T.cores[others[i]], ("hd" + x, NC * i, NC * i + NC), home("la" + x, r), out[a:a + e], "rl" + x)
+                                for x, i, a, e in hand], "lland")
     g.wait_ge(T.sem["lland"], n)
 
 
@@ -273,88 +281,89 @@ def rank_program(g, core, T, topo):
     MID = ZERO - (above + below) // 2
 
     dma("y", V("uc", 0, 8), T.u[:, 0:8], "du")
-    dma("s", V("xt", 0, 64), T.x[:, 960:1024], "de")
+    dma("y", V("xt", 0, 512), T.x[:, 0:512], "dx0")
+    dma("y", V("xt", 512, 1024), T.x[:, 512:1024], "dx1")
     rs = fill(H(192), 1.0)
     ones = sub(rs, 32, 192)
-    dma("s", V("xt", 64, 576), T.x[:, 0:512], "dx0")
-    sync("y", [], [ones])
-    dma("y", V("xt", 576, 1088), T.x[:, 512:1024], "dx1")
+    sync("y", [], [V("xt", 0, 512)])
     dma("y", V("wt", 0, EARLY), T.w[:, 0:EARLY], "dw0")
-    fill(V("xt", 1088, 1600), 0.0)
 
     lane = iota(I1(), [[0, 1]], 0, 1)
     jj = iota(H(64), [[0, 4], [1, 16]])
     base = iota(H(64), [[1, 4], [16, 16]], -MID)
     gap = above - (ZERO - MID)
     where = iota(F(4), [[10240 + gap, 2], [3072 + gap, 2]])
+    GT_, e0 = F(68), F(37)
     pos = iota(F(35), [[1, 35]], -2)
     w2 = iota(F(16), [[1, 16]], 200, 16)
-    GT_, e0 = F(68), F(37)
     t_l = iota(F(3), [[16, 3]], 0)
-    iota(sub(e0, 35, 37), [[-2, 2]], 2)
 
     def put(o, c):
         return act(o, sub(ones, 0, len(range(o[1], o[2], o[3]))), AF.Copy, scale=c)
 
-    win, cells, Z, XB, fd, PT, ra = H(2500), H(272), H(80), H(176), H(136), H(48), H(NV)
+    win, cells, Z, XB, fd, PT, ra = H(2500), H(272), H(80), H(176), H(144), H(48), H(NV)
     jI = ts(I1(), lane, 31, A.bitwise_and, 1, A.logical_shift_right)
     oI = ts(I1(), lane, 1, A.bitwise_and)
-    cut = ts(F1(), jI, -15.5, ADD)
     iI = ts(I1(), lane, 15, A.bitwise_and)
-    sig = ts(F1(), oI, -2.0, MUL, 1.0, ADD)
-    iF = ts(F1(), iI, 0.0, ADD)
-    quant("la", SL * N + 16, LW, "xt", 1088)
-    h8 = ts(I1(), lane, 8, A.bitwise_and)
-    g16 = ts(I1(), lane, 16, A.bitwise_and)
-    ft = H(128)
+    cut = ts(F1(), jI, -15.5, ADD)
+    ft = H(256)
+    put(V("xt", 1024, 1088), 0.0)
     put(ra, CARRY)
     put(col(cells, 271), 0.0)
     put(col(rs, 16), 0.0)
-    put(sub(win, RING, RING + 128), 0.0)
-    put(col(ra, 1), 1.0 if r == N - 1 else 0.0)
-    side = act(H(64), jj, AF.Sign, 1.0, cut)
     for t in (0, 1):
         lin(V("ut", t + 2, 512, 4), sub(ones, 0, 128), 0.0, V("uc", t + 2, t + 3))
         ts(V("ut", t, 512, 4), sub(ones, 0, 128), V("uc", t, t + 1), MUL)
+    sig = ts(F1(), oI, -2.0, MUL, 1.0, ADD)
+    side = act(H(64), jj, AF.Sign, 1.0, cut)
+    put(col(ra, 1), 1.0 if r == N - 1 else 0.0)
+    small = put(H(16), CARRY / 16)
     back = lin(H(16), sub(side, 0, 16), -7.96875, 8.03125)
     forth = lin(H(16), sub(side, 0, 16), 7.96875, 8.03125)
-    for a in (0, 64):
+    for a in range(0, 256, 64):
         lin(sub(ft, a, a + 64), side, 7.96875, 8.03125)
+    put(sub(win, RING, RING + 128), 0.0)
 
     near = neighbours(r)
     sgn = H(256)
     for h in (0, 1):
         a = G0 + 128 * h
-        quant("gr", 144 * h, 144 * h + 144, "xt", 576 * h)
+        quant("gr", a, a + 128 + 16 * h, "xt", 4 * a)
         if h == 0:
             quant("u", 0, 128, "ut", 0)
-            rz = reduce(F1(), back, MUL)
+        else:
+            for to, x, e in ((aides[2], "q", out), (aides[:2], "s", inner)):
+                send([(to, V("gr" + x, c, c + 16), V("he" + x, 16 * i, 16 * i + 16), share(e, i, 2), "h0") for i, c in enumerate((240, 0))], "lhalo")
         mm(V("ps", 512 * h, 512 * h + 128), V("uq", 0, 128), V("us", 0, 128), V("grq", a, a + 128), V("grs", a, a + 128), True, True)
-        if h == 0:
-            send([(T.cores[k], V("grq", a, a + 16), V("grq", b, b + 16), share(out, i, len(near)), "rhc") for i, (k, a, b) in enumerate(near)], "lhalo")
-            send([(aides, V("grs", 0, 32), V("hes", 0, 32), inner, "h0")], "lhalo")
-            t_f = iota(H(136), [[0, 8], [-15, NV]], 16)
     wide = sum(len(out) // len(neighbours(k)) for k, a, b in near)
-    for n, rsem, m in (("grq", "rhc", 1), ("grs", "rhs", 2)):
+    for n, rsem, m in (("grq", "rhq", 1), ("grs", "rhs", 2)):
         lands([V(n, G0 + (UP if k < r else DOWN), G0 + 16 + (UP if k < r else DOWN)) for k, a, b in near], rsem, m * wide)
-    ts(sub(ft, 0, 128, 16), sub(ones, 0, 8), rz, MUL, CARRY / 16, MUL)
+    rz = reduce(F1(), back, MUL)
+    eq, iF = F(16), F1()
+    late = [lambda: scan(eq, forth, sub(ones, 0, 16)), lambda: ts(iF, iI, 0.0, ADD)]
+    late[r > 0]()
     ts(sub(sgn, 0, 128), V("ps", 0, 128), sig, MUL, 0.0, GT)
-    eq = scan(F(16), forth, sub(ones, 0, 16))
+    act(sub(ft, 0, 256, 16), small, AF.Copy, rz)
     ts(sub(sgn, 128, 256), V("ps", 512, 640), sig, MUL, 0.0, GT)
-    scan(sub(cells, 0, 128), ft, sub(sgn, 0, 128), col(eq, 15) if r == 0 else 0.0)
-    tl = ts(F1(), g16, -turn / 2.0, MUL, 63.5 + 8 * turn, ADD)
-    scan(sub(cells, 128, 256), ft, sub(sgn, 128, 256), col(cells, 127))
-    i4 = ts(F1(), h8, -7.0, MUL, 63.5 - 16 * max(r - 1, 0), ADD)
-    own = scan(H(NV), ra, sub(cells, 15, 272, -16), col(cells, 255))
-    ts(sub(Z, 15, 80), sub(ones, 0, 65), sig, MUL, 0.5, MUL)
-    seen = lambda k: V("sg", NV * (N - 1 - k), NV * (N - k))
-    send([([T.cores[k] for k in others], own, seen(r), out, "rsign")], "lsign")
-    lands([seen(k) for k in others], "rsign", (N - 1) * len(out))
+    late[r == 0]()
+    scan(sub(cells, 0, 256), ft, sgn, col(eq, 15) if r == 0 else 0.0)
+    h8 = ts(I1(), lane, 8, A.bitwise_and)
+    own = scan(seen(r, r), ra, sub(cells, 15, 272, -16), col(cells, 255))
+    g16 = ts(I1(), lane, 16, A.bitwise_and)
+    send([([T.cores[k] for k in others], own, [seen(r, k) for k in others], out, "rsign")], "lsign")
+    lands([seen(k, r) for k in others], "rsign", (N - 1) * len(out))
+    every = V("sg", seen(N - 1, r)[1], seen(0, r)[2])
+    mine, n = NV * (N - r), every[2] - every[1]
     g.sync.wait_ge(T.sem["lsign"], count["lsign"])
     known["y"]["lsign"] = count["lsign"]
     for k, (a, b) in ((1, (EARLY, 4096)), (2, (4096, 5120))):
         dma("y", V("wt", a, b), T.w[:, a:b], "dw%d" % k)
-    iota(sub(XB, 144, 176), [[0, 32]], 0)
+    t_f = iota(H(136), [[0, 8], [-15, NV]], 16)
+    iota(sub(e0, 35, 37), [[-2, 2]], 2)
+    if r > 0:
+        iota(sub(fd, mine, mine + PAD), [[0, PAD]], 1)
+        iota(sub(every, mine, mine + PAD), [[0, PAD]], 0)
+    iota(sub(XB, n, n + 32), [[0, 32]], 0)
     iota(col(GT_, 67), [[0, 1]], 256)
     t_d, firsts = F(8), [8 * d for d in ranks[1::2]]
     nb = [i for i in range(1, 5) if i == 4 or firsts[i] < firsts[i - 1]][0]
@@ -362,38 +371,39 @@ def rank_program(g, core, T, topo):
         if a < b:
             iota(sub(t_d, 2 * a, 2 * b), [[firsts[min(a + 1, b - 1)] - firsts[a], b - a], [0, 2]], firsts[a])
     t_n = iota(F(8), [[-128, 8]], -64 + 16 * max(r - 1, 0) - 8 * r)
+    iota(V("xt", 1088, 1536), [[0, 448]], 0)
 
+    act(sub(Z, 15, 80), sub(ones, 0, 65), AF.Copy, sig)
     ahead = act(F1(), iF, AF.Relu, 5.0, -49.0)
-    d5 = act(F(4), where, AF.Abs, -1.0 / 1024, iF)
     behind = act(F1(), iF, AF.Relu, -5.0, 16.0)
+    d5 = act(F(4), where, AF.Abs, -1.0 / 1024, iF)
     thr = lin(F1(), col(eq, 15), LEVEL)
     delta = lin(F1(), behind, -1.0, ahead)
     edge = act(F(4), d5, AF.Relu, -1024.0, float(above))
+    keep = act(F(2), sub(d5, 1, 3), AF.Sign, 1.0, -gap / 1024.0)
+    d0 = act(F(35), pos, AF.Abs, -0.5, iF)
     val, vb = H(256), H(48)
     lin(sub(val, 0, 64), base, 1.0, delta)
-    keep = act(F(2), sub(d5, 1, 3), AF.Sign, 1.0, -gap / 1024.0)
-    lin(sub(val, 64, 128), sub(val, 0, 64), 1.0, 4.0)
-    d0 = act(F(35), pos, AF.Abs, -0.5, iF)
-    lin(sub(val, 128, 256), sub(val, 0, 128), 1.0, 8.0)
     wa = lin(col(GT_, 65), iF, -1.0, -1.0 - BIG)
-    lin(sub(val, 0, 16), sub(val, 0, 16), col(keep, 0), col(edge, 1))
-    lin(sub(val, 240, 256), sub(val, 240, 256), col(keep, 1), col(edge, 2))
     act(sub(e0, 0, 35), d0, AF.Relu, -2.0, 1.0)
-    th0 = lin(F1(), thr, -1.0, col(own, 16))
+    for a in (192, 64, 128):
+        lin(sub(val, a, a + 64), sub(val, 0, 64), 1.0, a / 16.0)
     dA = lin(F(35), sub(e0, 0, 35), wa, 1.0)
+    lin(sub(val, 240, 256), sub(val, 240, 256), col(keep, 1), col(edge, 2))
+    th0 = lin(F1(), thr, -1.0, col(own, 16))
+    lin(sub(val, 0, 16), sub(val, 0, 16), col(keep, 0), col(edge, 1))
     t15 = lin(F1(), thr, -1.0, col(own, 1))
-    lin(col(GT_, 0), iF, -2.0, 2.0 * (127 - (BIG - 1) // 2 - BIG))
+    act(sub(fd, 0, mine), sub(t_f, 0, mine), AF.Relu, CARRY)
+    if r > 0:
+        act(sub(fd, mine + PAD, n), sub(t_f, 0, NV * r), AF.Relu, CARRY)
     th15 = lin(F1(), t15, 1.0 / CARRY)
-    act(fd, t_f, AF.Relu, CARRY)
+    lin(col(GT_, 0), iF, -2.0, 2.0 * (127 - (BIG - 1) // 2 - BIG))
     lin(sub(PT, 32, 34), sub(pos, 2, 4), -2 * ROUND, ROUND)
-    for a in (0, 16):
-        lin(sub(vb, a, a + 16), sub(val, 15, 256, -16), 1.0, col(edge, 3))
-    lin(sub(vb, 32, 48), sub(val, 0, 256, 16), 1.0, col(edge, 0))
 
     for a in (17, 33):
         ts(sub(Z, a, a + 14), sub(own, 2, 16, -1), thr, LT, -0.5, ADD)
     PI = H(96)
-    i5 = ts(F1(), i4, iF, SUB)
+    i4 = ts(F1(), h8, -7.0, MUL, 63.5 - 16 * max(r - 1, 0), ADD)
     AC = scan(H(64), sub(rs, 0, 64), sub(Z, 15, 79))
     tr(sub(PI, 0, 32), sub(Z, 16, 48))
     tr(sub(PI, 32, 96), AC)
@@ -402,97 +412,88 @@ def rank_program(g, core, T, topo):
     away = tt(F(16), idle, w2, MUL)
     ci = total(F1(), F(32), sub(PI, 64, 96), AF.Identity)
     lin(col(GT_, 66), ci, 2.0, iF)
-    tabd = lin(F(8), t_d, 1.0, tl)
-    dg = tt(F(35), dA, sub(e0, 2, 37), SUB)
+    tl = ts(F1(), g16, -turn / 2.0, MUL, 63.5 + 8 * turn, ADD)
     o6 = tt(F(16), sub(num, 33, 64, 2), away, ADD)
     off_l = ts(new("aU", 3), t_l, iF, ADD, 3.2, MUL)
     off = ts(new("aU", 16), o6, RING - 1.0, ADD)
-    bF = ts(F1(), iF, -16.0, MUL)
+    dg = tt(F(35), dA, sub(e0, 2, 37), SUB)
+    off_a = ts(new("aU", 1), iF, 3.2, MUL, 31.0, MIN)
     scatter(win, off, val)
-    DT = H(160)
-    put(sub(DT, 128, 160), 0.0)
-    nb = lin(F(8), t_n, 1.0, i5)
-    lbk = lin(F1(), iF, 1.0, 16.0 + 4 * SL)
 
     G = F(64)
-    act(sub(G, 0, 32), sub(ones, 0, 32), AF.Sign, th0, col(seen(r - 1), 0) if r > 0 else 0.0)
-    act(sub(G, 32, 64), sub(ones, 0, 32), AF.Sign, th15, col(seen(r + 1), 16) if r < N - 1 else 0.0)
+    act(sub(G, 0, 32), sub(ones, 0, 32), AF.Sign, th0, col(seen(r - 1, r), 0) if r > 0 else 0.0)
+    act(sub(G, 32, 64), sub(ones, 0, 32), AF.Sign, th15, col(seen(r + 1, r), 16) if r < N - 1 else 0.0)
+    for a in (0, 16):
+        lin(sub(vb, a, a + 16), sub(val, 15, 256, -16), 1.0, col(edge, 3))
+    lin(sub(vb, 32, 48), sub(val, 0, 256, 16), 1.0, col(edge, 0))
     act(sub(win, RING + 128, RING + 192), sub(win, RING, RING + 64), AF.Copy)
-    fx, sb, FB = H(144), H(176), F(68)
-    n = NV * r
-    if r > 0:
-        scan(sub(fx, 144 - n, 144), sub(fd, 0, n), V("sg", 136 - n, 136), col(own, 16))
-    m = NV * (N - 1 - r)
-    if m:
-        scan(sub(fx, 8, 8 + m), sub(fd, 0, m), V("sg", 0, m))
-    if r > 0:
-        ts(sub(XB, 144 - n, 144), sub(fx, 144 - n, 144), thr, LT, -0.5, ADD)
-    else:
-        n = 1
-        ts(col(XB, 143), col(own, 16), thr, LT, -0.5, ADD)
+    i5 = lin(F1(), iF, -1.0, i4)
+    tabd = lin(F(8), t_d, 1.0, tl)
+    bF = lin(F1(), iF, -16.0)
+    DT = H(160)
+    put(sub(DT, 128, 160), 0.0)
+    FB, m = F(68), max(NV * r, 1)
+    fx = scan(H(n), sub(fd, 0, n), every)
+    quant("w", 0, 128, "wt", 0)
+    ts(sub(XB, 0, n), fx, thr, LT, -0.5, ADD)
     tr(sub(GT_, 1, 65), G)
-    scan(sub(sb, 144 - n, 176), sub(ones, 0, n + 32), sub(XB, 144 - n, 176))
+    sb = scan(H(m + 32), sub(ones, 0, m + 32), sub(XB, n - m, n + 32))
     scan(sub(FB, 0, 35), dg, sub(GT_, 33, 68))
     scan(sub(FB, 35, 68, -1), sub(dg, 0, 33), sub(GT_, 0, 33, -1))
-    tr(sub(PT, 0, 32), sub(sb, 144, 176))
+    tr(sub(PT, 0, 32), sub(sb, m, m + 32))
     offb = ts(new("aU", 3), sub(FB, 33, 36), 0.5, MUL, RING + (BIG - 1) / 2, ADD)
     w5 = scan(F(34), sub(ones, 0, 34), sub(PT, 0, 34), i5)
     scatter(win, offb, vb)
     off_d = ts(new("aU", 8), tabd, col(w5, 31), SUB, col(w5, 33), ADD)
-    scan(sub(fx, 8 + m, 8 + m + NV), sub(fd, 0, NV), own, V("sg", m - 1, m) if m else 0.0)
-    D = gather(H(128), sub(win, RING, RING + 192), off_d)
-    m = min(m + NV, 136 - n)
-    ts(sub(XB, 8, 8 + m), sub(fx, 8, 8 + m), thr, LT, -0.5, ADD)
-    tr(sub(DT, 0, 128), D)
-    X = scan(H(136), sub(ones, 0, 136), sub(XB, 8, 144, -1))
-    lw = new("aU", 48)
-    run("v", [lw], [DT, off_l], lambda e: e.tensor_scalar(ap(lw), ap(DT).indirect(ap(off_l)), float(MID + G0), None, ADD))
+    nb = lin(F(8), t_n, 1.0, i5)
+    lbk = lin(F1(), iF, 1.0, 16.0 + 4 * SL)
+    D = H(128)
+    for a, b, q in ((0, 2, "v"), (2, 8, "s")):
+        gather(sub(D, 16 * a, 16 * b), sub(win, RING, RING + 192), sub(off_d, a, b), q)
+    X = scan(H(n), sub(ones, 0, n), sub(XB, 0, n, -1))
+    XS = sub(side, 0, 32)
+    if r > 0:
+        act(sub(XS, 0, r), sub(X, 15, NV * r, NV), AF.Copy)
+    lin(sub(XS, r, N), sub(X, n - mine + 15, n, NV), 1.0, -PAD / 2.0 if r > 0 else 0.0)
+    tr(sub(DT, 0, 32), sub(D, 0, 32))
+    tr(sub(DT, 32, 128), sub(D, 32, 128))
+    first, lw = new("aU", 16), new("aU", 48)
+    for o, w, l in ((first, sub(DT, 0, 32), off_a), (lw, DT, off_l)):
+        run("v", [o], [w, l], lambda e: e.tensor_scalar(ap(o), ap(w).indirect(ap(l)), float(MID + G0), None, ADD))
 
     gq, gs = V("grq", 0, PW), V("grs", 0, PW)
-    slot = lambda n, i: V(n, NC * i, NC * i + NC)
-    for n, a, b, q in PICKS:
-        if n == "s":
-            gather(V("sls", NC * a, NC * b), gs, sub(lw, 5 * a, 5 * b), q)
+    for x, a, b, q in PICKS:
+        l = sub(lw if a else first, 5 * a, 5 * b)
+        if x == "s":
+            gather(V("sls", NC * a, NC * b), gs, l, q)
         else:
-            pickc(V("slq", NC * a, NC * b), gq, sub(lw, 5 * a, 5 * b))
-    eng = {"i": inner, "o": out, "a": out + inner}
-    for call in CALLS:
-        writes = []
-        for kind, i, e, a, k in call:
-            e = eng[e][a:a + k]
-            if kind == "S":
-                writes.append((aides[i], V("sls", NC * PLANES[i][0], NC * (PLANES[i][0] + 4)), V("hds", 0, 4 * NC), e, "hS"))
-            elif kind == "R":
-                writes.append((aides[i], slot("slq", RELAYED[i]), V("hdq", 0, NC), e, "hR"))
-            else:
-                writes.append((T.cores[others[i]], slot("slq", i), home("laq", r), e, "rlc"))
-        send(writes, "lland")
-    lands([home("laq", k) for k in others], "rlc",
-          sum(len(out) if i in RELAYED else engines_of("D", i) for i in [order(k, T, topo).index(r) for k in others]))
-    lands([home("las", k) for k in others], "rls", 2 * (N - 1))
+            pickc(V("slq", NC * a, NC * b), gq, l)
+    for k, call in enumerate(CALLS):
+        send([(T.cores[others[a]], V("sl" + x, NC * a, NC * b), home("la" + x, r), (out + inner)[e:e + w], "rl" + x) if h is None else
+              (aides[h], V("sl" + x, NC * a, NC * b), V("hd" + x, NC * a, NC * b), (out + inner)[e:e + w], "c%d" % k)
+              for x, a, b, h, e, w in call], "lland")
+    for x in "qs":
+        lands([home("la" + x, k) for k in others], "rl" + x, sum(last_engines(x, order(k, T, topo).index(r)) for k in others))
 
-    XS = sub(side, 0, 32)
-    act(sub(XS, 0, 8), sub(X, 15, 136, NV), AF.Copy)
+    tr(sub(XB, n - 32, n), XS)
     pickc(V("laq", SL * r, SL * r + SL), gq, sub(lw, 34, 40))
-    XT = tr(sub(XB, 112, 144), XS)
-    C = scan(F(64), sub(ones, 0, 64), sub(XB, 112, 176), bF)
-    quant("w", 0, 256, "wt", 0)
+    C = scan(F(64), sub(ones, 0, 64), sub(XB, n - 32, n + 32), bF)
+    quant("la", SL * N + 16, LW, "xt", 1024)
     CT = tr(F(32), sub(C, 32, 64))
-    quant("w", 256, 768, "wt", 1024)
+    quant("w", 128, 640, "wt", 512)
+    quant("w", 640, 1024, "wt", 2560)
     cnt, junk = F(16), F(64)
     for c in range(8):
         total(col(cnt, c), sub(junk, 8 * c, 8 * c + 8), sub(CT, 0, 8), AF.Sign, col(nb, c))
     lin(sub(cnt, 8, 16), sub(cnt, 0, 8), 1.0, -32.0 / SL)
     gather(V("las", SL * r, SL * r + SL), gs, sub(lw, 34, 40), "s")
-    quant("w", 768, 1024, "wt", 3072)
-    lu = ts(new("aU", 16), cnt, -SL / 2.0, MUL, lbk, ADD)
     quant("w", 1024, 1280, "wt", 4096)
+    lu = ts(new("aU", 16), cnt, -SL / 2.0, MUL, lbk, ADD)
 
     tk = lambda n, k, w=1: V(n, 128 * k, 128 * (k + w))
-    for k in (0, 2, 4):
-        w = min(2, 5 - k)
+    for k, w, q in ((0, 2, "s"), (2, 2, "s"), (4, 1, "s")):
         pickc(tk("tq", k, w), V("laq", 16 * k, LW), sub(lu, 0, 8 * w))
-        gather(tk("ts", k, w), V("las", 16 * k, LW), sub(lu, 0, 8 * w), "s")
+        gather(tk("ts", k, w), V("las", 16 * k, LW), sub(lu, 0, 8 * w), q)
     for k in range(5):
         for o in (0, 1):
             a = 128 * (2 * KW[k] + o)

from concourse.bass import DstId, RemoteDMATransfer
from concourse.mybir import dt, AluOpType, ActivationFunctionType, AxisListType

N = 8
NS = 16
NC = 5 * NS
SL = NC + 16
LW = SL * N + 16 + 128
G0, ZERO, UP, DOWN, PW = 0, 256, 272, 288, 304
KW = (1, 3, 0, 4, 2)
NV = 17
PAD = 7
CARRY = 1.0 / 16
LEVEL = 1.096
ROUND = 1.5 * 2 ** 30
RING = 96
BIG = 193
EARLY = 2048
F8, U8, BF, F32 = "float8_e4m3fn_x4", "uint8", "bfloat16", "float32"
SCRATCH = {"aF": ("sbuf", [128, 4096], F32), "aH": ("sbuf", [128, 8192], BF), "aI": ("sbuf", [128, 256], "int32"),
           "aU": ("sbuf", [128, 512], "uint16"), "sg": ("sbuf", [128, 160], BF), "xt": ("sbuf", [128, 1600], BF),
           "uc": ("sbuf", [128, 16], BF), "ut": ("sbuf", [128, 512], BF), "wt": ("sbuf", [128, 5120], BF),
           "yo": ("sbuf", [128, 256], F32), "ps": ("psum", [128, 2048], F32)}
for _n, _w in (("u", 128), ("w", 1280), ("gr", PW), ("sl", NC * 7), ("la", LW), ("t", 640)):
    SCRATCH[_n + "q"] = ("sbuf", [128, _w], F8)
    SCRATCH[_n + "s"] = ("sbuf", [128, _w], U8)
SCRATCH.update({"hes": ("sbuf", [128, 128], U8), "heq": ("sbuf", [128, 32], F8), "hdq": ("sbuf", [128, 7 * NC], F8), "hds": ("sbuf", [128, 7 * NC], U8)})
PICKS = [(x, a, min(a + 2, 7), q) for a in (0, 2, 4, 6) for x, q in ("qv", "ss")]
CALLS = ((("q", 0, 1, 0, 0, 8), ("q", 1, 2, 1, 8, 8)),
         (("s", 0, 2, 0, 8, 4), ("s", 2, 4, 1, 12, 4)), (("q", 2, 3, None, 0, 4), ("q", 3, 4, None, 4, 4)),
         (("s", 4, 6, 2, 8, 8),), (("q", 4, 5, None, 0, 4), ("q", 5, 6, None, 4, 4), ("q", 6, 7, 2, 8, 8)),
         (("s", 6, 7, None, 0, 8),))
HANDS = (((("q", 0, 0, 8),), (("s", 0, 0, 4), ("s", 1, 4, 4))), ((("q", 1, 0, 8),), (("s", 2, 0, 4), ("s", 3, 4, 4))),
         ((("s", 4, 0, 4), ("s", 5, 4, 4)), (("q", 6, 0, 8),)))
DMAS = ["dx0", "dx1", "du", "dw0", "dw1", "dw2", "dy0", "dy1"]
SEMAPHORES = ["qv", "qs", "qt", "qg"] + DMAS + ["rsign", "lsign", "rhq", "rhs", "lhalo", "rlq", "rls", "lland", "h0"] + ["c%d" % _k for _k in range(len(CALLS))]
A = AluOpType
AF = ActivationFunctionType
AX = AxisListType.X
MUL, ADD, SUB, MAX, MIN = A.mult, A.add, A.subtract, A.max, A.min
EQ, NE, LT, GE, GT = A.is_equal, A.not_equal, A.is_lt, A.is_ge, A.is_gt


def fused(g, T, topo, writes, lsem):
    xs = []
    for to, src, dst, engines, rsem in writes:
        to = to if isinstance(to, list) else [to]
        sides = [T[v[0]][:, v[1]:v[2]] for v in [src] + (dst if isinstance(dst, list) else [dst] * len(to))]
        if SCRATCH[src[0]][2] == F8:
            sides = [v.bitcast(dt.uint8) for v in sides]
        xs.append(RemoteDMATransfer(dst_ids=[DstId(rid=topo.addr(c)[0], pnc=topo.addr(c)[1]) for c in to],
                                    dma_engine_mask=sum(1 << e for e in engines), remote_sem=T.sem[rsem], srcs=sides[:1], dsts=sides[1:]))
    g.remote_dma_fused(xs, local_sem=T.sem[lsem])
    return sum(len(w[3]) for w in writes)


def order(r, T, topo):
    chip = [topo.chip(c) for c in T.cores]
    plane = [d % N for d in range(r + 1, r + N + 1) if d % N == r or topo.same_plane(chip[r], chip[d % N])]
    return [k for d in plane for k in ([m for m in range(N) if topo.mates(chip[m], chip[d])][0], d)]


def helpers(core, T, topo):
    free = [c for c in topo.cores_of(core) if c != core and all(topo.may_write(c, d) for d in T.cores)]
    return sorted(free, key=lambda c: topo.die(c) == topo.die(core))


def share(engines, k, n):
    w = len(engines) // n
    return engines[w * k:w * k + w]


def neighbours(r):
    return [(k, a, G0 + b) for k, a, b in ((r + 1, 0, UP), (r - 1, 16, DOWN)) if 0 <= k < N]


def home(n, k):
    return (n, SL * k + 16, SL * k + SL, 1)


def seen(k, r):
    a = -(-NV * (N - 1 - r) // 8) * 8 + NV * (r - k) + (PAD if k < r else 0)
    return ("sg", a, a + NV, 1)


def last_engines(n, i):
    return sum([w[5] for call in CALLS for w in call if w[:2] == (n, i) and w[3] is None] +
               [w[3] for hand in HANDS for call in hand for w in call if w[:2] == (n, i)])


def hand_on(g, core, T, topo):
    mine = [c for c in topo.cores_of(core) if T.rank_of(c) is not None]
    if not mine or core not in helpers(mine[0], T, topo):
        return
    r, h = T.rank_of(mine[0]), helpers(mine[0], T, topo).index(core)
    others = order(r, T, topo)[:-1]
    out = topo.engines(core, T.cores[others[0]])
    near = neighbours(r)
    g.wait_ge(T.sem["h0"], 8)
    x, a, w = ("s", 8 * h, 8) if h < 2 else ("q", 0, 16)
    n = fused(g, T, topo, [(T.cores[k], ("he" + x, c + a, c + a + w), ("gr" + x, d + a, d + a + w), share(out, i, len(near)), "rh" + x)
                           for i, (k, c, d) in enumerate(near)], "lland")
    for hand in HANDS[h]:
        for k, call in enumerate(CALLS):
            if any(w[3] == h and w[0] == x[0] and w[1] <= x[1] < w[2] for w in call for x in hand):
                g.wait_ge(T.sem["c%d" % k], sum(w[5] for w in call if w[3] == h))
        n += fused(g, T, topo, [(T.cores[others[i]], ("hd" + x, NC * i, NC * i + NC), home("la" + x, r), out[a:a + e], "rl" + x)
                                for x, i, a, e in hand], "lland")
    g.wait_ge(T.sem["lland"], n)


def rank_program(g, core, T, topo):
    r = T.rank_of(core)
    if r is None:
        return hand_on(g, core, T, topo)
    queues = {"v": g.vector, "s": g.scalar, "t": g.tensor, "g": g, "y": g.sync}
    csem = {"v": "qv", "s": "qs", "t": "qt", "g": "qg"}
    count = {}
    known = {q: {} for q in queues}
    hist = {}
    used = {"aF": 8, "aH": 16, "aI": 0, "aU": 0}
    unit = {"aF": 8, "aH": 16, "aI": 8, "aU": 16}

    def V(name, a, b, step=1):
        return (name, a, b, step)

    def new(arena, n):
        a = used[arena]
        used[arena] = a + -(-n // unit[arena]) * unit[arena]
        return V(arena, a, a + n)

    def sub(v, a, b, step=1):
        return V(v[0], v[1] + a, v[1] + b, step)

    def col(v, a):
        return sub(v, a, a + 1)

    def ap(v):
        if v[3] < 0:
            return T[v[0]][:, v[2] - 1:v[1] - 1:v[3]]
        return T[v[0]][:, v[1]:v[2]:v[3]] if v[3] != 1 else T[v[0]][:, v[1]:v[2]]

    def note(v, write, q, sem, val, clock):
        hist.setdefault(v[0], []).append((v, write, q, sem, val, clock))

    def sync(q, outs, ins):
        need = {}
        for group, out in ((outs, True), (ins, False)):
            for v in group:
                for (o, write, oq, sem, val, clock) in hist.get(v[0], []):
                    if not (write or out) or o[1] >= v[2] or v[1] >= o[2]:
                        continue
                    if v[3] == o[3] and v[3] > 1 and (v[1] - o[1]) % v[3]:
                        continue
                    if val > need.get(sem, (0, None))[0]:
                        need[sem] = (val, clock)
        mine = csem.get(q)
        for sem in sorted(need, key=lambda s: (s == mine, s in DMAS, s)):
            val, clock = need[sem]
            if known[q].get(sem, 0) >= val:
                continue
            queues[q].wait_ge(T.sem[sem], val)
            for s2, v2 in list(clock.items()) + [(sem, val)]:
                known[q][s2] = max(known[q].get(s2, 0), v2)

    def run(q, outs, ins, call, sem=None, n=1):
        sync(q, outs, ins)
        sem = sem or csem[q]
        count[sem] = count.get(sem, 0) + n
        call(queues[q]).then_inc(T.sem[sem], n)
        clock = dict(known[q])
        for v in outs:
            note(v, True, q, sem, count[sem], clock)
        for v in ins:
            note(v, False, q, sem, count[sem], clock)

    def sc(s, ins):
        if isinstance(s, tuple):
            ins.append(s)
            return ap(s)
        return s

    def ts(o, i, s1, op0, s2=None, op1=None):
        ins = [i]
        a, b = sc(s1, ins), sc(s2, ins)
        if op1 is None:
            run("v", [o], ins, lambda e: e.tensor_scalar(ap(o), ap(i), a, None, op0))
        else:
            run("v", [o], ins, lambda e: e.tensor_scalar(ap(o), ap(i), a, b, op0, op1))
        return o

    def tt(o, a, b, op):
        run("v", [o], [a, b], lambda e: e.tensor_tensor(ap(o), ap(a), ap(b), op))
        return o

    def cp(o, i):
        run("v", [o], [i], lambda e: e.tensor_copy(ap(o), ap(i)))
        return o

    def tr(o, i):
        run("v", [o], [i], lambda e: e.transpose(ap(o), ap(i)))
        return o

    def scan(o, d0, d1, init=0.0):
        ins = [d0, d1]
        s = sc(init, ins)
        run("v", [o], ins, lambda e: e.tensor_tensor_scan(ap(o), ap(d0), ap(d1), s, MUL, ADD))
        return o

    def fill(o, c):
        run("v", [o], [], lambda e: e.memset(ap(o), c))
        return o

    def reduce(o, i, op):
        run("v", [o], [i], lambda e: e.tensor_reduce(ap(o), ap(i), AX, op))
        return o

    def gather(o, win, off, q="v"):
        if q == "v":
            run("v", [o], [win, off], lambda e: e.tensor_copy(ap(o), ap(win).indirect(ap(off))))
        else:
            run("s", [o], [win, off], lambda e: e.activation(ap(o), ap(win).indirect(ap(off)), AF.Copy))
        return o

    def scatter(win, off, val):
        run("v", [win], [off, val], lambda e: e.tensor_copy(ap(win).indirect(ap(off)), ap(val)))

    def act(o, i, func, scale=1.0, bias=0.0):
        ins = [i]
        a, b = sc(scale, ins), sc(bias, ins)
        run("s", [o], ins, lambda e: e.activation(ap(o), ap(i), func, bias=b, scale=a))
        return o

    def total(o, junk, i, func, bias=0.0):
        ins = [i]
        b = sc(bias, ins)
        run("s", [o, junk], ins, lambda e: e.activation(ap(junk), ap(i), func, bias=b, accum_out=ap(o)))
        return o

    def lin(o, i, scale=1.0, bias=0.0):
        return act(o, i, AF.Identity, scale, bias)

    def iota(o, pattern, base=0, lane=0):
        run("g", [o], [], lambda e: e.iota(ap(o), pattern, base, lane, allow_small_or_imprecise_dtypes=o[0] != "aI"))
        return o

    def dma(q, o, i, sem):
        run(q, [v for v in (o,) if isinstance(v, tuple)], [v for v in (i,) if isinstance(v, tuple)],
            lambda e: e.dma_start(ap(o) if isinstance(o, tuple) else o, ap(i) if isinstance(i, tuple) else i), sem, 16)

    def quant(n, a, b, t, c):
        q, s, i = V(n + "q", a, b), V(n + "s", a, b), V(t, c, c + 4 * (b - a))
        run("v", [q, s], [i], lambda e: e.quantize_mx(ap(q), ap(s), ap(i)))

    def pickc(cq, wq, off):
        run("v", [cq], [wq, off], lambda e: e.tensor_copy(ap(cq).bitcast(dt.uint32), ap(wq).bitcast(dt.uint32).indirect(ap(off))))

    def mm(o, wq, ws, xq, xs, start, stop):
        run("t", [o] if start else [], [wq, ws, xq, xs], lambda e: e.matmul_mx(ap(o), ap(wq), ap(ws), ap(xq), ap(xs), start, stop))
        if not start:
            note(o, True, "t", "qt", count["qt"], dict(known["t"]))

    def send(writes, lsem):
        sync("g", [], [w[1] for w in writes])
        count[lsem] = count.get(lsem, 0) + fused(g, T, topo, writes, lsem)

    def lands(views, rsem, n):
        count[rsem] = count.get(rsem, 0) + n
        for v in views:
            note(v, True, None, rsem, count[rsem], {})

    F1 = lambda: new("aF", 1)
    H, F, I1 = lambda n: new("aH", n), lambda n: new("aF", n), lambda: new("aI", 1)
    ranks = order(r, T, topo)
    others = ranks[:-1]
    turn = ranks[-2] - r
    aides = helpers(core, T, topo)
    out = topo.engines(core, T.cores[others[0]])
    inner = [e for e in topo.engines(core, aides[0]) if e not in out]
    above, below = (UP if r > 0 else ZERO) + 16, (DOWN if r < N - 1 else ZERO) - 256
    MID = ZERO - (above + below) // 2

    dma("y", V("uc", 0, 8), T.u[:, 0:8], "du")
    dma("y", V("xt", 0, 512), T.x[:, 0:512], "dx0")
    dma("y", V("xt", 512, 1024), T.x[:, 512:1024], "dx1")
    rs = fill(H(192), 1.0)
    ones = sub(rs, 32, 192)
    sync("y", [], [V("xt", 0, 512)])
    dma("y", V("wt", 0, EARLY), T.w[:, 0:EARLY], "dw0")

    lane = iota(I1(), [[0, 1]], 0, 1)
    jj = iota(H(64), [[0, 4], [1, 16]])
    base = iota(H(64), [[1, 4], [16, 16]], -MID)
    gap = above - (ZERO - MID)
    where = iota(F(4), [[10240 + gap, 2], [3072 + gap, 2]])
    GT_, e0 = F(68), F(37)
    pos = iota(F(35), [[1, 35]], -2)
    w2 = iota(F(16), [[1, 16]], 200, 16)
    t_l = iota(F(3), [[16, 3]], 0)

    def put(o, c):
        return act(o, sub(ones, 0, len(range(o[1], o[2], o[3]))), AF.Copy, scale=c)

    win, cells, Z, XB, fd, PT, ra = H(2500), H(272), H(80), H(176), H(144), H(48), H(NV)
    jI = ts(I1(), lane, 31, A.bitwise_and, 1, A.logical_shift_right)
    oI = ts(I1(), lane, 1, A.bitwise_and)
    iI = ts(I1(), lane, 15, A.bitwise_and)
    cut = ts(F1(), jI, -15.5, ADD)
    ft = H(256)
    put(V("xt", 1024, 1088), 0.0)
    put(ra, CARRY)
    put(col(cells, 271), 0.0)
    put(col(rs, 16), 0.0)
    for t in (0, 1):
        lin(V("ut", t + 2, 512, 4), sub(ones, 0, 128), 0.0, V("uc", t + 2, t + 3))
        ts(V("ut", t, 512, 4), sub(ones, 0, 128), V("uc", t, t + 1), MUL)
    sig = ts(F1(), oI, -2.0, MUL, 1.0, ADD)
    side = act(H(64), jj, AF.Sign, 1.0, cut)
    put(col(ra, 1), 1.0 if r == N - 1 else 0.0)
    small = put(H(16), CARRY / 16)
    back = lin(H(16), sub(side, 0, 16), -7.96875, 8.03125)
    forth = lin(H(16), sub(side, 0, 16), 7.96875, 8.03125)
    for a in range(0, 256, 64):
        lin(sub(ft, a, a + 64), side, 7.96875, 8.03125)
    put(sub(win, RING, RING + 128), 0.0)

    near = neighbours(r)
    sgn = H(256)
    for h in (0, 1):
        a = G0 + 128 * h
        quant("gr", a, a + 128 + 16 * h, "xt", 4 * a)
        if h == 0:
            quant("u", 0, 128, "ut", 0)
        else:
            for to, x, e in ((aides[2], "q", out), (aides[:2], "s", inner)):
                send([(to, V("gr" + x, c, c + 16), V("he" + x, 16 * i, 16 * i + 16), share(e, i, 2), "h0") for i, c in enumerate((240, 0))], "lhalo")
        mm(V("ps", 512 * h, 512 * h + 128), V("uq", 0, 128), V("us", 0, 128), V("grq", a, a + 128), V("grs", a, a + 128), True, True)
    wide = sum(len(out) // len(neighbours(k)) for k, a, b in near)
    for n, rsem, m in (("grq", "rhq", 1), ("grs", "rhs", 2)):
        lands([V(n, G0 + (UP if k < r else DOWN), G0 + 16 + (UP if k < r else DOWN)) for k, a, b in near], rsem, m * wide)
    rz = reduce(F1(), back, MUL)
    eq, iF = F(16), F1()
    late = [lambda: scan(eq, forth, sub(ones, 0, 16)), lambda: ts(iF, iI, 0.0, ADD)]
    late[r > 0]()
    ts(sub(sgn, 0, 128), V("ps", 0, 128), sig, MUL, 0.0, GT)
    act(sub(ft, 0, 256, 16), small, AF.Copy, rz)
    ts(sub(sgn, 128, 256), V("ps", 512, 640), sig, MUL, 0.0, GT)
    late[r == 0]()
    scan(sub(cells, 0, 256), ft, sgn, col(eq, 15) if r == 0 else 0.0)
    h8 = ts(I1(), lane, 8, A.bitwise_and)
    own = scan(seen(r, r), ra, sub(cells, 15, 272, -16), col(cells, 255))
    g16 = ts(I1(), lane, 16, A.bitwise_and)
    send([([T.cores[k] for k in others], own, [seen(r, k) for k in others], out, "rsign")], "lsign")
    lands([seen(k, r) for k in others], "rsign", (N - 1) * len(out))
    every = V("sg", seen(N - 1, r)[1], seen(0, r)[2])
    mine, n = NV * (N - r), every[2] - every[1]
    g.sync.wait_ge(T.sem["lsign"], count["lsign"])
    known["y"]["lsign"] = count["lsign"]
    for k, (a, b) in ((1, (EARLY, 4096)), (2, (4096, 5120))):
        dma("y", V("wt", a, b), T.w[:, a:b], "dw%d" % k)
    t_f = iota(H(136), [[0, 8], [-15, NV]], 16)
    iota(sub(e0, 35, 37), [[-2, 2]], 2)
    if r > 0:
        iota(sub(fd, mine, mine + PAD), [[0, PAD]], 1)
        iota(sub(every, mine, mine + PAD), [[0, PAD]], 0)
    iota(sub(XB, n, n + 32), [[0, 32]], 0)
    iota(col(GT_, 67), [[0, 1]], 256)
    t_d, firsts = F(8), [8 * d for d in ranks[1::2]]
    nb = [i for i in range(1, 5) if i == 4 or firsts[i] < firsts[i - 1]][0]
    for a, b in ((0, nb), (nb, 4)):
        if a < b:
            iota(sub(t_d, 2 * a, 2 * b), [[firsts[min(a + 1, b - 1)] - firsts[a], b - a], [0, 2]], firsts[a])
    t_n = iota(F(8), [[-128, 8]], -64 + 16 * max(r - 1, 0) - 8 * r)
    iota(V("xt", 1088, 1536), [[0, 448]], 0)

    act(sub(Z, 15, 80), sub(ones, 0, 65), AF.Copy, sig)
    ahead = act(F1(), iF, AF.Relu, 5.0, -49.0)
    behind = act(F1(), iF, AF.Relu, -5.0, 16.0)
    d5 = act(F(4), where, AF.Abs, -1.0 / 1024, iF)
    thr = lin(F1(), col(eq, 15), LEVEL)
    delta = lin(F1(), behind, -1.0, ahead)
    edge = act(F(4), d5, AF.Relu, -1024.0, float(above))
    keep = act(F(2), sub(d5, 1, 3), AF.Sign, 1.0, -gap / 1024.0)
    d0 = act(F(35), pos, AF.Abs, -0.5, iF)
    val, vb = H(256), H(48)
    lin(sub(val, 0, 64), base, 1.0, delta)
    wa = lin(col(GT_, 65), iF, -1.0, -1.0 - BIG)
    act(sub(e0, 0, 35), d0, AF.Relu, -2.0, 1.0)
    for a in (192, 64, 128):
        lin(sub(val, a, a + 64), sub(val, 0, 64), 1.0, a / 16.0)
    dA = lin(F(35), sub(e0, 0, 35), wa, 1.0)
    lin(sub(val, 240, 256), sub(val, 240, 256), col(keep, 1), col(edge, 2))
    th0 = lin(F1(), thr, -1.0, col(own, 16))
    lin(sub(val, 0, 16), sub(val, 0, 16), col(keep, 0), col(edge, 1))
    t15 = lin(F1(), thr, -1.0, col(own, 1))
    act(sub(fd, 0, mine), sub(t_f, 0, mine), AF.Relu, CARRY)
    if r > 0:
        act(sub(fd, mine + PAD, n), sub(t_f, 0, NV * r), AF.Relu, CARRY)
    th15 = lin(F1(), t15, 1.0 / CARRY)
    lin(col(GT_, 0), iF, -2.0, 2.0 * (127 - (BIG - 1) // 2 - BIG))
    lin(sub(PT, 32, 34), sub(pos, 2, 4), -2 * ROUND, ROUND)

    for a in (17, 33):
        ts(sub(Z, a, a + 14), sub(own, 2, 16, -1), thr, LT, -0.5, ADD)
    PI = H(96)
    i4 = ts(F1(), h8, -7.0, MUL, 63.5 - 16 * max(r - 1, 0), ADD)
    AC = scan(H(64), sub(rs, 0, 64), sub(Z, 15, 79))
    tr(sub(PI, 0, 32), sub(Z, 16, 48))
    tr(sub(PI, 32, 96), AC)
    idle = tt(F(16), sub(PI, 1, 32, -2), sub(PI, 0, 31, -2), NE)
    num = scan(F(64), sub(ones, 0, 64), sub(PI, 0, 64, -1))
    away = tt(F(16), idle, w2, MUL)
    ci = total(F1(), F(32), sub(PI, 64, 96), AF.Identity)
    lin(col(GT_, 66), ci, 2.0, iF)
    tl = ts(F1(), g16, -turn / 2.0, MUL, 63.5 + 8 * turn, ADD)
    o6 = tt(F(16), sub(num, 33, 64, 2), away, ADD)
    off_l = ts(new("aU", 3), t_l, iF, ADD, 3.2, MUL)
    off = ts(new("aU", 16), o6, RING - 1.0, ADD)
    dg = tt(F(35), dA, sub(e0, 2, 37), SUB)
    off_a = ts(new("aU", 1), iF, 3.2, MUL, 31.0, MIN)
    scatter(win, off, val)

    G = F(64)
    act(sub(G, 0, 32), sub(ones, 0, 32), AF.Sign, th0, col(seen(r - 1, r), 0) if r > 0 else 0.0)
    act(sub(G, 32, 64), sub(ones, 0, 32), AF.Sign, th15, col(seen(r + 1, r), 16) if r < N - 1 else 0.0)
    for a in (0, 16):
        lin(sub(vb, a, a + 16), sub(val, 15, 256, -16), 1.0, col(edge, 3))
    lin(sub(vb, 32, 48), sub(val, 0, 256, 16), 1.0, col(edge, 0))
    act(sub(win, RING + 128, RING + 192), sub(win, RING, RING + 64), AF.Copy)
    i5 = lin(F1(), iF, -1.0, i4)
    tabd = lin(F(8), t_d, 1.0, tl)
    bF = lin(F1(), iF, -16.0)
    DT = H(160)
    put(sub(DT, 128, 160), 0.0)
    FB, m = F(68), max(NV * r, 1)
    fx = scan(H(n), sub(fd, 0, n), every)
    quant("w", 0, 128, "wt", 0)
    ts(sub(XB, 0, n), fx, thr, LT, -0.5, ADD)
    tr(sub(GT_, 1, 65), G)
    sb = scan(H(m + 32), sub(ones, 0, m + 32), sub(XB, n - m, n + 32))
    scan(sub(FB, 0, 35), dg, sub(GT_, 33, 68))
    scan(sub(FB, 35, 68, -1), sub(dg, 0, 33), sub(GT_, 0, 33, -1))
    tr(sub(PT, 0, 32), sub(sb, m, m + 32))
    offb = ts(new("aU", 3), sub(FB, 33, 36), 0.5, MUL, RING + (BIG - 1) / 2, ADD)
    w5 = scan(F(34), sub(ones, 0, 34), sub(PT, 0, 34), i5)
    scatter(win, offb, vb)
    off_d = ts(new("aU", 8), tabd, col(w5, 31), SUB, col(w5, 33), ADD)
    nb = lin(F(8), t_n, 1.0, i5)
    lbk = lin(F1(), iF, 1.0, 16.0 + 4 * SL)
    D = H(128)
    for a, b, q in ((0, 2, "v"), (2, 8, "s")):
        gather(sub(D, 16 * a, 16 * b), sub(win, RING, RING + 192), sub(off_d, a, b), q)
    X = scan(H(n), sub(ones, 0, n), sub(XB, 0, n, -1))
    XS = sub(side, 0, 32)
    if r > 0:
        act(sub(XS, 0, r), sub(X, 15, NV * r, NV), AF.Copy)
    lin(sub(XS, r, N), sub(X, n - mine + 15, n, NV), 1.0, -PAD / 2.0 if r > 0 else 0.0)
    tr(sub(DT, 0, 32), sub(D, 0, 32))
    tr(sub(DT, 32, 128), sub(D, 32, 128))
    first, lw = new("aU", 16), new("aU", 48)
    for o, w, l in ((first, sub(DT, 0, 32), off_a), (lw, DT, off_l)):
        run("v", [o], [w, l], lambda e: e.tensor_scalar(ap(o), ap(w).indirect(ap(l)), float(MID + G0), None, ADD))

    gq, gs = V("grq", 0, PW), V("grs", 0, PW)
    for x, a, b, q in PICKS:
        l = sub(lw if a else first, 5 * a, 5 * b)
        if x == "s":
            gather(V("sls", NC * a, NC * b), gs, l, q)
        else:
            pickc(V("slq", NC * a, NC * b), gq, l)
    for k, call in enumerate(CALLS):
        send([(T.cores[others[a]], V("sl" + x, NC * a, NC * b), home("la" + x, r), (out + inner)[e:e + w], "rl" + x) if h is None else
              (aides[h], V("sl" + x, NC * a, NC * b), V("hd" + x, NC * a, NC * b), (out + inner)[e:e + w], "c%d" % k)
              for x, a, b, h, e, w in call], "lland")
    for x in "qs":
        lands([home("la" + x, k) for k in others], "rl" + x, sum(last_engines(x, order(k, T, topo).index(r)) for k in others))

    tr(sub(XB, n - 32, n), XS)
    pickc(V("laq", SL * r, SL * r + SL), gq, sub(lw, 34, 40))
    C = scan(F(64), sub(ones, 0, 64), sub(XB, n - 32, n + 32), bF)
    quant("la", SL * N + 16, LW, "xt", 1024)
    CT = tr(F(32), sub(C, 32, 64))
    quant("w", 128, 640, "wt", 512)
    quant("w", 640, 1024, "wt", 2560)
    cnt, junk = F(16), F(64)
    for c in range(8):
        total(col(cnt, c), sub(junk, 8 * c, 8 * c + 8), sub(CT, 0, 8), AF.Sign, col(nb, c))
    lin(sub(cnt, 8, 16), sub(cnt, 0, 8), 1.0, -32.0 / SL)
    gather(V("las", SL * r, SL * r + SL), gs, sub(lw, 34, 40), "s")
    quant("w", 1024, 1280, "wt", 4096)
    lu = ts(new("aU", 16), cnt, -SL / 2.0, MUL, lbk, ADD)

    tk = lambda n, k, w=1: V(n, 128 * k, 128 * (k + w))
    for k, w, q in ((0, 2, "s"), (2, 2, "s"), (4, 1, "s")):
        pickc(tk("tq", k, w), V("laq", 16 * k, LW), sub(lu, 0, 8 * w))
        gather(tk("ts", k, w), V("las", 16 * k, LW), sub(lu, 0, 8 * w), q)
    for k in range(5):
        for o in (0, 1):
            a = 128 * (2 * KW[k] + o)
            mm(V("ps", 1024 + 512 * o, 1152 + 512 * o), V("wq", a, a + 128), V("ws", a, a + 128), tk("tq", k), tk("ts", k), k == 0, k == 4)
    cp(V("yo", 0, 128), V("ps", 1024, 1152))
    act(V("yo", 128, 256), V("ps", 1536, 1664), AF.Copy)
    dma("y", T.y[:, 0:128], V("yo", 0, 128), "dy0")
    dma("s", T.y[:, 128:256], V("yo", 128, 256), "dy1")
    for sem in sorted(SEMAPHORES, key=lambda s: (s in ("dy0", "dy1"), s in csem.values())):
        if count.get(sem, 0) > max(known[q].get(sem, 0) for q in queues):
            g.wait_ge(T.sem[sem], count[sem])
